import numpy as np, ml_dtypes
CORES = [9,25,41,57]
N = 4
BF = ml_dtypes.bfloat16
W, K, T, S, ND = 4096, 256, 4, 1, 2
def stir(rng, a, n):
    r = rng.random(a.shape, dtype=np.float32)
    s = np.concatenate([np.sort(r, axis=-1), np.full(r.shape[:-1] + (1,), 2, np.float32)], axis=-1)
    return np.where(r < np.take_along_axis(s, n[..., None], -1), (a + rng.integers(1, 64, a.shape)) & 63, a)
def near(rng, pro, n, counts):
    a = pro[np.arange(8)[None, :, None], rng.integers(0, pro.shape[1], (N, 8, n))]
    return stir(rng, a, rng.choice(np.array(counts), (N, 8, n)))
def protos(rng, first):
    return stir(rng, np.repeat(first, 2, axis=1), np.full((8, 2), 3))
def parts(rng):
    pro = protos(rng, rng.integers(0, 64, (8, 1, 16)))
    return (near(rng, pro, K, [0, 1, 1, 2, 2, 3, 16]), rng.integers(0, 256, (N, 8, K, 16)), near(rng, pro, W, [0, 1, 1, 2, 3, 16]), rng.integers(0, 256, (N, 8, W, 16)),
            rng.integers(0, 256, (8, 16, 2)), rng.integers(900, 1900, (N, 8, 16)))
def tile(a):
    return np.ascontiguousarray(a.transpose(0, 1, 3, 2)).reshape(N, 128, -1).astype(np.float32).astype(BF)
def pack(x, g, lx, lm, w, lim):
    return {"xw": tile(x), "gw": tile(g), "lex": tile(lx), "mng": tile(lm),
            "wts": np.ascontiguousarray(np.broadcast_to(w.reshape(1, 128, 2), (N, 128, 2))).astype(np.int32), "th": lim.reshape(N, 128, 1).astype(np.int32)}
def setup_inputs(rng):
    return pack(*parts(rng))
def setup_inputs_spread(rng):
    pro = protos(rng, (64 * rng.random((8, 1, 16)) ** 3).astype(np.int64))
    x = near(rng, pro, K, [0, 1, 1, 2, 3, 4, 16]); lx = near(rng, pro, W, [0, 1, 1, 2, 4, 16])
    g = np.floor(256 * rng.random((N, 8, K, 1)) ** 2 * rng.random((N, 8, K, 16))).astype(np.int64)
    lm = np.floor(256 * rng.random((N, 8, W, 1)) ** 2 * rng.random((N, 8, W, 16))).astype(np.int64)
    w = np.exp2(8 * rng.random((8, 16, 2))).astype(np.int64) - 1; w = np.where(rng.random(w.shape) < 0.25, rng.integers(0, 256, w.shape), w)
    lim = np.minimum(np.exp2(4 + 8.2 * rng.random((N, 8, 16))).astype(np.int64), 4081)
    return pack(x, g, lx, lm, w, lim)
def setup_inputs_ends(rng):
    base = np.repeat(63 * rng.integers(0, 2, (8, 1, 16)), 2, axis=1); base[:, 1] = np.where(rng.random((8, 16)) < 0.15, 63 - base[:, 1], base[:, 1])
    def some(n, share):
        a = base[np.arange(8)[None, :, None], rng.integers(0, 2, (N, 8, n))]
        return np.where(rng.random(a.shape) < share, np.where(rng.random(a.shape) < 0.6, 63 - a, rng.choice(np.array([1, 31, 62]), a.shape)), a)
    def both(n):
        return 255 * np.where(rng.random((N, 8, n, 1)) < 0.5, rng.integers(0, 2, (N, 8, n, 1)), rng.integers(0, 2, (N, 8, n, 16)))
    x = some(K, 0.08); lx = some(W, 0.1); g = both(K); lm = both(W)
    w = 255 * rng.integers(0, 2, (8, 16, 2)); w[:5, 15] = 65; w[5, :, 0] = 255; w[6, 0] = 65; w[7, 14:, 0] = 65; w[7, 14:, 1] = 0
    w[4, 13, 0] = 89; w[4, 13, 1] = 0; w[4, 14, 0] = 0; w[4, 14, 1] = 227
    lim = np.full((N, 8, 16), 4081); odd = np.arange(N) % 2 == 1
    lim = np.where(odd[:, None, None] & (rng.random(lim.shape) < 0.25), 0, lim); lim[:, 0, 0] = 0
    x[:, 0, :, 0] = 63; lx[:, 0, :, 0] = 63
    x[:, 5, 1] = 63; x[:, 5, K - 1] = 63
    for i in (3, K - 2):
        x[:, 1:5, i] = 0; x[:, 1:5, i, 15] = 63
    p = (((W - 1) ** 2 >> 5) + W - 1) & (W - 1)
    lx[:, 1:5, p] = 0; lx[:, 1:5, p, 15] = 63; lx[:, 1:5, p, 13] = 63
    x[:, 4, 4] = 0; x[:, 4, 4, 13] = 46; x[:, 4, 4, 14] = 36; x[:, 4, 4, 15] = 63
    p = ((4093 * 4075 >> 5) + 4093) & (W - 1)
    lx[:, 4, p] = x[:, 4, 4]; lx[:, 4, p, 0] = 63; lx[:, 4, p + 1] = 63; lm[:, 4, p] = 255; g[:, 4, 4] = 0
    x[:, 7, 4] = 0; x[:, 7, 4, 14] = 63; g[:, 7, 4] = 0
    for i in (5, K - 1):
        x[:, 7, i] = 0; x[:, 7, i, 15] = 63; g[:, 7, i] = 255 if i == 5 else 0
    lx[:, 7, 0] = 63; lx[:, 7, W - 1] = 0; lx[:, 7, W - 1, 14:] = 63; lm[:, 7, W - 1] = 255
    g[:, 6, :, 15] = 255; lm[:, 6, :, 15] = 255; g[:, 6, :, 14] = 0; lm[:, 6, :, 14] = 0
    return pack(x, g, lx, lm, w, lim)
def setup_inputs_corners(rng):
    pro = rng.integers(0, 64, (8, 1, 16)); lx = near(rng, pro, W, [0, 0, 1]); lx[:, :, 0] = pro[:, 0]
    x = near(rng, pro, K, [0, 1, ND, ND + 1, ND + 2, 16])
    w = rng.integers(0, 256, (8, 16, 2)); w[0] = 0; w[1] = 255; w[2, :, 0] = 0; w[2, :, 1] = 255; w[3, :, 1] = w[3, :, 0]; w[4, :15] = 0; w[4, 15] = 255; w[5, 1:] = 0; w[5, 0] = 255
    w[6] = 255 * rng.integers(0, 2, (16, 2)); w = w[rng.permutation(8)]
    def mean(n):
        return np.where(rng.random((N, 8, n, 1)) < 0.6, 255 * rng.integers(0, 2, (N, 8, n, 1)), rng.integers(0, 256, (N, 8, n, 16)))
    case = (np.arange(8)[None, :] + np.arange(N)[:, None] + rng.integers(0, 5)) % 5; case = case[:, :, None]
    lim = np.where(case == 0, 0, np.where(case == 1, 4081, np.where(case == 2, 4081 * rng.integers(0, 2, (N, 8, 16)), np.where(case == 3, 1, rng.integers(900, 1900, (N, 8, 16))))))
    return pack(x, mean(K), lx, mean(W), w, lim)
def setup_inputs_ties(rng):
    pro = rng.integers(0, 64, (8, 1, 16)); far = np.where(rng.permutation(8) < 4, 0, rng.integers(130, 251, 8)).reshape(8, 1, 1)
    b = rng.integers(0, 255 - far, (8, 1, 16)); side = rng.integers(0, 2, (8, 1, 16))
    x = near(rng, pro, K, [0, 1, 1, 1]); lx = near(rng, pro, W, [0, ND, ND, ND + 1])
    g = b + far * side + rng.integers(0, 2, (N, 8, K, 16)); lm = b + far * (1 - side) + rng.integers(0, 2, (N, 8, W, 16))
    lim = np.where(far[:, 0] == 0, rng.integers(5, 13, (N, 8, 16)), 16 * far[:, 0] + rng.integers(-3, 5, (N, 8, 16)))
    return pack(x, g, lx, lm, rng.integers(0, 256, (8, 16, 2)), lim)
def setup_inputs_alike(rng):
    o = rng.permutation(64); al = o[:4]; kinds = (rng.integers(0, 4, (8, 1, 16)) + (rng.random((8, 6, 16)) < 0.12) * rng.integers(1, 4, (8, 6, 16))) & 3
    pro = al[kinds]; x = near(rng, pro, K, [0]); lx = near(rng, pro, W, [0])
    g = rng.integers(0, 256, (N, 8, K, 16)); lm = rng.integers(0, 256, (N, 8, W, 16)); w = rng.integers(0, 256, (8, 16, 2))
    even = (np.arange(N) % 2 == 0)[:, None, None]
    lim = np.where((rng.random((N, 8, 1)) < 0.6) | even, 4081, rng.integers(900, 1900, (N, 8, 16)))
    two = np.sort(o[4:12].reshape(4, 2), axis=1); spot = np.arange(W); four = [int(e) for e in rng.permutation(8)[:4]]
    for e in four:
        lx[:, e] = pro[e, 0]; lx[:, e, :, 0] = two[spot & 3, 1]; lx[:, e, :, 14] = spot & 63; lx[:, e, :, 15] = spot >> 6
        w[e] = 0; w[e, 14, 0] = 1; w[e, 15, 0] = 64; lim[:, e] = 4081
    for r in range(N):
        j = rng.permutation(W >> 1)[:K]
        put = [4 * (j >> 1) + 2 + (j & 1),
               np.full(K, 4 * rng.integers(0, W >> 2) + 2 + rng.integers(0, 2)),
               4 * rng.permutation(W >> 2)[:K] + (np.arange(K) >= 256),
               np.repeat(4 * rng.permutation(W >> 2)[:K >> 1] + (np.arange(K >> 1) & 3), 2)]
        for e, p in zip(four, put):
            x[r, e] = pro[e, 0]; x[r, e, :, 0] = two[p & 3, 0]; x[r, e, :, 14] = p & 63; x[r, e, :, 15] = p >> 6
    e = four[2]
    g[:, e] = rng.integers(0, 41, (N, K, 16)) + 200 * even; lm[:, e] = rng.integers(0, 41, (N, W, 16)); lim[:, e] = rng.integers(700, 2500, (N, 16))
    return pack(x, g, lx, lm, w, lim)
def check_inputs(d):
    bad = []
    for k, lo, hi in (("xw", 0, 63), ("gw", 0, 255), ("lex", 0, 63), ("mng", 0, 255), ("wts", 0, 255), ("th", 0, 4081)):
        a = np.asarray(d[k]).astype(np.float64)
        if not (np.min(a) >= lo and np.max(a) <= hi): bad.append("range of " + k)
        elif np.any(a != np.floor(a)): bad.append("whole numbers of " + k)
    a = np.asarray(d["wts"])
    if np.any(a != a[:1]): bad.append("wts alike on all ranks")
    return bad
def visit(t, x, g, lx, lm, w, lim):
    p = w[..., :1] * x; u = (np.add.reduce(p, axis=1, keepdims=True) - p) & (W - 1)
    p = w[..., 1:] * x; u2 = (np.add.reduce(p, axis=1, keepdims=True) - p) & (W - 1)
    h = (((u * u2) >> 5) + u) & (W - 1)
    c = np.take_along_axis(lx, h.reshape(8, 1, 16 * K), 2).reshape(8, 16, 16, K)
    m = np.take_along_axis(lm, h.reshape(8, 1, 16 * K), 2).reshape(8, 16, 16, K)
    differ = np.add.reduce((c != x[:, :, None, :]).astype(np.int32), axis=1)
    far = np.add.reduce(np.abs(m - g[:, :, None, :]), axis=1)
    lane = np.arange(16); b = c[:, lane, lane, :]
    pair = (b != x) & (differ <= ND + 1)
    has = np.any(pair, axis=1); f = np.argmax(pair, axis=1)[:, None, :]
    def at(a):
        return np.take_along_axis(a, f, 1)[:, 0]
    xa, xb, hf = at(x), at(b), at(h)
    free = at((far < lim).astype(np.int32)) == 1
    pc = 64 * np.minimum(xa, xb) + np.maximum(xa, xb)
    flag = np.zeros(4096, bool); flag[pc[has & ~free]] = True
    merge = has & free & ~flag[pc]
    mf = np.take_along_axis(lm, hf[:, None, :], 2)
    row = lane[None, :, None]
    xn = np.where((row == f) & merge[:, None, :], np.minimum(x, b), x)
    xn = np.where((row == t) & ~has[:, None, :], b, xn)
    gn = np.where(merge[:, None, :], (g + mf) >> 1, g)
    for e in range(8):
        for i in np.flatnonzero(merge[e])[::-1]:
            lx[e, :, hf[e, i]] = xn[e, :, i]; lm[e, :, hf[e, i]] = gn[e, :, i]
    x[...] = xn; g[...] = gn
def reference(xw, gw, lex, mng, wts, th):
    x = xw.astype(np.float32).astype(np.int32).reshape(N, 8, 16, K); g = gw.astype(np.float32).astype(np.int32).reshape(N, 8, 16, K)
    lx = lex.astype(np.float32).astype(np.int32).reshape(N, 8, 16, W); lm = mng.astype(np.float32).astype(np.int32).reshape(N, 8, 16, W)
    w = wts.astype(np.int32).reshape(N, 8, 16, 2); lim = th.astype(np.int32).reshape(N, 8, 16, 1)
    for t in range(T):
        for r in range(N):
            v = (r + S * t) % N; visit(t, x[r], g[r], lx[v], lm[v], w[v], lim[v])
    return {"yx": x.reshape(N, 128, K).astype(np.float32).astype(BF), "yg": g.reshape(N, 128, K).astype(np.float32).astype(BF),
            "yl": lx.reshape(N, 128, W).astype(np.float32).astype(BF), "ym": np.add.reduce(lm, axis=3).reshape(N, 128, 1).astype(np.float32)}

@@ -1,0 +1,590 @@
+from concourse.mybir import AluOpType as A, ActivationFunctionType as F, AxisListType as X
+
+K = 256
+W = 4096
+NV = 4
+CH = 64
+PARTS = ((0, 128), (128, 256))
+CFG = {"xs": 6, "cs": 4, "eqs": 6, "chains": (((0, 64),), ((64, 128), (128, 192), (192, 256))), "lm": 1, "gv": 1, "xk": 3, "vs": 16, "go": 1}
+
+SCRATCH = {}
+
+
+def _buf(name, cols, dtype, where="sbuf", rows=128):
+    SCRATCH[name] = (where, [rows, cols], dtype)
+
+
+for _t in range(NV + 1):
+    _buf("xin%d" % _t, K, "bfloat16")
+    _buf("gin%d" % _t, K, "bfloat16")
+for _d, _l in (
+        ("bfloat16", (("xo", NV * K), ("go", NV * K), ("zt", NV * 128), ("lx", W + K), ("lm", W + K), ("ones", 128), ("ones64", 512),
+                      ("bo1", 128), ("bo", 128), ("idn", 128), ("lt", 128), ("gt", 128), ("c1", 128), ("c2", 128), ("c3", 128),
+                      ("zb", 128), ("za", 128), ("e1", 128), ("bd", 128), ("w1", 256), ("w2", 128), ("lk", 2048), ("lb", 2048),
+                      ("bow", 128), ("thl", K), ("nid", 128), ("idx", 384), ("bo64", 128), ("n4096", 256), ("cb", 256), ("xb", K), ("nx", K),
+                      ("oz", 512), ("ra", 512), ("io0", 64), ("ion", 64), ("fb", 512), ("cg", 4096), ("d", 4096), ("pair", K),
+                      ("ep", K), ("gs", K), ("ca", 2 * K), ("dg", K), ("gm", K), ("en", K), ("ndx", K), ("xa", 1024), ("xh", 1024),
+                      ("chh", 1024), ("h1", 64), ("tb", K), ("rm", K), ("f", K), ("ea", 2048), ("ls", K))),
+        ("float16", (("lb16", 2048), ("id16", 128), ("nid16", 128), ("bo16", 384), ("h16", K), ("eh", K))),
+        ("int32", (("wti", 2), ("thi", 1), ("jci", 1), ("jcj", 1), ("pr", K), ("p2", K), ("h", K), ("xi", 16), ("x3", 16))),
+        ("uint16", (("hu", K), ("hq", 16), ("of", 16), ("hr", K), ("so", 16))),
+        ("float32", (("thr", NV), ("wf", 2), ("thc", 1), ("jc", 1), ("io16", 16), ("md", 16), ("dm0", 16), ("dmp", 16), ("dmq", 16), ("pw", 16),
+                     ("nb", 1), ("u2s", K), ("hqf", 16), ("qs", 48), ("xq", 16), ("q1", 16), ("thq", 16), ("th2", 16), ("q2", 16), ("hqx", 16), ("sq", 16), ("cq", 16),
+                     ("nf", 16), ("dg1", K), ("dg2", K), ("mt", K), ("yv", K), ("nm", 16), ("hqm", 16), ("hqs", 16),
+                     ("lq2", 16), ("sm", 3)))):
+    for _n, _c in _l:
+        _buf(_n, _c, _d)
+SCRATCH["t1"] = ("sbuf", [128, 3, K], "float16")
+SCRATCH["eq"] = ("sbuf", [128, 16, 272], "bfloat16")
+for _n in ("pu1", "pu2", "pxp", "ppa", "ppb", "pq", "pval", "ph"):
+    _buf(_n, 512, "float32", "psum")
+
+SEMAPHORES = ["v", "s", "p", "gc", "loc"]
+SEMAPHORES += ["ld%d" % _i for _i in range(6)] + ["st%d" % _i for _i in range(4)]
+SEMAPHORES += ["ax%d" % _i for _i in range(1, NV + 1)] + ["ag%d" % _i for _i in range(1, NV + 1)]
+
+
+def tracker(g, T):
+    queue = {"V": g.vector, "S": g.scalar, "P": g.tensor, "G": g, "Y": g.sync}
+    own = {"V": "v", "S": "s", "P": "p", "G": "gc"}
+    total = {}
+    know = {q: {} for q in queue}
+    log = {}
+
+    def span(a):
+        if len(a) == 1:
+            return a[0], 0, SCRATCH[a[0]][1][1]
+        return a
+
+    def need(q, reads, writes):
+        found = []
+        for wr, accs in ((False, reads), (True, writes)):
+            for a in accs:
+                name, lo, hi = span(a)
+                bank = SCRATCH[name][0] == "psum"
+                for r in log.get(name, ()):
+                    lap = r["lo"] < hi and lo < r["hi"]
+                    if bank and r["q"] != q:
+                        found.append(r)
+                    elif lap and (r["wr"] or wr):
+                        if bank and q == "P":
+                            continue
+                        found.append(r)
+        return found
+
+    def wait(q, found):
+        for r in sorted(found, key=lambda r: -r["seq"]):
+            if know[q].get(r["sem"], 0) < r["val"]:
+                queue[q].wait_ge(T.sem[r["sem"]], r["val"])
+                for s, v in r["clock"].items():
+                    know[q][s] = max(know[q].get(s, 0), v)
+
+    seq = [0]
+
+    def note(q, sem, val, clock, reads, writes, dma):
+        seq[0] += 1
+        for wr, accs in ((True, writes), (False, reads)):
+            for a in accs:
+                name, lo, hi = span(a)
+                rows = log.setdefault(name, [])
+                if wr:
+                    rows[:] = [r for r in rows if not (lo <= r["lo"] and r["hi"] <= hi)]
+                rows.append({"q": q, "sem": sem, "val": val, "clock": clock, "lo": lo, "hi": hi, "wr": wr, "dma": dma, "seq": seq[0]})
+
+    def op(q, call, reads=(), writes=()):
+        wait(q, need(q, reads, writes))
+        sem = own[q]
+        call(queue[q]).then_inc(T.sem[sem], 1)
+        total[sem] = total.get(sem, 0) + 1
+        clock = dict(know[q])
+        clock[sem] = total[sem]
+        note(q, sem, total[sem], clock, reads, writes, False)
+
+    def dma(q, call, sem, reads=(), writes=()):
+        wait(q, need(q, reads, writes))
+        call(queue[q]).then_inc(T.sem[sem], 16)
+        clock = dict(know[q])
+        clock[sem] = 16
+        note("dma", sem, 16, clock, reads, writes, True)
+
+    def arrive(sem, val, writes):
+        note("dma", sem, val, {sem: val}, (), writes, True)
+
+    def ready(q, reads):
+        wait(q, need(q, reads, ()))
+
+    def finish():
+        for sem, q in (("v", "G"), ("s", "G"), ("p", "G"), ("gc", "V")):
+            if know[q].get(sem, 0) < total[sem]:
+                queue[q].wait_ge(T.sem[sem], total[sem])
+
+    return op, dma, arrive, ready, finish
+
+
+def rank_program(g, core, T, topo):
+    rank = T.rank_of(core)
+    if rank is None:
+        return
+    op, dma, arrive, ready, finish = tracker(g, T)
+
+    def v(a):
+        if a[0] == "t1":
+            return T.t1[:, a[1] // K, a[1] % K:a[1] % K + a[2] - a[1]]
+        return T[a[0]][:] if len(a) == 1 else T[a[0]][:, a[1]:a[2]] if len(a) == 3 else T[a[0]][:, a[1]:a[2]:a[3]]
+
+    def rw(*a):
+        return tuple(x[:3] for x in a if isinstance(x, tuple))
+
+    def sc(x):
+        return v(x) if isinstance(x, tuple) else x
+
+    def ts(out, i0, s1, o0, s2=None, o1=None):
+        if o1 is None:
+            op("V", lambda e: e.tensor_scalar(v(out), v(i0), sc(s1), None, o0), rw(i0, s1), rw(out))
+        else:
+            op("V", lambda e: e.tensor_scalar(v(out), v(i0), sc(s1), sc(s2), o0, o1), rw(i0, s1, s2), rw(out))
+
+    def tt(out, a, b, o):
+        op("V", lambda e: e.tensor_tensor(v(out), v(a), v(b), o), rw(a, b), rw(out))
+
+    def gat(out, win, offs, b, o):
+        op("V", lambda e: e.tensor_tensor(v(out), v(win).indirect(v(offs)), v(b), o), rw(win, offs, b), rw(out))
+
+    def cp(out, a):
+        op("V", lambda e: e.tensor_copy(v(out), v(a)), rw(a), rw(out))
+
+    def scat(win, offs, a):
+        op("V", lambda e: e.tensor_copy(v(win).indirect(v(offs)), v(a)), rw(offs, a), rw(win))
+
+    def fill(out, c):
+        op("V", lambda e: e.memset(v(out), c), (), rw(out))
+
+    def act(out, a, fn, bias=None, scale=None, offs=None, acc=None):
+        kw = {}
+        if bias is not None:
+            kw["bias"] = sc(bias)
+        if scale is not None:
+            kw["scale"] = scale
+        if acc is not None:
+            kw["accum_out"] = v(acc)
+        src = v(a) if offs is None else v(a).indirect(v(offs))
+        op("S", lambda e: e.activation(v(out), src, fn, **kw), rw(a, bias, offs), rw(out, acc))
+
+    def mm(out, l, rh, st=True, sp=True):
+        op("P", lambda e: e.matmul(v(out), v(l), v(rh), start=st, stop=sp), rw(l, rh), rw(out))
+
+    def to_q(out, lname, src, st=True, sp=True):
+        for b in range(16):
+            op("P", lambda e: e.matmul(v(out), T[lname][:, 128 * b:128 * b + 128], T[src[0]][:, src[1] + b:src[2]:16],
+                                       start=st and b == 0, stop=sp and b == 15), ((lname,), src), rw(out))
+
+    def load(q, out, src, sem):
+        dma(q, lambda e: e.dma_start(v(out), src[:]), sem, (), (out,))
+
+    load("S", ("xin0",), T.xw, "ld0")
+    load("Y", ("wti",), T.wts, "ld1")
+    load("Y", ("lx", 0, W), T.lex, "ld2")
+    load("S", ("thi",), T.th, "ld3")
+    load("Y", ("gin0",), T.gw, "ld4")
+    load("Y", ("lm", 0, W), T.mng, "ld5")
+
+    fill(("ones",), 1.0)
+    fill(("ones64",), 1.0)
+
+    def sel(out, i, pat, o, base, cm, rows=128):
+        op("G", lambda e: e.affine_select(T[out][0:rows, :], T[i][0:rows, :], pat, o, 0.0, base, cm), ((i,),), ((out,),))
+
+    def iota(out, pat, base, cm, **kw):
+        op("G", lambda e: e.iota(T[out][:], pat, base, cm, **kw), (), ((out,),))
+
+    small = {"allow_small_or_imprecise_dtypes": True}
+    sel("bo1", "ones", [[-16, 8], [0, 16]], A.is_ge, 0, 1)
+    sel("bo", "bo1", [[16, 8], [0, 16]], A.is_ge, 15, -1)
+    sel("idn", "ones", [[-1, 128]], A.is_equal, 0, 1)
+    iota("jci", [[0, 1]], 0, 1)
+    iota("io16", [[1, 16]], 0, 0, **small)
+    sel("lt", "bo", [[1, 128]], A.is_gt, 0, -1)
+    sel("gt", "bo", [[-1, 128]], A.is_gt, 0, 1)
+    iota("io0", [[1, 64]], 0, 0, **small)
+    iota("ion", [[1, 64]], -64, 0, **small)
+    iota("dm0", [[16, 16]], W, 0, **small)
+    sel("ra", "ones64", [[-1, 4], [0, 8], [-4, 16]], A.is_equal, 0, 1, 64)
+
+    fill(("cb", 0, 128), 4160.0)
+    fill(("cb", 128, 256), 67584.0)
+    fill(("oz", 0, K), 1.0)
+    fill(("oz", K, 2 * K), 0.0)
+    fill(("lk",), 0.0)
+    ts(("n4096", 0, 128), ("idn",), -4096.0, A.mult)
+    ts(("n4096", 128, 256), ("idn",), -131072.0, A.mult)
+    tt(("bd",), ("bo",), ("idn",), A.subtract)
+    ts(("c1",), ("idn",), -17.0, A.mult)
+    cp(("wf",), ("wti",))
+    ts(("w1", 0, 128), ("bd",), ("wf", 0, 1), A.mult)
+    ts(("w2",), ("bd",), ("wf", 1, 2), A.mult)
+    ts(("w1", 128, 256), ("bd",), ("wf", 0, 1), A.mult, 32.0, A.mult)
+    tt(("e1",), ("bo",), ("c1",), A.add)
+    fill(("lb",), 0.0)
+
+    def blocks(out, src):
+        for k in range(16):
+            act((out, 128 * k + k, 128 * (k + 1), 16), (src, k, 128, 16), F.Copy)
+
+    def consts2():
+        ts(("c2",), ("lt",), 2.0, A.mult)
+        ts(("c3",), ("lt",), 64.0, A.mult)
+        tt(("zb",), ("c2",), ("idn",), A.subtract)
+        tt(("c2",), ("c3",), ("c1",), A.add)
+        tt(("za",), ("c2",), ("gt",), A.add)
+        for t in range(NV):
+            act(("zt", 128 * t, 128 * t + 128), ("zb",), F.Copy)
+        for t in range(NV):
+            act(("zt", 128 * t + t, 128 * t + 128, 16), ("za", t, 128, 16), F.Copy)
+        ts(("jcj",), ("jci",), 15, A.bitwise_and)
+        cp(("id16",), ("idn",))
+        cp(("jc",), ("jcj",))
+        ts(("thc",), ("thi",), -2048.0, A.add, 1 / 64.0, A.mult)
+        ts(("md",), ("io16",), ("jc",), A.is_equal)
+        ts(("thr",), ("md", 0, NV), -0.5, A.add)
+
+    def consts3():
+        cp(("lb16",), ("lb",))
+        ts(("nid",), ("idn",), -1.0, A.mult)
+        cp(("bo16", 0, 128), ("bo",))
+        ts(("bo16", 128, 256), ("bo",), 64.0, A.mult)
+        ts(("bo16", 256, 384), ("bo",), 2048.0, A.mult)
+        ts(("bo64",), ("bo",), 64.0, A.mult)
+        ts(("nb",), ("jc",), -4.0, A.mult, -1.5, A.add)
+        ts(("nid16",), ("idn",), -1.0, A.mult)
+        for i, c in enumerate((-1 / 64.0, 0.5, -0.5)):
+            ts(("idx", 128 * i, 128 * i + 128), ("idn",), c, A.mult)
+        ts(("dmp",), ("dm0",), ("jc",), A.add)
+        ts(("dmq",), ("dmp",), 1 / 16.0, A.mult)
+
+    def consts4():
+        fill(("rm",), 0.5)
+        fill(("rm", 0, K, 16), 32768.0)
+        op("V", lambda e: e.tensor_tensor_scan(v(("thl",)), v(("rm",)), v(("oz", K, 2 * K)), 2.0 ** -13, A.mult, A.add),
+           (("rm",), ("oz", K, 2 * K)), (("thl",),))
+        tt(("pw",), ("md",), ("thl", 0, 16), A.mult)
+        op("V", lambda e: e.tensor_reduce(v(("sm", 0, 1)), v(("pw",)), X.X, A.add), (("pw",),), (("sm", 0, 1),))
+        ts(("bow",), ("bo",), ("sm", 0, 1), A.mult, 0.5, A.mult)
+
+    nxt = T.cores[(rank + 1) % len(T.cores)]
+    rid, pid = topo.addr(nxt)[0], topo.addr(nxt)[1]
+    mask = topo.mask(core, nxt)
+    neng = len(topo.engines(core, nxt))
+
+    def send(src, dst, sem):
+        ready("G", (src,))
+        g.remote_dma(T[dst][:], v(src), T.sem[sem], T.sem.loc, pid, rid, mask)
+
+    lex, mng = ("lx", 0, W), ("lm", 0, W)
+    soon = []
+    late = [consts3, consts4]
+
+    for t in range(NV):
+        XI, GI = ("xin%d" % t,), ("gin%d" % t,)
+        XO, GO = ("xo", K * t, K * t + K), ("go", K * t, K * t + K)
+        if t:
+            arrive("ax%d" % t, neng, (XI,))
+            arrive("ag%d" % t, neng, (GI,))
+        wide = ((0, CH, "pu1", "ppa", "pval"), (CH, K, "pu2", "ph", "ppb"))
+        for c0, c1, bu, b2, b1 in wide:
+            n = c1 - c0
+            for i, w in ((1, ("w2",)), (0, ("w1", 0, 128))):
+                mm((bu, n * (1 - i), n * (2 - i)), w, ("xin%d" % t, c0, c1))
+            for i in (1, 0):
+                act(("fb", K * i + c0, K * i + c1), (bu, n * (1 - i), n * (2 - i)), F.Identity, 130 - 2047.5 / 4096, 1 / 4096.0)
+        for c0, c1, bu, b2, b1 in wide:
+            n = c1 - c0
+            for r, i, q, w in (((b2, 0, n), 1, 0, ("w2",)), ((b1, 0, n), 0, 0, ("w1", 0, 128)), ((b1, n, 2 * n), 0, 128, ("w1", 128, 256))):
+                mm(r, ("cb", q, q + 128), ("oz", 0, n), True, False)
+                mm(r, w, ("xin%d" % t, c0, c1), False, False)
+                mm(r, ("n4096", q, q + 128), ("fb", K * i + c0, K * i + c1), False, True)
+            act(("u2s", c0, c1), (b2, 0, n), F.Copy)
+        mm(("pxp", 0, K), ("idn",), XI)
+
+        def um(c0, c1, q):
+            b, o, n = ("pval", 0, CH) if c1 <= CH else ("ppb", CH, K - CH)
+            return (b, c0 - o + n * q, c1 - o + n * q)
+
+        for chain in CFG["chains"]:
+            for c0, c1 in chain:
+                tt(("pr", c0, c1), ("u2s", c0, c1), um(c0, c1, 0), A.mult)
+            for c0, c1 in chain:
+                tt(("p2", c0, c1), ("pr", c0, c1), um(c0, c1, 1), A.add)
+            for c0, c1 in chain:
+                ts(("h", c0, c1), ("p2", c0, c1), 5, A.arith_shift_right, 4095, A.bitwise_and)
+            for c0, c1 in chain:
+                cp(("hu", c0, c1), ("h", c0, c1))
+            for job in soon:
+                job()
+            soon = []
+        if t == 0:
+            blocks("lk", "e1")
+            blocks("lb", "bo")
+            consts2()
+        vs = K - CFG["vs"]
+        for c in range(0, K, CH):
+            e1 = min(c + CH, vs)
+            act(("cg", 16 * c, 16 * e1), lex, F.Copy, offs=("hu", c, e1))
+
+        def compare(c):
+            bank = "ppa" if c < PARTS[0][1] else "ppb"
+            o = c - (0 if bank == "ppa" else PARTS[1][0])
+            for k in range(16):
+                d0 = 16 * c + k * CH
+                tt(("d", d0, d0 + CH), ("cg", 16 * c + k, 16 * (c + CH), 16), ("pxp", c, c + CH), A.not_equal)
+            for k in range(16):
+                d0 = 16 * c + k * CH
+                mm((bank, o, o + CH), ("lk", 128 * k, 128 * k + 128), ("d", d0, d0 + CH), k == 0, k == 15)
+
+        def pairs(p):
+            p0, p1 = PARTS[p]
+            bank, n = ("ppa", "ppb")[p], p1 - p0
+            ts(("pair", p0, p1), (bank, 0, n), -13.5, A.is_lt)
+            mm((bank, n, 2 * n), ("zt", 128 * t, 128 * t + 128), ("pair", p0, p1))
+
+        def lanes(p):
+            p0, p1 = PARTS[p]
+            bank, n = ("ppa", "ppb")[p], p1 - p0
+            ts(("ep", p0, p1), (bank, n, 2 * n), ("thr", t, t + 1), A.is_lt)
+            tt(("eh", p0, p1), ("ep", p0, p1), ("pu1", p0, p1), A.mult)
+            to_q(("pq", p0 // 16, p1 // 16), "lb16", ("eh", p0, p1))
+
+        def lanes2(p):
+            p0, p1 = PARTS[p]
+            bank, n = ("ppa", "ppb")[p], p1 - p0
+            ts(("t1", K + p0, K + p1), (bank, n, 2 * n), -0.5, A.is_lt, -64.0, A.mult)
+            tt(("t1", p0, p1), ("ep", p0, p1), ("pxp", p0, p1), A.mult)
+
+        def lanes3(p):
+            p0, p1 = PARTS[p]
+            ts(("t1", 2 * K + p0, 2 * K + p1), ("t1", K + p0, K + p1), ("thc",), A.mult)
+
+        def places(p):
+            a0, a1 = PARTS[p][0] // 16, PARTS[p][1] // 16
+            ts(("hq", a0, a1), ("pq", a0, a1), 2048.0, A.add)
+
+        def dist(p):
+            p0, p1 = PARTS[p]
+            bank, n = ("ppa", "ppb")[p], p1 - p0
+            act(("gs", p0, p1), mng, F.Copy, offs=("hq", p0 // 16, p1 // 16))
+            mm((bank, 0, n), ("nid",), ("gin%d" % t, p0, p1), True, False)
+            mm((bank, 0, n), ("idn",), ("gs", p0, p1), False, True)
+            act(("ca", K + p0, K + p1), (bank, 0, n), F.Abs)
+
+        def dist_v(p):
+            p0, p1 = PARTS[p]
+            gat(("gs", p0, p1), mng, ("hq", p0 // 16, p1 // 16), ("gin%d" % t, p0, p1), A.subtract)
+            act(("ca", K + p0, K + p1), ("gs", p0, p1), F.Abs)
+
+        def first_q(p):
+            for b in range(16):
+                op("P", lambda e: e.matmul(T.ph[:, 24 * p:24 * p + 24], T.lb16[:, 128 * b:128 * b + 128],
+                                           T.t1[:, :, PARTS[p][0] + b:PARTS[p][1]:16], start=b == 0, stop=b == 15),
+                   (("lb16",),) + tuple(("t1", K * i + PARTS[p][0], K * i + PARTS[p][1]) for i in range(3)), (("ph", 24 * p, 24 * p + 24),))
+
+        def first_x(p):
+            o = 24 * p
+            tt(("xq", 8 * p, 8 * p + 8), ("qs", o, o + 8), ("qs", o + 8, o + 16), A.add)
+
+        def first_th(p, i):
+            o, q = 24 * p, (8 * p, 8 * p + 8)
+            if i == 0:
+                ts(("q1",) + q, ("qs", o + 8, o + 16), -32.0, A.mult)
+            else:
+                tt(("thq",) + q, ("q1",) + q, ("qs", o + 16, o + 24), A.subtract)
+
+        def xhot(a0, a1):
+            for a in range(a0, a1):
+                ts(("xh", 64 * a, 64 * a + 64), ("ion",), ("xq", a, a + 1), A.is_equal)
+
+        def letter(p):
+            p0, p1 = PARTS[p]
+            gat(("ca", p0, p1), lex, ("hq", p0 // 16, p1 // 16), ("ep", p0, p1), A.mult)
+
+        ts(("h16",), ("hu",), -2048.0, A.add)
+        if CFG["lm"] or not t:
+            for job in late:
+                job()
+            late = []
+        def share():
+            op("V", lambda e: e.tensor_copy(v(("cg", 16 * vs, 4096)), v(lex).indirect(v(("hu", vs, K)))), (lex, ("hu", vs, K)), (("cg", 16 * vs, 4096),))
+        compare(0)
+        mm(("pu1", 0, K), ("id16",), ("h16",))
+        for job in late:
+            job()
+        late = []
+        compare(CH)
+        if vs < K:
+            share()
+        if PARTS[0][1] == 2 * CH:
+            pairs(0)
+        compare(2 * CH)
+        if PARTS[0][1] == 3 * CH:
+            pairs(0)
+        lanes(0)
+        compare(3 * CH)
+        lanes2(0)
+        pairs(1)
+        lanes3(0)
+        first_q(0)
+        places(0)
+        dist(0)
+        letter(0)
+        lanes(1)
+        lanes2(1)
+        cp(("qs", 0, 24), ("ph", 0, 24))
+        lanes3(1)
+        first_x(0)
+        first_th(0, 0)
+        first_q(1)
+        k1 = CFG["xk"]
+        xhot(0, k1)
+        places(1)
+        first_th(0, 1)
+        if CFG["gv"]:
+            dist_v(1)
+        else:
+            dist(1)
+        letter(1)
+        cp(("qs", 24, 48), ("ph", 24, 48))
+        nx, ns = 16 - CFG["xs"], 16 - CFG["cs"]
+        k2 = min(8, nx)
+        xhot(k1, k1 + 1)
+        first_x(1)
+        first_th(1, 0)
+        xhot(k1 + 1, k1 + 2)
+        first_th(1, 1)
+        xhot(k1 + 2, k2)
+        for a in range(nx, 16):
+            act(("xa", 64 * a, 64 * a + 64), ("ion",), F.Abs, ("xq", a, a + 1), -1.0)
+        act(("xh", 64 * nx, 1024), ("xa", 64 * nx, 1024), F.Relu, 1.0, -1.0)
+        xhot(max(k2, k1 + 2), nx)
+        to_q(("pq", 32, 64), "lb", ("ca", 0, 2 * K))
+        tt(("nf",), ("pq", 48, 64), ("thq",), A.is_ge)
+        cp(("cq",), ("pq", 32, 48))
+        ts(("xi",), ("xq",), 64.0, A.mult)
+        for a in range(ns, 16):
+            act(("xa", 64 * (a - ns), 64 * (a - ns) + 64), ("io0",), F.Abs, ("cq", a, a + 1), -1.0)
+        for a in range(ns, 16):
+            act(("chh", 64 * a, 64 * a + 64), ("xa", 64 * (a - ns), 64 * (a - ns) + 64), F.Relu, ("nf", a, a + 1), -1.0)
+        for a in range(ns):
+            ts(("chh", 64 * a, 64 * a + 64), ("io0",), ("pq", 32 + a, 33 + a), A.is_equal, ("nf", a, a + 1), A.mult)
+        mm(("pxp", K, 2 * K), ("id16",), ("t1", 0, K), True, False)
+        mm(("pxp", K, 2 * K), ("nid",), ("ca", 0, K), False, True)
+        mm(("pval", K, 2 * K), ("bo16", 0, 128), ("t1", 0, K))
+        act(("mt",), ("pval", K, 2 * K), F.Abs, ("nb",))
+        act(("rm",), ("mt",), F.Relu, 32768.0, -16384.0)
+
+        for a in range(16):
+            x, c = ("xh", 64 * a, 64 * a + 64), ("chh", 64 * a, 64 * a + 64)
+            for l, r in ((x, c), (c, x)):
+                op("P", lambda e: e.matmul(T.ph[0:64, 0:64], v(l), v(r), start=a == 0 and l is x, stop=a == 15 and l is c),
+                   (l, r), (("ph", 0, 64),))
+        ts(("x3",), ("xi",), 192, A.bitwise_and)
+        tt(("th2",), ("thq",), ("pq", 48, 64), A.subtract)
+        tt(("x3",), ("pq", 32, 48), ("x3",), A.add)
+        tt(("en",), ("pxp", K, 2 * K), ("t1", K, 2 * K), A.mult)
+        act(("ndx",), ("en",), F.Relu, None, -1 / 64.0)
+        mm(("ppb", 0, K), ("bo16", 0, 128), ("eh",))
+        op("V", lambda e: e.tensor_scalar(T.h1[0:64, :], T.ph[0:64, 0:64], 1.0, None, A.min), (("ph", 0, 64),), (("h1",),))
+        for q in range(4):
+            op("P", lambda e: e.matmul(T.ph[:, K + 64 * q:K + 64 * q + 64], T.ra[0:64, 128 * q:128 * q + 128], T.h1[0:64, :],
+                                       start=True, stop=True), (("ra",), ("h1",)), (("ph", K + 64 * q, K + 64 * q + 64),))
+        act(("tb",), ("ph", K, 2 * K), F.Copy)
+        cp(("of",), ("x3",))
+        ts(("hr",), ("ppb", 0, K), 2048.0, A.add)
+        ts(("q2",), ("th2",), 0.0, A.is_le, 8192.0, A.mult)
+        cp(("hqf",), ("hq",))
+        mm(("pu1", 0, K), ("idn",), XI, True, False)
+        mm(("pu1", 0, K), ("idn",), ("ca", 0, K), False, False)
+        mm(("pu1", 0, K), ("nid16",), ("t1", 0, K), False, False)
+        mm(("pu1", 0, K), ("idx", 0, 128), ("en",), False, True)
+        act(("xb",), ("pu1", 0, K), F.Copy)
+        for p in (0, 1):
+            p0, p1 = PARTS[p]
+            src = ("gs", p0, p1) if p and CFG["gv"] else (("ppa", "ppb")[p], 0, p1 - p0)
+            act(("dg1", p0, p1), src, F.Identity, -0.25, 0.5)
+        act(("dg2",), ("dg1",), F.Identity, 12582912.0)
+        val = ("pval", 0, K)
+        mm(val, ("bo64",), ("ca", K, 2 * K), True, False)
+        mm(val, ("bo16", 128, 256), ("t1", 2 * K, 3 * K), False, False)
+        mm(val, ("bo16", 256, 384), ("t1", K, 2 * K), False, False)
+        mm(val, ("idn",), ("xb",), False, False)
+        gat(("f",), ("tb",), ("of",), ("rm",), A.mult)
+        mm(val, ("bo64",), ("f",), False, True)
+        tt(("nx",), ("pu1", 0, K), ("ndx",), A.subtract)
+        tt(("hqx",), ("q2",), ("hqf",), A.add)
+        tt(("yv",), val, ("nx",), A.max)
+        tt(XO, ("yv",), ("pu1", 0, K), A.min)
+        send(XO, "xin%d" % (t + 1), "ax%d" % (t + 1))
+        act(("pval", K, 2 * K), val, F.Sign, 0.5)
+        to_q(("pq", 80, 96), "lb", ("f", 0, K))
+        nv = 16 - CFG["eqs"]
+        tt(("sq",), ("hqx",), ("pq", 80, 96), A.add)
+        ts(("hqs", nv, 16), ("sq", nv, 16), -2048.0, A.add)
+        for a in range(nv, 16):
+            e0 = 128 * (a - 8)
+            act(("ea", e0, e0 + K - 16 * a), ("ppb", 16 * a, K), F.Abs, ("hqs", a, a + 1), -1.0)
+        for a in range(nv, 16):
+            e0 = 128 * (a - 8)
+            op("S", lambda e: e.activation(T.eq[:, a, 0:K - 16 * a], v(("ea", e0, e0 + K - 16 * a)), F.Relu, bias=1.0, scale=-1.0),
+               (("ea", e0, e0 + K - 16 * a),), (("eq", 272 * a, 256 * a + 256),))
+        for a in range(nv):
+            op("V", lambda e: e.tensor_scalar(T.eq[:, a, 0:K - 16 * a], v(("hr", 16 * a, K)), v(("sq", a, a + 1)), None, A.is_equal),
+               (("hr",), ("sq",)), (("eq", 272 * a, 256 * a + 256),))
+        tt(("nm",), ("pq", 80, 96), ("th2",), A.is_ge)
+        tt(("nm",), ("nm",), ("dmp",), A.mult)
+        tt(("hqm",), ("nm",), ("hqf",), A.max)
+        mm(("ph", 0, K), ("bo",), ("oz", K, 2 * K), True, False)
+        for a in range(15):
+            op("P", lambda e: e.matmul(T.ph[:, 16 * a + 16:K], v(("bo64",)), T.eq[:, a, 16:K - 16 * a], start=False, stop=False),
+               (("bo64",), ("eq", 272 * a, 256 * a + 256)), (("ph", 0, K),))
+        op("P", lambda e: e.matmul(T.ph[:, 0:K], v(("bow",)), T.eq[:, :, 0:16], start=False, stop=True),
+           (("bow",), ("eq", 0, 4096)), (("ph", 0, K),))
+        act(("dg",), ("dg2",), F.Identity, -12582912.0)
+        tt(("gm",), ("dg",), ("pval", K, 2 * K), A.mult)
+        tt(("ls",), ("ph", 0, K), ("thl",), A.is_ge)
+        to_q(("pq", 64, 80), "lb", ("ls", 0, K))
+        mm(("pxp", K, 2 * K), ("idn",), GI, True, False)
+        mm(("pxp", K, 2 * K), ("idx", 128, 256), ("dg",), False, False)
+        mm(("pxp", K, 2 * K), ("idx", 256, 384), ("gm",), False, True)
+        tt(("lq2",), ("pq", 64, 80), ("dmq",), A.mult)
+        tt(("lq2",), ("hqm",), ("lq2",), A.max)
+        cp(("so",), ("lq2",))
+        scat(("lx",), ("so",), XO)
+
+        def new_meanings(GO=GO, t=t):
+            cp(GO, ("pxp", K, 2 * K))
+            send(GO, "gin%d" % (t + 1), "ag%d" % (t + 1))
+        if CFG["go"] and t < NV - 1:
+            soon.append(new_meanings)
+        else:
+            new_meanings()
+
+        def meanings(GO=GO):
+            scat(("lm",), ("so",), GO)
+        late.append(meanings)
+
+    def store(q, y, a, sem):
+        dma(q, lambda e: e.dma_start(y[:], v(a)), sem, (a,), ())
+
+    for job in late:
+        job()
+    arrive("ax%d" % NV, neng, (("xin%d" % NV,),))
+    arrive("ag%d" % NV, neng, (("gin%d" % NV,),))
+    store("Y", T.yx, ("xin%d" % NV,), "st1")
+    store("Y", T.yl, lex, "st0")
+    store("Y", T.yg, ("gin%d" % NV,), "st2")
+    h = W // 2
+    op("V", lambda e: e.tensor_reduce(T.sm[:, 0:1], T.lm[:, 0:h], X.X, A.add), (("lm", 0, h),), (("sm", 0, 1),))
+    act(("cg", 0, h), ("lm", h, W), F.Copy, acc=("sm", 1, 2))
+    tt(("sm", 2, 3), ("sm", 0, 1), ("sm", 1, 2), A.add)
+    store("S", T.ym, ("sm", 2, 3), "st3")
+    for i in range(4):
+        g.wait_ge(T.sem["st%d" % i], 16)
+    g.wait_ge(T.sem.loc, 2 * NV * neng)
+    finish()

@@ -4,8 +4,7 @@ K = 256
 W = 4096
 NV = 4
 CH = 64
-PARTS = ((0, 128), (128, 256))
-CFG = {"xs": 6, "cs": 4, "eqs": 6, "chains": (((0, 64),), ((64, 128), (128, 192), (192, 256))), "lm": 1, "gv": 1, "xk": 3, "vs": 16, "go": 1}
+CFG = {"parts": ((0, 128), (128, 256)), "vs": 32, "eqs": 5, "nsc": 1, "xs": (0, 0, 0, 0), "mn": (1, 1, 1, 1), "xq": 0, "gc": 64, "wait": 0.17, "far": 2.0, "pe": 0.55, "hs": 64, "fill": 0.1}
 
 SCRATCH = {}
 
@@ -18,118 +17,165 @@ for _t in range(NV + 1):
     _buf("xin%d" % _t, K, "bfloat16")
     _buf("gin%d" % _t, K, "bfloat16")
 for _d, _l in (
-        ("bfloat16", (("xo", NV * K), ("go", NV * K), ("zt", NV * 128), ("lx", W + K), ("lm", W + K), ("ones", 128), ("ones64", 512),
-                      ("bo1", 128), ("bo", 128), ("idn", 128), ("lt", 128), ("gt", 128), ("c1", 128), ("c2", 128), ("c3", 128),
-                      ("zb", 128), ("za", 128), ("e1", 128), ("bd", 128), ("w1", 256), ("w2", 128), ("lk", 2048), ("lb", 2048),
-                      ("bow", 128), ("thl", K), ("nid", 128), ("idx", 384), ("bo64", 128), ("n4096", 256), ("cb", 256), ("xb", K), ("nx", K),
-                      ("oz", 512), ("ra", 512), ("io0", 64), ("ion", 64), ("fb", 512), ("cg", 4096), ("d", 4096), ("pair", K),
-                      ("ep", K), ("gs", K), ("ca", 2 * K), ("dg", K), ("gm", K), ("en", K), ("ndx", K), ("xa", 1024), ("xh", 1024),
-                      ("chh", 1024), ("h1", 64), ("tb", K), ("rm", K), ("f", K), ("ea", 2048), ("ls", K))),
-        ("float16", (("lb16", 2048), ("id16", 128), ("nid16", 128), ("bo16", 384), ("h16", K), ("eh", K))),
-        ("int32", (("wti", 2), ("thi", 1), ("jci", 1), ("jcj", 1), ("pr", K), ("p2", K), ("h", K), ("xi", 16), ("x3", 16))),
+        ("bfloat16", (("xo", NV * K), ("go", NV * K), ("lx", W + K), ("lm", W + K), ("ones", 512),
+                      ("bo1", 128), ("bo", 128), ("idn", 128), ("lt", 128), ("c1", 128), ("e1", 128), ("bd", 128), ("w1", 256), ("w2", 128),
+                      ("lk", 2048), ("lb", 2048), ("nlb", 512), ("ids", 6 * 128), ("bos", 7 * 128), ("zb", 128), ("cb", 3 * 128), ("cbr", 384),
+                      ("c120", K), ("bow", 128), ("thl", K), ("thr", K), ("drow", K), ("ia", K), ("ib", K), ("ra", 512), ("io2", 64),
+                      ("sel", 32), ("fb", 2 * K), ("cg", 16 * K), ("d", 16 * K), ("sg", K), ("xq", K), ("xa", K), ("xl", K), ("nn", K), ("yy", K),
+                      ("gs", K), ("mn", K), ("mx", K), ("xn", K), ("ms", K), ("dg", K), ("gm", K), ("xh", 1024), ("chh", 1024), ("xt", 1024),
+                      ("h1", 64), ("tb", K), ("f", K), ("ea", 2048), ("ls", K), ("zero", K))),
+        ("float16", (("lb16", 2048), ("id16", 128), ("bo16", 128), ("h16", K), ("eh", K), ("io9", 64))),
+        ("int32", (("wti", 2), ("thi", 1), ("tha", 2), ("jci", 1), ("jcj", 1), ("pr", K), ("p2", K), ("h", K))),
         ("uint16", (("hu", K), ("hq", 16), ("of", 16), ("hr", K), ("so", 16))),
-        ("float32", (("thr", NV), ("wf", 2), ("thc", 1), ("jc", 1), ("io16", 16), ("md", 16), ("dm0", 16), ("dmp", 16), ("dmq", 16), ("pw", 16),
-                     ("nb", 1), ("u2s", K), ("hqf", 16), ("qs", 48), ("xq", 16), ("q1", 16), ("thq", 16), ("th2", 16), ("q2", 16), ("hqx", 16), ("sq", 16), ("cq", 16),
-                     ("nf", 16), ("dg1", K), ("dg2", K), ("mt", K), ("yv", K), ("nm", 16), ("hqm", 16), ("hqs", 16),
-                     ("lq2", 16), ("sm", 3)))):
+        ("float32", (("wf", 2), ("thf", 2), ("jc", 1), ("io16", 16), ("md", 16), ("pw", 16), ("col", 8), ("u2s", K), ("hqf", 16), ("tsum", 12),
+                     ("nf", 16), ("xw2", 32), ("sq", 16), ("hqs", 16), ("dg1", K), ("lq", 16), ("sm", 3)))):
     for _n, _c in _l:
         _buf(_n, _c, _d)
-SCRATCH["t1"] = ("sbuf", [128, 3, K], "float16")
 SCRATCH["eq"] = ("sbuf", [128, 16, 272], "bfloat16")
-for _n in ("pu1", "pu2", "pxp", "ppa", "ppb", "pq", "pval", "ph"):
+for _n in ("pxp", "pca", "pcb", "psb", "phv", "pq", "pwd", "ptb"):
     _buf(_n, 512, "float32", "psum")
 
 SEMAPHORES = ["v", "s", "p", "gc", "loc"]
 SEMAPHORES += ["ld%d" % _i for _i in range(6)] + ["st%d" % _i for _i in range(4)]
 SEMAPHORES += ["ax%d" % _i for _i in range(1, NV + 1)] + ["ag%d" % _i for _i in range(1, NV + 1)]
 
+CYCLE = 0.83e-3
+BIG = 2.0 ** 27
 
-def tracker(g, T):
-    queue = {"V": g.vector, "S": g.scalar, "P": g.tensor, "G": g, "Y": g.sync}
-    own = {"V": "v", "S": "s", "P": "p", "G": "gc"}
-    total = {}
-    know = {q: {} for q in queue}
-    log = {}
 
-    def span(a):
-        if len(a) == 1:
-            return a[0], 0, SCRATCH[a[0]][1][1]
-        return a
+def span(a):
+    return (a[0], 0, SCRATCH[a[0]][1][1]) if len(a) == 1 else a[:3]
 
-    def need(q, reads, writes):
-        found = []
-        for wr, accs in ((False, reads), (True, writes)):
+
+def order(calls):
+    log, banks, sent = {}, {}, {}
+    for i, c in enumerate(calls):
+        dep = {}
+        for wr, accs in ((False, c["r"]), (True, c["w"])):
             for a in accs:
                 name, lo, hi = span(a)
-                bank = SCRATCH[name][0] == "psum"
-                for r in log.get(name, ()):
-                    lap = r["lo"] < hi and lo < r["hi"]
-                    if bank and r["q"] != q:
-                        found.append(r)
-                    elif lap and (r["wr"] or wr):
-                        if bank and q == "P":
-                            continue
-                        found.append(r)
-        return found
+                for j, l, h, w in log.get(name, ()):
+                    if l < hi and lo < h and (w or wr):
+                        dep[j] = CFG["wait"]
+        for name in {span(a)[0] for a in c["r"] + c["w"] if SCRATCH[a[0]][0] == "psum"}:
+            b = banks.setdefault(name, {"q": None, "now": [], "before": []})
+            if b["q"] != c["q"]:
+                b["q"], b["before"], b["now"] = c["q"], b["now"], []
+            for j in b["before"]:
+                dep[j] = CFG["wait"]
+            if c["q"] == "P":
+                for j in b["now"]:
+                    dep[j] = 0.0
+                b["now"] = b["now"][-1:]
+            b["now"].append(i)
+        if c["q"] == "A":
+            dep[sent[c["sem"]]] = 0.0
+        if "sent" in c:
+            sent[c["sent"]] = i
+        for wr, accs in ((True, c["w"]), (False, c["r"])):
+            for a in accs:
+                name, lo, hi = span(a)
+                rows = log.setdefault(name, [])
+                if wr:
+                    rows[:] = [r for r in rows if not (lo <= r[1] and r[2] <= hi)]
+                rows.append((i, lo, hi, wr))
+        dep.pop(i, None)
+        c["dep"], c["next"], c["left"], c["at"] = dep, [], len(dep), 0.0
+        for j in dep:
+            calls[j]["next"].append(i)
+    for i in reversed(range(len(calls))):
+        c = calls[i]
+        c["way"] = c["cost"] + c["lag"] + max([calls[j]["way"] + calls[j]["dep"][i] for j in c["next"]], default=0.0) + c.get("first", 0.0)
+    free = {q: 0.0 for q in "VSPGYA"}
+    ready = {q: [] for q in free}
+    for i, c in enumerate(calls):
+        if not c["left"]:
+            ready[c["q"]].append(i)
+    out = []
+    while len(out) < len(calls):
+        q = min((q for q in free if ready[q]), key=lambda q: max(free[q], min(calls[i]["at"] for i in ready[q])))
+        best = max(ready[q], key=lambda i: (calls[i]["way"], -i))
+        fits = [i for i in ready[q] if max(free[q], calls[i]["at"]) + calls[i]["cost"] <= calls[best]["at"] + CFG["fill"]]
+        if fits:
+            now = max(free[q], min(calls[i]["at"] for i in fits))
+            best = max((i for i in fits if calls[i]["at"] <= now), key=lambda i: (calls[i]["way"], -i))
+        c = calls[best]
+        ready[q].remove(best)
+        free[q] = max(free[q], c["at"]) + c["cost"]
+        out.append(c)
+        for j in c["next"]:
+            n = calls[j]
+            n["at"] = max(n["at"], free[q] + c["lag"] + n["dep"][best])
+            n["left"] -= 1
+            if not n["left"]:
+                ready[n["q"]].append(j)
+    return out
 
-    def wait(q, found):
-        for r in sorted(found, key=lambda r: -r["seq"]):
-            if know[q].get(r["sem"], 0) < r["val"]:
-                queue[q].wait_ge(T.sem[r["sem"]], r["val"])
-                for s, v in r["clock"].items():
-                    know[q][s] = max(know[q].get(s, 0), v)
 
-    seq = [0]
-
-    def note(q, sem, val, clock, reads, writes, dma):
-        seq[0] += 1
-        for wr, accs in ((True, writes), (False, reads)):
+def issue(g, T, calls):
+    queue = {"V": g.vector, "S": g.scalar, "P": g.tensor, "G": g, "Y": g.sync}
+    own = {"V": "v", "S": "s", "P": "p", "G": "gc"}
+    total, log = {}, {}
+    know = {q: {} for q in queue}
+    for seq, c in enumerate(calls):
+        q, sem = c["q"], c.get("sem")
+        if q == "A":
+            val, clock = c["val"], {sem: c["val"]}
+        else:
+            found = []
+            for wr, accs in ((False, c["r"]), (True, c["w"])):
+                for a in accs:
+                    name, lo, hi = span(a)
+                    bank = SCRATCH[name][0] == "psum"
+                    for r in log.get(name, ()):
+                        if bank and r["q"] != q:
+                            found.append(r)
+                        elif r["lo"] < hi and lo < r["hi"] and (r["wr"] or wr) and not (bank and q == "P"):
+                            found.append(r)
+            for r in sorted(found, key=lambda r: -r["seq"]):
+                if know[q].get(r["sem"], 0) < r["val"]:
+                    queue[q].wait_ge(T.sem[r["sem"]], r["val"])
+                    for s, x in r["clock"].items():
+                        know[q][s] = max(know[q].get(s, 0), x)
+            if "sent" in c:
+                c["call"](g)
+                continue
+            if sem:
+                val = 16
+                c["call"](queue[q]).then_inc(T.sem[sem], 16)
+            else:
+                sem = own[q]
+                c["call"](queue[q]).then_inc(T.sem[sem], 1)
+                val = total[sem] = total.get(sem, 0) + 1
+            clock = dict(know[q])
+            clock[sem] = val
+        for wr, accs in ((True, c["w"]), (False, c["r"])):
             for a in accs:
                 name, lo, hi = span(a)
                 rows = log.setdefault(name, [])
                 if wr:
                     rows[:] = [r for r in rows if not (lo <= r["lo"] and r["hi"] <= hi)]
-                rows.append({"q": q, "sem": sem, "val": val, "clock": clock, "lo": lo, "hi": hi, "wr": wr, "dma": dma, "seq": seq[0]})
-
-    def op(q, call, reads=(), writes=()):
-        wait(q, need(q, reads, writes))
-        sem = own[q]
-        call(queue[q]).then_inc(T.sem[sem], 1)
-        total[sem] = total.get(sem, 0) + 1
-        clock = dict(know[q])
-        clock[sem] = total[sem]
-        note(q, sem, total[sem], clock, reads, writes, False)
-
-    def dma(q, call, sem, reads=(), writes=()):
-        wait(q, need(q, reads, writes))
-        call(queue[q]).then_inc(T.sem[sem], 16)
-        clock = dict(know[q])
-        clock[sem] = 16
-        note("dma", sem, 16, clock, reads, writes, True)
-
-    def arrive(sem, val, writes):
-        note("dma", sem, val, {sem: val}, (), writes, True)
-
-    def ready(q, reads):
-        wait(q, need(q, reads, ()))
-
-    def finish():
-        for sem, q in (("v", "G"), ("s", "G"), ("p", "G"), ("gc", "V")):
-            if know[q].get(sem, 0) < total[sem]:
-                queue[q].wait_ge(T.sem[sem], total[sem])
-
-    return op, dma, arrive, ready, finish
+                rows.append({"q": "dma" if c.get("sem") else q, "sem": sem, "val": val, "clock": clock, "lo": lo, "hi": hi, "wr": wr, "seq": seq})
+    for sem, q in (("v", "G"), ("s", "G"), ("p", "G"), ("gc", "V")):
+        if know[q].get(sem, 0) < total[sem]:
+            queue[q].wait_ge(T.sem[sem], total[sem])
 
 
 def rank_program(g, core, T, topo):
     rank = T.rank_of(core)
     if rank is None:
         return
-    op, dma, arrive, ready, finish = tracker(g, T)
+    calls = []
+    parts = CFG["parts"]
+
+    def op(q, call, reads, writes, cost, lag=0.0, **more):
+        calls.append(dict(more, q=q, call=call, r=tuple(reads), w=tuple(writes), cost=cost, lag=lag))
 
     def v(a):
-        if a[0] == "t1":
-            return T.t1[:, a[1] // K, a[1] % K:a[1] % K + a[2] - a[1]]
+        if a[0] == "eq" and len(a) > 1:
+            return T.eq[:, a[1] // 272, a[1] % 272:a[1] % 272 + a[2] - a[1]]
+        if len(a) == 6:
+            return T[a[0]][a[4]:a[5], a[1]:a[2]:a[3]]
         return T[a[0]][:] if len(a) == 1 else T[a[0]][:, a[1]:a[2]] if len(a) == 3 else T[a[0]][:, a[1]:a[2]:a[3]]
 
     def rw(*a):
@@ -138,137 +184,153 @@ def rank_program(g, core, T, topo):
     def sc(x):
         return v(x) if isinstance(x, tuple) else x
 
+    def cols(a):
+        return len(range(span(a)[1], span(a)[2], a[3] if len(a) > 3 else 1))
+
+    def cyc(n, *sides):
+        narrow = all(SCRATCH[a[0]][2] in ("bfloat16", "float16", "uint16") for a in sides)
+        return CYCLE * max(64, n / 2 if sides and narrow else n)
+
     def ts(out, i0, s1, o0, s2=None, o1=None):
-        if o1 is None:
-            op("V", lambda e: e.tensor_scalar(v(out), v(i0), sc(s1), None, o0), rw(i0, s1), rw(out))
-        else:
-            op("V", lambda e: e.tensor_scalar(v(out), v(i0), sc(s1), sc(s2), o0, o1), rw(i0, s1, s2), rw(out))
+        more = (None, o0) if o1 is None else (sc(s2), o0, o1)
+        op("V", lambda e: e.tensor_scalar(v(out), v(i0), sc(s1), *more), rw(i0, s1, s2), rw(out), cyc(cols(out), out, i0))
 
     def tt(out, a, b, o):
-        op("V", lambda e: e.tensor_tensor(v(out), v(a), v(b), o), rw(a, b), rw(out))
+        both = SCRATCH[a[0]][0] == SCRATCH[b[0]][0]
+        op("V", lambda e: e.tensor_tensor(v(out), v(a), v(b), o), rw(a, b), rw(out), cyc(cols(out) * (2 if both else 1)))
 
     def gat(out, win, offs, b, o):
-        op("V", lambda e: e.tensor_tensor(v(out), v(win).indirect(v(offs)), v(b), o), rw(win, offs, b), rw(out))
+        op("V", lambda e: e.tensor_tensor(v(out), v(win).indirect(v(offs)), v(b), o), rw(win, offs, b), rw(out), 0.05 + 1.56 * CYCLE * cols(out))
+
+    def pick(out, win, offs):
+        op("V", lambda e: e.tensor_copy(v(out), v(win).indirect(v(offs))), rw(win, offs), rw(out), 0.05 + 1.56 * CYCLE * cols(out))
 
     def cp(out, a):
-        op("V", lambda e: e.tensor_copy(v(out), v(a)), rw(a), rw(out))
+        op("V", lambda e: e.tensor_copy(v(out), v(a)), rw(a), rw(out), cyc(cols(out), out, a))
 
     def scat(win, offs, a):
-        op("V", lambda e: e.tensor_copy(v(win).indirect(v(offs)), v(a)), rw(offs, a), rw(win))
+        op("V", lambda e: e.tensor_copy(v(win).indirect(v(offs)), v(a)), rw(offs, a), rw(win), 0.05 + 3.8 * CYCLE * cols(a))
 
     def fill(out, c):
-        op("V", lambda e: e.memset(v(out), c), (), rw(out))
+        op("V", lambda e: e.memset(v(out), c), (), rw(out), cyc(cols(out), out))
 
     def act(out, a, fn, bias=None, scale=None, offs=None, acc=None):
         kw = {}
         if bias is not None:
             kw["bias"] = sc(bias)
         if scale is not None:
-            kw["scale"] = scale
+            kw["scale"] = sc(scale)
         if acc is not None:
             kw["accum_out"] = v(acc)
         src = v(a) if offs is None else v(a).indirect(v(offs))
-        op("S", lambda e: e.activation(v(out), src, fn, **kw), rw(a, bias, offs), rw(out, acc))
+        op("S", lambda e: e.activation(v(out), src, fn, **kw), rw(a, bias, scale, offs), rw(out, acc),
+           cyc(cols(out)) if offs is None else 0.065 + 1.56 * CYCLE * cols(out))
 
-    def mm(out, l, rh, st=True, sp=True):
-        op("P", lambda e: e.matmul(v(out), v(l), v(rh), start=st, stop=sp), rw(l, rh), rw(out))
+    def mm(out, l, rh, st=True, sp=True, ap=None):
+        op("P", lambda e: e.matmul(v(out), v(l), v(rh) if ap is None else ap, start=st, stop=sp), rw(l, rh), rw(out),
+           CFG["pe"] * CYCLE * max(min(64, cols(l)), cols(out)))
 
-    def to_q(out, lname, src, st=True, sp=True):
-        for b in range(16):
-            op("P", lambda e: e.matmul(v(out), T[lname][:, 128 * b:128 * b + 128], T[src[0]][:, src[1] + b:src[2]:16],
-                                       start=st and b == 0, stop=sp and b == 15), ((lname,), src), rw(out))
+    def mms(out, terms):
+        for i, (l, rh) in enumerate(terms):
+            mm(out, l, rh, i == 0, i == len(terms) - 1)
 
-    def load(q, out, src, sem):
-        dma(q, lambda e: e.dma_start(v(out), src[:]), sem, (), (out,))
+    def to_q(out, lname, *srcs):
+        mms(out, [((lname, 128 * b, 128 * b + 128), (s[0], s[1] + b, s[2], 16)) for s in srcs for b in range(16)])
 
-    load("S", ("xin0",), T.xw, "ld0")
-    load("Y", ("wti",), T.wts, "ld1")
-    load("Y", ("lx", 0, W), T.lex, "ld2")
-    load("S", ("thi",), T.th, "ld3")
-    load("Y", ("gin0",), T.gw, "ld4")
-    load("Y", ("lm", 0, W), T.mng, "ld5")
+    def dma(q, out, src, sem, reads, writes, lag, **more):
+        op(q, lambda e: e.dma_start(out, src), reads, writes, 0.05, lag, sem=sem, **more)
 
-    fill(("ones",), 1.0)
-    fill(("ones64",), 1.0)
-
-    def sel(out, i, pat, o, base, cm, rows=128):
-        op("G", lambda e: e.affine_select(T[out][0:rows, :], T[i][0:rows, :], pat, o, 0.0, base, cm), ((i,),), ((out,),))
+    def sel(out, i, pat, o, base, cm):
+        op("G", lambda e: e.affine_select(v(out), v(i), pat, o, 0.0, base, cm), rw(i), rw(out), 0.17 + 2 * CYCLE * cols(out))
 
     def iota(out, pat, base, cm, **kw):
-        op("G", lambda e: e.iota(T[out][:], pat, base, cm, **kw), (), ((out,),))
+        op("G", lambda e: e.iota(T[out][:], pat, base, cm, **kw), (), ((out,),), 0.13 + 2 * CYCLE * cols((out,)))
+
+    def block(name, i):
+        return (name, 128 * i, 128 * i + 128)
+
+    for i, (q, out, src, lag) in enumerate((("S", ("xin0",), T.xw, 1.5), ("Y", ("wti",), T.wts, 1.5), ("Y", ("lx", 0, W), T.lex, 5.0),
+                                            ("S", ("thi",), T.th, 1.5), ("Y", ("gin0",), T.gw, 5.5), ("Y", ("lm", 0, W), T.mng, 9.0))):
+        dma(q, v(out), src[:], "ld%d" % i, (), (out,), lag, first=1e4 - 1e3 * i)
 
     small = {"allow_small_or_imprecise_dtypes": True}
-    sel("bo1", "ones", [[-16, 8], [0, 16]], A.is_ge, 0, 1)
-    sel("bo", "bo1", [[16, 8], [0, 16]], A.is_ge, 15, -1)
-    sel("idn", "ones", [[-1, 128]], A.is_equal, 0, 1)
+    one = ("ones", 0, 128)
+    fill(("ones",), 1.0)
+    sel(("bo1",), one, [[-16, 8], [0, 16]], A.is_ge, 0, 1)
+    sel(("bo",), ("bo1",), [[16, 8], [0, 16]], A.is_ge, 15, -1)
+    sel(("idn",), one, [[-1, 128]], A.is_equal, 0, 1)
     iota("jci", [[0, 1]], 0, 1)
     iota("io16", [[1, 16]], 0, 0, **small)
-    sel("lt", "bo", [[1, 128]], A.is_gt, 0, -1)
-    sel("gt", "bo", [[-1, 128]], A.is_gt, 0, 1)
-    iota("io0", [[1, 64]], 0, 0, **small)
-    iota("ion", [[1, 64]], -64, 0, **small)
-    iota("dm0", [[16, 16]], W, 0, **small)
-    sel("ra", "ones64", [[-1, 4], [0, 8], [-4, 16]], A.is_equal, 0, 1, 64)
+    sel(("lt",), ("bo",), [[1, 128]], A.is_gt, 0, -1)
+    iota("io2", [[1, 64]], 2, 0, **small)
+    iota("ia", [[32, 16], [0, 16]], 0, 0, **small)
+    iota("ib", [[0, 16], [2, 16]], 0, 0, **small)
+    sel(("ra", 0, 512, 1, 0, 64), ("ones", 0, 512, 1, 0, 64), [[-1, 4], [0, 8], [-4, 16]], A.is_equal, 0, 1)
 
-    fill(("cb", 0, 128), 4160.0)
-    fill(("cb", 128, 256), 67584.0)
-    fill(("oz", 0, K), 1.0)
-    fill(("oz", K, 2 * K), 0.0)
-    fill(("lk",), 0.0)
-    ts(("n4096", 0, 128), ("idn",), -4096.0, A.mult)
-    ts(("n4096", 128, 256), ("idn",), -131072.0, A.mult)
+    fill(("cbr", 0, 192), 4160.0)
+    fill(("cbr", 192, 384), 67584.0)
+    fill(("zero",), 0.0)
+    fill(("c120",), 120.0)
+    idm, bom, con = {1: ("idn",)}, {1: ("bo",)}, {}
+    for i, c in enumerate((-1, -32, 64, -256, 0.5, -0.5)):
+        idm[c] = block("ids", i)
+        ts(idm[c], ("idn",), float(c), A.mult)
+    for i, c in enumerate((-64, 64, -1 / 64.0, -1, 64 * BIG, BIG / 8, 0.5)):
+        bom[c] = block("bos", i)
+        ts(bom[c], ("bo",), float(c), A.mult)
+    for i, c in enumerate((16, -64, -0.25)):
+        con[c] = block("cb", i)
+        fill(con[c], c / 128.0)
     tt(("bd",), ("bo",), ("idn",), A.subtract)
-    ts(("c1",), ("idn",), -17.0, A.mult)
     cp(("wf",), ("wti",))
     ts(("w1", 0, 128), ("bd",), ("wf", 0, 1), A.mult)
     ts(("w2",), ("bd",), ("wf", 1, 2), A.mult)
     ts(("w1", 128, 256), ("bd",), ("wf", 0, 1), A.mult, 32.0, A.mult)
+    ts(("c1",), ("idn",), -17.0, A.mult)
     tt(("e1",), ("bo",), ("c1",), A.add)
+    fill(("lk",), 0.0)
     fill(("lb",), 0.0)
-
-    def blocks(out, src):
+    for out, src in (("lk", ("e1", 0)), ("lb", bom[0.5])):
         for k in range(16):
-            act((out, 128 * k + k, 128 * (k + 1), 16), (src, k, 128, 16), F.Copy)
-
-    def consts2():
-        ts(("c2",), ("lt",), 2.0, A.mult)
-        ts(("c3",), ("lt",), 64.0, A.mult)
-        tt(("zb",), ("c2",), ("idn",), A.subtract)
-        tt(("c2",), ("c3",), ("c1",), A.add)
-        tt(("za",), ("c2",), ("gt",), A.add)
-        for t in range(NV):
-            act(("zt", 128 * t, 128 * t + 128), ("zb",), F.Copy)
-        for t in range(NV):
-            act(("zt", 128 * t + t, 128 * t + 128, 16), ("za", t, 128, 16), F.Copy)
-        ts(("jcj",), ("jci",), 15, A.bitwise_and)
-        cp(("id16",), ("idn",))
-        cp(("jc",), ("jcj",))
-        ts(("thc",), ("thi",), -2048.0, A.add, 1 / 64.0, A.mult)
-        ts(("md",), ("io16",), ("jc",), A.is_equal)
-        ts(("thr",), ("md", 0, NV), -0.5, A.add)
-
-    def consts3():
-        cp(("lb16",), ("lb",))
-        ts(("nid",), ("idn",), -1.0, A.mult)
-        cp(("bo16", 0, 128), ("bo",))
-        ts(("bo16", 128, 256), ("bo",), 64.0, A.mult)
-        ts(("bo16", 256, 384), ("bo",), 2048.0, A.mult)
-        ts(("bo64",), ("bo",), 64.0, A.mult)
-        ts(("nb",), ("jc",), -4.0, A.mult, -1.5, A.add)
-        ts(("nid16",), ("idn",), -1.0, A.mult)
-        for i, c in enumerate((-1 / 64.0, 0.5, -0.5)):
-            ts(("idx", 128 * i, 128 * i + 128), ("idn",), c, A.mult)
-        ts(("dmp",), ("dm0",), ("jc",), A.add)
-        ts(("dmq",), ("dmp",), 1 / 16.0, A.mult)
-
-    def consts4():
-        fill(("rm",), 0.5)
-        fill(("rm", 0, K, 16), 32768.0)
-        op("V", lambda e: e.tensor_tensor_scan(v(("thl",)), v(("rm",)), v(("oz", K, 2 * K)), 2.0 ** -13, A.mult, A.add),
-           (("rm",), ("oz", K, 2 * K)), (("thl",),))
-        tt(("pw",), ("md",), ("thl", 0, 16), A.mult)
-        op("V", lambda e: e.tensor_reduce(v(("sm", 0, 1)), v(("pw",)), X.X, A.add), (("pw",),), (("sm", 0, 1),))
-        ts(("bow",), ("bo",), ("sm", 0, 1), A.mult, 0.5, A.mult)
+            act((out, 128 * k + k, 128 * (k + 1), 16), (src[0], src[1] + k, src[1] + 128, 16), F.Copy)
+    ts(("lb16",), ("lb",), 2.0, A.mult)
+    ts(("nlb",), ("lb", 0, 512), -2.0, A.mult)
+    cp(("id16",), ("idn",))
+    cp(("bo16",), ("bo",))
+    tt(("c1",), idm[0.5], ("lt",), A.subtract)
+    ts(("zb",), ("c1",), 8192.0, A.mult)
+    ts(("jcj",), ("jci",), 15, A.bitwise_and)
+    cp(("jc",), ("jcj",))
+    ts(("md",), ("io16",), ("jc",), A.is_equal)
+    for i, c in enumerate((1.0, 2.0, 33088.0)):
+        ts(("col", i, i + 1), ("jc",), -8192.0, A.mult, c - 4096.0, A.add)
+    ts(("col", 3, 4), ("jc",), 4.0, A.mult, 2.0, A.add)
+    ts(("col", 4, 5), ("md", 0, 1), -120 * BIG, A.mult)
+    ts(("col", 5, 6), ("md", 1, 2), -BIG, A.mult)
+    ts(("col", 6, 7), ("md", 0, 1), 8192.0, A.mult)
+    ts(("io9",), ("io2",), 958.0, A.add)
+    ts(("tha", 0, 1), ("thi",), 0xFF0, A.bitwise_and)
+    ts(("tha", 1, 2), ("thi",), 15, A.bitwise_and)
+    cp(("thf",), ("tha",))
+    cp(("sel", 0, 8), ("bo", 0, 128, 16))
+    ts(("sel", 8, 16), ("bo", 0, 128, 16), -2.0, A.mult)
+    for i in (0, 1):
+        ts(("sel", 16 + 8 * i, 24 + 8 * i), ("bo", 0, 128, 16), ("thf", i, i + 1), A.mult, 1 / 64.0, A.mult)
+    mms(("pwd", 0, 8), ((one, ("sel", 16, 24)), (one, ("sel", 24, 32))))
+    ts(("tsum", 0, 8), ("pwd", 0, 8), 64.0, A.mult)
+    for hf in (0, 1):
+        cp(("tsum", 8, 12, 1, 64 * hf, 64 * hf + 64), ("tsum", 4 * hf, 4 * hf + 4, 1, 64 * hf, 64 * hf + 64))
+    fill(("ms",), 0.5)
+    fill(("ms", 0, K, 16), 32768.0)
+    op("V", lambda e: e.tensor_tensor_scan(v(("thl",)), v(("ms",)), v(("zero",)), 2.0 ** -13, A.mult, A.add),
+       (("ms",), ("zero",)), (("thl",),), cyc(128))
+    tt(("pw",), ("md",), ("thl", 0, 16), A.mult)
+    op("V", lambda e: e.tensor_reduce(v(("col", 7, 8)), v(("pw",)), X.X, A.add), (("pw",),), (("col", 7, 8),), cyc(64))
+    ts(("bow",), ("bo",), ("col", 7, 8), A.mult, BIG / 2, A.mult)
+    ts(("thr",), ("thl",), ("col", 5, 6), A.mult, ("col", 4, 5), A.add)
+    ts(("ia",), ("ia",), ("md", 1, 2), A.mult, ("col", 6, 7), A.add)
+    ts(("ib",), ("ib",), ("md", 2, 3), A.mult)
+    tt(("drow",), ("ia",), ("ib",), A.add)
 
     nxt = T.cores[(rank + 1) % len(T.cores)]
     rid, pid = topo.addr(nxt)[0], topo.addr(nxt)[1]
@@ -276,315 +338,165 @@ def rank_program(g, core, T, topo):
     neng = len(topo.engines(core, nxt))
 
     def send(src, dst, sem):
-        ready("G", (src,))
-        g.remote_dma(T[dst][:], v(src), T.sem[sem], T.sem.loc, pid, rid, mask)
+        op("G", lambda e: e.remote_dma(T[dst][:], v(src), T.sem[sem], T.sem.loc, pid, rid, mask), (src,), (), 0.3, CFG["far"], sent=sem)
+        op("A", None, (), ((dst,),), 0.0, sem=sem, val=neng)
 
     lex, mng = ("lx", 0, W), ("lm", 0, W)
-    soon = []
-    late = [consts3, consts4]
+
+    def words(out, terms, p0, p1):
+        n = (p1 - p0) // 16
+        for hf in range(8 // n):
+            r = (128 * hf * n // 8, 128 * (hf + 1) * n // 8)
+            mms(("pwd", out + p0 // 16, out + p1 // 16, 1) + r,
+                [((l, p0, p1, 1) + r, ("sel", s + n * hf, s + n * hf + n, 1) + r) for l, s in terms])
 
     for t in range(NV):
-        XI, GI = ("xin%d" % t,), ("gin%d" % t,)
+        xi, gi = "xin%d" % t, "gin%d" % t
         XO, GO = ("xo", K * t, K * t + K), ("go", K * t, K * t + K)
-        if t:
-            arrive("ax%d" % t, neng, (XI,))
-            arrive("ag%d" % t, neng, (GI,))
-        wide = ((0, CH, "pu1", "ppa", "pval"), (CH, K, "pu2", "ph", "ppb"))
-        for c0, c1, bu, b2, b1 in wide:
-            n = c1 - c0
-            for i, w in ((1, ("w2",)), (0, ("w1", 0, 128))):
-                mm((bu, n * (1 - i), n * (2 - i)), w, ("xin%d" % t, c0, c1))
-            for i in (1, 0):
-                act(("fb", K * i + c0, K * i + c1), (bu, n * (1 - i), n * (2 - i)), F.Identity, 130 - 2047.5 / 4096, 1 / 4096.0)
-        for c0, c1, bu, b2, b1 in wide:
-            n = c1 - c0
-            for r, i, q, w in (((b2, 0, n), 1, 0, ("w2",)), ((b1, 0, n), 0, 0, ("w1", 0, 128)), ((b1, n, 2 * n), 0, 128, ("w1", 128, 256))):
-                mm(r, ("cb", q, q + 128), ("oz", 0, n), True, False)
-                mm(r, w, ("xin%d" % t, c0, c1), False, False)
-                mm(r, ("n4096", q, q + 128), ("fb", K * i + c0, K * i + c1), False, True)
-            act(("u2s", c0, c1), (b2, 0, n), F.Copy)
-        mm(("pxp", 0, K), ("idn",), XI)
-
-        def um(c0, c1, q):
-            b, o, n = ("pval", 0, CH) if c1 <= CH else ("ppb", CH, K - CH)
-            return (b, c0 - o + n * q, c1 - o + n * q)
-
-        for chain in CFG["chains"]:
-            for c0, c1 in chain:
-                tt(("pr", c0, c1), ("u2s", c0, c1), um(c0, c1, 0), A.mult)
-            for c0, c1 in chain:
-                tt(("p2", c0, c1), ("pr", c0, c1), um(c0, c1, 1), A.add)
-            for c0, c1 in chain:
-                ts(("h", c0, c1), ("p2", c0, c1), 5, A.arith_shift_right, 4095, A.bitwise_and)
-            for c0, c1 in chain:
-                cp(("hu", c0, c1), ("h", c0, c1))
-            for job in soon:
-                job()
-            soon = []
-        if t == 0:
-            blocks("lk", "e1")
-            blocks("lb", "bo")
-            consts2()
-        vs = K - CFG["vs"]
-        for c in range(0, K, CH):
-            e1 = min(c + CH, vs)
-            act(("cg", 16 * c, 16 * e1), lex, F.Copy, offs=("hu", c, e1))
-
-        def compare(c):
-            bank = "ppa" if c < PARTS[0][1] else "ppb"
-            o = c - (0 if bank == "ppa" else PARTS[1][0])
-            for k in range(16):
-                d0 = 16 * c + k * CH
-                tt(("d", d0, d0 + CH), ("cg", 16 * c + k, 16 * (c + CH), 16), ("pxp", c, c + CH), A.not_equal)
-            for k in range(16):
-                d0 = 16 * c + k * CH
-                mm((bank, o, o + CH), ("lk", 128 * k, 128 * k + 128), ("d", d0, d0 + CH), k == 0, k == 15)
-
-        def pairs(p):
-            p0, p1 = PARTS[p]
-            bank, n = ("ppa", "ppb")[p], p1 - p0
-            ts(("pair", p0, p1), (bank, 0, n), -13.5, A.is_lt)
-            mm((bank, n, 2 * n), ("zt", 128 * t, 128 * t + 128), ("pair", p0, p1))
-
-        def lanes(p):
-            p0, p1 = PARTS[p]
-            bank, n = ("ppa", "ppb")[p], p1 - p0
-            ts(("ep", p0, p1), (bank, n, 2 * n), ("thr", t, t + 1), A.is_lt)
-            tt(("eh", p0, p1), ("ep", p0, p1), ("pu1", p0, p1), A.mult)
-            to_q(("pq", p0 // 16, p1 // 16), "lb16", ("eh", p0, p1))
-
-        def lanes2(p):
-            p0, p1 = PARTS[p]
-            bank, n = ("ppa", "ppb")[p], p1 - p0
-            ts(("t1", K + p0, K + p1), (bank, n, 2 * n), -0.5, A.is_lt, -64.0, A.mult)
-            tt(("t1", p0, p1), ("ep", p0, p1), ("pxp", p0, p1), A.mult)
-
-        def lanes3(p):
-            p0, p1 = PARTS[p]
-            ts(("t1", 2 * K + p0, 2 * K + p1), ("t1", K + p0, K + p1), ("thc",), A.mult)
-
-        def places(p):
-            a0, a1 = PARTS[p][0] // 16, PARTS[p][1] // 16
-            ts(("hq", a0, a1), ("pq", a0, a1), 2048.0, A.add)
-
-        def dist(p):
-            p0, p1 = PARTS[p]
-            bank, n = ("ppa", "ppb")[p], p1 - p0
-            act(("gs", p0, p1), mng, F.Copy, offs=("hq", p0 // 16, p1 // 16))
-            mm((bank, 0, n), ("nid",), ("gin%d" % t, p0, p1), True, False)
-            mm((bank, 0, n), ("idn",), ("gs", p0, p1), False, True)
-            act(("ca", K + p0, K + p1), (bank, 0, n), F.Abs)
-
-        def dist_v(p):
-            p0, p1 = PARTS[p]
-            gat(("gs", p0, p1), mng, ("hq", p0 // 16, p1 // 16), ("gin%d" % t, p0, p1), A.subtract)
-            act(("ca", K + p0, K + p1), ("gs", p0, p1), F.Abs)
-
-        def first_q(p):
-            for b in range(16):
-                op("P", lambda e: e.matmul(T.ph[:, 24 * p:24 * p + 24], T.lb16[:, 128 * b:128 * b + 128],
-                                           T.t1[:, :, PARTS[p][0] + b:PARTS[p][1]:16], start=b == 0, stop=b == 15),
-                   (("lb16",),) + tuple(("t1", K * i + PARTS[p][0], K * i + PARTS[p][1]) for i in range(3)), (("ph", 24 * p, 24 * p + 24),))
-
-        def first_x(p):
-            o = 24 * p
-            tt(("xq", 8 * p, 8 * p + 8), ("qs", o, o + 8), ("qs", o + 8, o + 16), A.add)
-
-        def first_th(p, i):
-            o, q = 24 * p, (8 * p, 8 * p + 8)
-            if i == 0:
-                ts(("q1",) + q, ("qs", o + 8, o + 16), -32.0, A.mult)
-            else:
-                tt(("thq",) + q, ("q1",) + q, ("qs", o + 16, o + 24), A.subtract)
-
-        def xhot(a0, a1):
-            for a in range(a0, a1):
-                ts(("xh", 64 * a, 64 * a + 64), ("ion",), ("xq", a, a + 1), A.is_equal)
-
-        def letter(p):
-            p0, p1 = PARTS[p]
-            gat(("ca", p0, p1), lex, ("hq", p0 // 16, p1 // 16), ("ep", p0, p1), A.mult)
-
+        for c0, c1, raw, un in ((0, CH, "pca", "psb"), (CH, K, "pcb", "phv")):
+            n, x = c1 - c0, (xi, c0, c1)
+            mms((raw, 0, n), ((one, ("cbr", 0, n)), (("w2",), x)))
+            mm((raw, n, 2 * n), block("w1", 0), x)
+            act(("fb", c0, c1), (raw, 0, n), F.Identity, -2047.5)
+            act(("fb", K + c0, K + c1), (raw, n, 2 * n), F.Identity, 530432.5)
+            mm((un, 0, 2 * n), one, ("cbr", 192 - n, 192 + n), True, False)
+            mm((un, 0, n), block("w1", 0), x, False, False)
+            mm((un, n, 2 * n), block("w1", 1), x, False, False)
+            mm((un, 0, n), idm[-1], ("fb", K + c0, K + c1), False, False)
+            mm((un, n, 2 * n), idm[-32], ("fb", K + c0, K + c1), False, True)
+            for e0 in range(c0, c1, CFG["hs"]):
+                e1 = min(c1, e0 + CFG["hs"])
+                tt(("u2s", e0, e1), (raw, e0 - c0, e1 - c0), ("fb", e0, e1), A.subtract)
+                tt(("pr", e0, e1), ("u2s", e0, e1), (un, e0 - c0, e1 - c0), A.mult)
+                tt(("p2", e0, e1), ("pr", e0, e1), (un, n + e0 - c0, n + e1 - c0), A.add)
+                ts(("h", e0, e1), ("p2", e0, e1), 5, A.arith_shift_right, 4095, A.bitwise_and)
+                cp(("hu", e0, e1), ("h", e0, e1))
+        mm(("pxp", 0, K), idm[1], (xi,))
         ts(("h16",), ("hu",), -2048.0, A.add)
-        if CFG["lm"] or not t:
-            for job in late:
-                job()
-            late = []
-        def share():
-            op("V", lambda e: e.tensor_copy(v(("cg", 16 * vs, 4096)), v(lex).indirect(v(("hu", vs, K)))), (lex, ("hu", vs, K)), (("cg", 16 * vs, 4096),))
-        compare(0)
-        mm(("pu1", 0, K), ("id16",), ("h16",))
-        for job in late:
-            job()
-        late = []
-        compare(CH)
+        if CFG["xq"]:
+            act(("xq",), (xi,), F.Identity, 128.625, 0.25)
+        else:
+            ts(("xq",), (xi,), 0.25, A.mult, 128.625, A.add)
+        vs = K - CFG["vs"]
+        for c in range(0, vs, CFG["gc"]):
+            act(("cg", 16 * c, 16 * min(c + CFG["gc"], vs)), lex, F.Copy, offs=("hu", c, min(c + CFG["gc"], vs)))
         if vs < K:
-            share()
-        if PARTS[0][1] == 2 * CH:
-            pairs(0)
-        compare(2 * CH)
-        if PARTS[0][1] == 3 * CH:
-            pairs(0)
-        lanes(0)
-        compare(3 * CH)
-        lanes2(0)
-        pairs(1)
-        lanes3(0)
-        first_q(0)
-        places(0)
-        dist(0)
-        letter(0)
-        lanes(1)
-        lanes2(1)
-        cp(("qs", 0, 24), ("ph", 0, 24))
-        lanes3(1)
-        first_x(0)
-        first_th(0, 0)
-        first_q(1)
-        k1 = CFG["xk"]
-        xhot(0, k1)
-        places(1)
-        first_th(0, 1)
-        if CFG["gv"]:
-            dist_v(1)
-        else:
-            dist(1)
-        letter(1)
-        cp(("qs", 24, 48), ("ph", 24, 48))
-        nx, ns = 16 - CFG["xs"], 16 - CFG["cs"]
-        k2 = min(8, nx)
-        xhot(k1, k1 + 1)
-        first_x(1)
-        first_th(1, 0)
-        xhot(k1 + 1, k1 + 2)
-        first_th(1, 1)
-        xhot(k1 + 2, k2)
-        for a in range(nx, 16):
-            act(("xa", 64 * a, 64 * a + 64), ("ion",), F.Abs, ("xq", a, a + 1), -1.0)
-        act(("xh", 64 * nx, 1024), ("xa", 64 * nx, 1024), F.Relu, 1.0, -1.0)
-        xhot(max(k2, k1 + 2), nx)
-        to_q(("pq", 32, 64), "lb", ("ca", 0, 2 * K))
-        tt(("nf",), ("pq", 48, 64), ("thq",), A.is_ge)
-        cp(("cq",), ("pq", 32, 48))
-        ts(("xi",), ("xq",), 64.0, A.mult)
-        for a in range(ns, 16):
-            act(("xa", 64 * (a - ns), 64 * (a - ns) + 64), ("io0",), F.Abs, ("cq", a, a + 1), -1.0)
-        for a in range(ns, 16):
-            act(("chh", 64 * a, 64 * a + 64), ("xa", 64 * (a - ns), 64 * (a - ns) + 64), F.Relu, ("nf", a, a + 1), -1.0)
-        for a in range(ns):
-            ts(("chh", 64 * a, 64 * a + 64), ("io0",), ("pq", 32 + a, 33 + a), A.is_equal, ("nf", a, a + 1), A.mult)
-        mm(("pxp", K, 2 * K), ("id16",), ("t1", 0, K), True, False)
-        mm(("pxp", K, 2 * K), ("nid",), ("ca", 0, K), False, True)
-        mm(("pval", K, 2 * K), ("bo16", 0, 128), ("t1", 0, K))
-        act(("mt",), ("pval", K, 2 * K), F.Abs, ("nb",))
-        act(("rm",), ("mt",), F.Relu, 32768.0, -16384.0)
+            pick(("cg", 16 * vs, 16 * K), lex, ("hu", vs, K))
+        for p, (p0, p1) in enumerate(parts):
+            n, cnt = p1 - p0, ("pca", "pcb")[p % 2]
+            a0, a1 = p0 // 16, p1 // 16
 
-        for a in range(16):
-            x, c = ("xh", 64 * a, 64 * a + 64), ("chh", 64 * a, 64 * a + 64)
-            for l, r in ((x, c), (c, x)):
-                op("P", lambda e: e.matmul(T.ph[0:64, 0:64], v(l), v(r), start=a == 0 and l is x, stop=a == 15 and l is c),
-                   (l, r), (("ph", 0, 64),))
-        ts(("x3",), ("xi",), 192, A.bitwise_and)
-        tt(("th2",), ("thq",), ("pq", 48, 64), A.subtract)
-        tt(("x3",), ("pq", 32, 48), ("x3",), A.add)
-        tt(("en",), ("pxp", K, 2 * K), ("t1", K, 2 * K), A.mult)
-        act(("ndx",), ("en",), F.Relu, None, -1 / 64.0)
-        mm(("ppb", 0, K), ("bo16", 0, 128), ("eh",))
-        op("V", lambda e: e.tensor_scalar(T.h1[0:64, :], T.ph[0:64, 0:64], 1.0, None, A.min), (("ph", 0, 64),), (("h1",),))
+            def my(name):
+                return (name, p0, p1)
+            for c in range(p0, p1, CH):
+                for k in range(16):
+                    d = ("d", 16 * c + k * CH, 16 * c + k * CH + CH)
+                    tt(d, ("cg", 16 * c + k, 16 * (c + CH), 16), ("pxp", c, c + CH), A.not_equal)
+                    mm((cnt, c - p0, c - p0 + CH), block("lk", k), d, k == 0, k == 15)
+            act(my("sg"), (cnt, 0, n), F.Sign, -13.5, -1.0)
+            z = (("zb",), my("sg"))
+            mms(("phv", 0, n), ((("id16",), my("h16")), z))
+            ts(my("eh"), ("phv", 0, n), ("col", 0, 1), A.add, -2048.0, A.max)
+            to_q(("pq", a0, a1), "lb16", my("eh"))
+            ts(("hq", a0, a1), ("pq", a0, a1), 32767.0, A.add)
+            mms(("psb", 0, n), ((idm[1], my(xi)), z))
+            mms(("psb", n, 2 * n), ((idm[64], my(xi)), (idm[-256], my("xq")), z))
+            mms(("psb", 2 * n, 3 * n), ((idm[1], ("cg", 16 * p0 + t, 16 * p1, 16)), (idm[-1], my(xi)), (bom[-64], my("sg"))))
+            act(my("xa"), ("psb", 0, n), F.Relu, ("col", 1, 2))
+            act(my("yy"), my("xa"), F.Relu, 64.0, -64.0)
+            act(my("xl"), ("psb", n, 2 * n), F.Relu, ("col", 2, 3))
+            act(my("nn"), ("psb", 2 * n, 3 * n), F.Relu, -960.0, ("md", t, t + 1))
+            words(0, (("xa", 0),), p0, p1)
+            act(("xw2", a0, a1), ("pwd", a0, a1), F.Copy)
+            xs = a0 + min(CFG["xs"][p], a1 - a0)
+            for a in range(a0, xs):
+                act(("xt", 64 * a, 64 * a + 64), ("io2",), F.Abs, ("xw2", a, a + 1), -1.0)
+            if xs > a0:
+                act(("xh", 64 * a0, 64 * xs), ("xt", 64 * a0, 64 * xs), F.Relu, 1.0, -1.0)
+            for a in range(xs, a1):
+                ts(("xh", 64 * a, 64 * a + 64), ("io2",), ("xw2", a, a + 1), A.is_equal)
+            act(my("gs"), mng, F.Copy, offs=("hq", a0, a1))
+            early = ((gi, 0), ("yy", 16), ("yy", 24))
+            if CFG["mn"][p]:
+                gat(my("mn"), mng, ("hq", a0, a1), my(gi), A.min)
+                words(48, early + (("gs", 0), ("mn", 8)), p0, p1)
+            else:
+                mms((cnt, K, K + n), ((idm[-1], my(gi)), (idm[1], my("gs"))))
+                act(my("mn"), (cnt, K, K + n), F.Abs)
+                words(48, early[1:] + (("mn", 0),), p0, p1)
+            gat(my("mx"), lex, ("hq", a0, a1), my("yy"), A.max)
+            words(16, (("mx", 0),), p0, p1)
+            tt(("nf", a0, a1), ("pwd", 48 + a0, 48 + a1), ("tsum", 0, 8) if n == 128 else ("tsum", 8, 12), A.is_ge)
+            cw = "pwd" if p1 == K else "xw2"
+            if p1 < K:
+                cp(("xw2", 16 + a0, 16 + a1), ("pwd", 16 + a0, 16 + a1))
+            for a in range(a0, a1):
+                x, c = ("xh", 64 * a, 64 * a + 64), ("chh", 64 * a, 64 * a + 64)
+                ts(c, ("io9",), (cw, 16 + a, 17 + a), A.is_equal, ("nf", a, a + 1), A.mult)
+                mm(("ptb", 0, 64, 1, 0, 64), x, c, a == 0, False)
+                mm(("ptb", 0, 64, 1, 0, 64), c, x, False, a == 15)
+        mms(("phv", 0, K), ((idm[1], (xi,)), (block("lb", t), ("c120",)), (idm[1], ("nn",)), (block("nlb", t), ("yy",))))
+        tt(("xn",), ("phv", 0, K), ("mx",), A.min)
+        ts(("hqf",), ("pq", 0, 16), 32767.0, A.add)
+        to_q(("pq", 16, 32), "lb", ("xl", 0, K), ("mx", 0, K))
+        ts(("of",), ("pq", 16, 32), 2.0, A.mult, -1024.0, A.add)
+        mms(("psb", 0, K), ((bom[1], ("xa",)), (bom[-1 / 64.0], ("xl",))))
+        act(("ms",), ("psb", 0, K), F.Copy)
+        ts(("h1", 0, 64, 1, 0, 64), ("ptb", 0, 64, 1, 0, 64), 1.0, A.min)
         for q in range(4):
-            op("P", lambda e: e.matmul(T.ph[:, K + 64 * q:K + 64 * q + 64], T.ra[0:64, 128 * q:128 * q + 128], T.h1[0:64, :],
-                                       start=True, stop=True), (("ra",), ("h1",)), (("ph", K + 64 * q, K + 64 * q + 64),))
-        act(("tb",), ("ph", K, 2 * K), F.Copy)
-        cp(("of",), ("x3",))
-        ts(("hr",), ("ppb", 0, K), 2048.0, A.add)
-        ts(("q2",), ("th2",), 0.0, A.is_le, 8192.0, A.mult)
-        cp(("hqf",), ("hq",))
-        mm(("pu1", 0, K), ("idn",), XI, True, False)
-        mm(("pu1", 0, K), ("idn",), ("ca", 0, K), False, False)
-        mm(("pu1", 0, K), ("nid16",), ("t1", 0, K), False, False)
-        mm(("pu1", 0, K), ("idx", 0, 128), ("en",), False, True)
-        act(("xb",), ("pu1", 0, K), F.Copy)
-        for p in (0, 1):
-            p0, p1 = PARTS[p]
-            src = ("gs", p0, p1) if p and CFG["gv"] else (("ppa", "ppb")[p], 0, p1 - p0)
-            act(("dg1", p0, p1), src, F.Identity, -0.25, 0.5)
-        act(("dg2",), ("dg1",), F.Identity, 12582912.0)
-        val = ("pval", 0, K)
-        mm(val, ("bo64",), ("ca", K, 2 * K), True, False)
-        mm(val, ("bo16", 128, 256), ("t1", 2 * K, 3 * K), False, False)
-        mm(val, ("bo16", 256, 384), ("t1", K, 2 * K), False, False)
-        mm(val, ("idn",), ("xb",), False, False)
-        gat(("f",), ("tb",), ("of",), ("rm",), A.mult)
-        mm(val, ("bo64",), ("f",), False, True)
-        tt(("nx",), ("pu1", 0, K), ("ndx",), A.subtract)
-        tt(("hqx",), ("q2",), ("hqf",), A.add)
-        tt(("yv",), val, ("nx",), A.max)
-        tt(XO, ("yv",), ("pu1", 0, K), A.min)
+            mm(("pca", 64 * q, 64 * q + 64), ("ra", 128 * q, 128 * q + 128, 1, 0, 64), ("h1", 0, 64, 1, 0, 64))
+        act(("tb",), ("pca", 0, K), F.Identity, -1.0, ("col", 3, 4))
+        mms(("pcb", 0, K), ((con[-0.25], ("ones", 0, K)), (idm[-0.5], (gi,)), (idm[0.5], ("gs",))))
+        act(("dg1",), ("pcb", 0, K), F.Identity, 12582912.0)
+        act(("dg",), ("dg1",), F.Identity, -12582912.0)
+        mm(("pwd", K, 2 * K), ("bo16",), ("eh",))
+        ts(("hr",), ("pwd", K, 2 * K), 32767.0, A.add)
+        gat(("f",), ("tb",), ("of",), ("ms",), A.is_equal)
+        mms(("pxp", K, 2 * K), ((con[-64], ("ones", 0, K)), (idm[1], (xi,)), (bom[64], ("f",))))
+        tt(XO, ("pxp", K, 2 * K), ("xn",), A.max)
         send(XO, "xin%d" % (t + 1), "ax%d" % (t + 1))
-        act(("pval", K, 2 * K), val, F.Sign, 0.5)
-        to_q(("pq", 80, 96), "lb", ("f", 0, K))
+        to_q(("pq", 32, 48), "lb", ("f", 0, K))
+        tt(("sq",), ("pq", 32, 48), ("hqf",), A.add)
         nv = 16 - CFG["eqs"]
-        tt(("sq",), ("hqx",), ("pq", 80, 96), A.add)
-        ts(("hqs", nv, 16), ("sq", nv, 16), -2048.0, A.add)
-        for a in range(nv, 16):
-            e0 = 128 * (a - 8)
-            act(("ea", e0, e0 + K - 16 * a), ("ppb", 16 * a, K), F.Abs, ("hqs", a, a + 1), -1.0)
-        for a in range(nv, 16):
-            e0 = 128 * (a - 8)
-            op("S", lambda e: e.activation(T.eq[:, a, 0:K - 16 * a], v(("ea", e0, e0 + K - 16 * a)), F.Relu, bias=1.0, scale=-1.0),
-               (("ea", e0, e0 + K - 16 * a),), (("eq", 272 * a, 256 * a + 256),))
-        for a in range(nv):
-            op("V", lambda e: e.tensor_scalar(T.eq[:, a, 0:K - 16 * a], v(("hr", 16 * a, K)), v(("sq", a, a + 1)), None, A.is_equal),
-               (("hr",), ("sq",)), (("eq", 272 * a, 256 * a + 256),))
-        tt(("nm",), ("pq", 80, 96), ("th2",), A.is_ge)
-        tt(("nm",), ("nm",), ("dmp",), A.mult)
-        tt(("hqm",), ("nm",), ("hqf",), A.max)
-        mm(("ph", 0, K), ("bo",), ("oz", K, 2 * K), True, False)
-        for a in range(15):
-            op("P", lambda e: e.matmul(T.ph[:, 16 * a + 16:K], v(("bo64",)), T.eq[:, a, 16:K - 16 * a], start=False, stop=False),
-               (("bo64",), ("eq", 272 * a, 256 * a + 256)), (("ph", 0, K),))
-        op("P", lambda e: e.matmul(T.ph[:, 0:K], v(("bow",)), T.eq[:, :, 0:16], start=False, stop=True),
-           (("bow",), ("eq", 0, 4096)), (("ph", 0, K),))
-        act(("dg",), ("dg2",), F.Identity, -12582912.0)
-        tt(("gm",), ("dg",), ("pval", K, 2 * K), A.mult)
-        tt(("ls",), ("ph", 0, K), ("thl",), A.is_ge)
-        to_q(("pq", 64, 80), "lb", ("ls", 0, K))
-        mm(("pxp", K, 2 * K), ("idn",), GI, True, False)
-        mm(("pxp", K, 2 * K), ("idx", 128, 256), ("dg",), False, False)
-        mm(("pxp", K, 2 * K), ("idx", 256, 384), ("gm",), False, True)
-        tt(("lq2",), ("pq", 64, 80), ("dmq",), A.mult)
-        tt(("lq2",), ("hqm",), ("lq2",), A.max)
-        cp(("so",), ("lq2",))
-        scat(("lx",), ("so",), XO)
+        if nv < 16:
+            ts(("hqs", nv, 16), ("sq", nv, 16), -32767.0, A.add)
+        bad = ("ptb", K, 2 * K)
+        mm(bad, bom[1], ("thr",), True, False)
+        mm(bad, bom[BIG / 8], ("yy",), False, False)
+        mm(bad, bom[64 * BIG], ("f",), False, False)
+        for a in range(16):
+            row = ("eq", 272 * a, 256 * a + 256)
+            if a < nv:
+                ts(row, ("hr", 16 * a, K), ("sq", a, a + 1), A.is_equal)
+            else:
+                e0 = 128 * (a - 8)
+                act(("ea", e0, e0 + K - 16 * a), ("pwd", K + 16 * a, 2 * K), F.Abs, ("hqs", a, a + 1), -1.0)
+                act(row, ("ea", e0, e0 + K - 16 * a), F.Relu, 1.0, -2.0)
+            if a < 15:
+                mm(("ptb", K + 16 * a + 16, 2 * K), bom[64 * BIG], ("eq", 272 * a + 16, 256 * a + 256), False, False)
+        mm(bad, ("bow",), ("eq", 0, 16 * 272), False, True, ap=T.eq[:, :, 0:16])
+        tt(("ls",), bad, ("drow",), A.min)
+        to_q(("pq", 48, 64), "lb", ("ls", 0, K))
+        tt(("lq",), ("pq", 48, 64), ("hqf",), A.max)
+        cp(("so",), ("lq",))
+        step = 16 // CFG["nsc"]
+        for a in range(0, 16, step):
+            scat(("lx",), ("so", a, a + step), ("xo", K * t + 16 * a, K * t + 16 * (a + step)))
+        mms(("pcb", K, 2 * K), ((con[16], ("ones", 0, K)), (bom[-1 / 64.0], ("yy",)), (bom[-1], ("f",))))
+        tt(("gm",), ("dg",), ("pcb", K, 2 * K), A.mult)
+        mms(("pca", K, 2 * K), ((idm[1], (gi,)), (idm[1], ("gm",))))
+        act(GO, ("pca", K, 2 * K), F.Copy)
+        send(GO, "gin%d" % (t + 1), "ag%d" % (t + 1))
+        for a in range(0, 16, step):
+            scat(("lm",), ("so", a, a + step), ("go", K * t + 16 * a, K * t + 16 * (a + step)))
 
-        def new_meanings(GO=GO, t=t):
-            cp(GO, ("pxp", K, 2 * K))
-            send(GO, "gin%d" % (t + 1), "ag%d" % (t + 1))
-        if CFG["go"] and t < NV - 1:
-            soon.append(new_meanings)
-        else:
-            new_meanings()
-
-        def meanings(GO=GO):
-            scat(("lm",), ("so",), GO)
-        late.append(meanings)
-
-    def store(q, y, a, sem):
-        dma(q, lambda e: e.dma_start(y[:], v(a)), sem, (a,), ())
-
-    for job in late:
-        job()
-    arrive("ax%d" % NV, neng, (("xin%d" % NV,),))
-    arrive("ag%d" % NV, neng, (("gin%d" % NV,),))
-    store("Y", T.yx, ("xin%d" % NV,), "st1")
-    store("Y", T.yl, lex, "st0")
-    store("Y", T.yg, ("gin%d" % NV,), "st2")
     h = W // 2
-    op("V", lambda e: e.tensor_reduce(T.sm[:, 0:1], T.lm[:, 0:h], X.X, A.add), (("lm", 0, h),), (("sm", 0, 1),))
+    op("V", lambda e: e.tensor_reduce(T.sm[:, 0:1], T.lm[:, 0:h], X.X, A.add), (("lm", 0, h),), (("sm", 0, 1),), cyc(h))
     act(("cg", 0, h), ("lm", h, W), F.Copy, acc=("sm", 1, 2))
     tt(("sm", 2, 3), ("sm", 0, 1), ("sm", 1, 2), A.add)
-    store("S", T.ym, ("sm", 2, 3), "st3")
+    for q, y, a, sem in (("Y", T.yl, lex, "st0"), ("Y", T.yx, ("xin%d" % NV,), "st1"), ("Y", T.yg, ("gin%d" % NV,), "st2"), ("S", T.ym, ("sm", 2, 3), "st3")):
+        dma(q, y[:], v(a), sem, (a,), (), 1.3 + cols(a) / 1.0e3)
+    issue(g, T, order(calls))
     for i in range(4):
         g.wait_ge(T.sem["st%d" % i], 16)
     g.wait_ge(T.sem.loc, 2 * NV * neng)
-    finish()

@@ -1,10 +1,14 @@
+import numpy as np
 from concourse.mybir import AluOpType as A, ActivationFunctionType as F, AxisListType as X
 
 K = 256
 W = 4096
 NV = 4
 CH = 64
-CFG = {"parts": ((0, 128), (128, 256)), "vs": 32, "eqs": 5, "nsc": 1, "xs": (0, 0, 0, 0), "mn": (1, 1, 1, 1), "xq": 0, "gc": 64, "wait": 0.17, "far": 2.0, "pe": 0.55, "hs": 64, "fill": 0.1}
+CFG = {"parts": ((0, 128), (128, 256)), "vs": 32, "eqs": 2, "nsc": 2, "xs": (0, 4, 0, 0), "mn": (1, 1, 1, 1), "xq": 0, "gc": 64, "wait": 0.18,
+       "sgv": (1, 0, 0, 0), "far": 1.5, "cut": 1, "pe": 0.5, "hs": 64, "rounds": 2, "vc": 16,
+       "two": (1, 0, 0, 0), "us": 0, "thin": 192}
+ORDER = {}
 
 SCRATCH = {}
 
@@ -21,14 +25,14 @@ for _d, _l in (
                       ("bo1", 128), ("bo", 128), ("idn", 128), ("lt", 128), ("c1", 128), ("e1", 128), ("bd", 128), ("w1", 256), ("w2", 128),
                       ("lk", 2048), ("lb", 2048), ("nlb", 512), ("ids", 6 * 128), ("bos", 7 * 128), ("zb", 128), ("cb", 3 * 128), ("cbr", 384),
                       ("c120", K), ("bow", 128), ("thl", K), ("thr", K), ("drow", K), ("ia", K), ("ib", K), ("ra", 512), ("io2", 64),
-                      ("sel", 32), ("fb", 2 * K), ("cg", 16 * K), ("d", 16 * K), ("sg", K), ("xq", K), ("xa", K), ("xl", K), ("nn", K), ("yy", K),
+                      ("sel", 48), ("fb", 2 * K), ("cg", 16 * K), ("d", 16 * K), ("sg", K), ("xq", K), ("xa", K), ("xl", K), ("nn", K), ("yy", K),
                       ("gs", K), ("mn", K), ("mx", K), ("xn", K), ("ms", K), ("dg", K), ("gm", K), ("xh", 1024), ("chh", 1024), ("xt", 1024),
                       ("h1", 64), ("tb", K), ("f", K), ("ea", 2048), ("ls", K), ("zero", K))),
-        ("float16", (("lb16", 2048), ("id16", 128), ("bo16", 128), ("h16", K), ("eh", K), ("io9", 64))),
+        ("float16", (("h16", K), ("eh", K), ("io9", 64))),
         ("int32", (("wti", 2), ("thi", 1), ("tha", 2), ("jci", 1), ("jcj", 1), ("pr", K), ("p2", K), ("h", K))),
         ("uint16", (("hu", K), ("hq", 16), ("of", 16), ("hr", K), ("so", 16))),
-        ("float32", (("wf", 2), ("thf", 2), ("jc", 1), ("io16", 16), ("md", 16), ("pw", 16), ("col", 8), ("u2s", K), ("hqf", 16), ("tsum", 12),
-                     ("nf", 16), ("xw2", 32), ("sq", 16), ("hqs", 16), ("dg1", K), ("lq", 16), ("sm", 3)))):
+        ("float32", (("wf", 2), ("thf", 2), ("jc", 1), ("io16", 16), ("md", 16), ("pw", 16), ("col", 11), ("u2s", K), ("hqf", 16), ("tsum", 12),
+                     ("nf", 16), ("xw2", 32), ("sq", 16), ("hqs", 16), ("dg1", K), ("lq", 16), ("sm", 10)))):
     for _n, _c in _l:
         _buf(_n, _c, _d)
 SCRATCH["eq"] = ("sbuf", [128, 16, 272], "bfloat16")
@@ -37,7 +41,7 @@ for _n in ("pxp", "pca", "pcb", "psb", "phv", "pq", "pwd", "ptb"):
 
 SEMAPHORES = ["v", "s", "p", "gc", "loc"]
 SEMAPHORES += ["ld%d" % _i for _i in range(6)] + ["st%d" % _i for _i in range(4)]
-SEMAPHORES += ["ax%d" % _i for _i in range(1, NV + 1)] + ["ag%d" % _i for _i in range(1, NV + 1)]
+SEMAPHORES += ["%s%d" % (_n, _i) for _n in ("ax", "bx", "ag") for _i in range(1, NV + 1)]
 
 CYCLE = 0.83e-3
 BIG = 2.0 ** 27
@@ -70,6 +74,9 @@ def order(calls):
             b["now"].append(i)
         if c["q"] == "A":
             dep[sent[c["sem"]]] = 0.0
+        if c.get("line"):
+            dep.setdefault(sent.get(c["line"], i), 0.0)
+            sent[c["line"]] = i
         if "sent" in c:
             sent[c["sent"]] = i
         for wr, accs in ((True, c["w"]), (False, c["r"])):
@@ -80,36 +87,50 @@ def order(calls):
                     rows[:] = [r for r in rows if not (lo <= r[1] and r[2] <= hi)]
                 rows.append((i, lo, hi, wr))
         dep.pop(i, None)
-        c["dep"], c["next"], c["left"], c["at"] = dep, [], len(dep), 0.0
-        for j in dep:
-            calls[j]["next"].append(i)
+        c["dep"], c["next"] = {j: x + calls[j]["lag"] for j, x in dep.items()}, {}
+        for j, x in c["dep"].items():
+            calls[j]["next"][i] = x
+
+    def place(rank, before, after, tail):
+        left = [len(c[before]) for c in calls]
+        at = [c["lag"] if tail else 0.0 for c in calls]
+        busy = {q: ([], []) for q in "VSPGYA"}
+        ready = {i for i in range(len(calls)) if not left[i]}
+        seq = []
+        while ready:
+            i = max(ready, key=lambda i: (rank[i], -i))
+            ready.remove(i)
+            c = calls[i]
+            starts, ends = busy[c["q"]]
+            k = int(np.searchsorted(ends, at[i], side="right")) if ends else 0
+            while k < len(starts) and starts[k] < at[i] + c["cost"] - 1e-9:
+                at[i] = max(at[i], ends[k])
+                k += 1
+            starts.insert(k, at[i])
+            ends.insert(k, at[i] + c["cost"])
+            seq.append(i)
+            for j, x in c[after].items():
+                at[j] = max(at[j], at[i] + c["cost"] + x)
+                left[j] -= 1
+                if not left[j]:
+                    ready.add(j)
+        return at, seq
+
+    way = [0.0] * len(calls)
     for i in reversed(range(len(calls))):
-        c = calls[i]
-        c["way"] = c["cost"] + c["lag"] + max([calls[j]["way"] + calls[j]["dep"][i] for j in c["next"]], default=0.0) + c.get("first", 0.0)
-    free = {q: 0.0 for q in "VSPGYA"}
-    ready = {q: [] for q in free}
-    for i, c in enumerate(calls):
-        if not c["left"]:
-            ready[c["q"]].append(i)
-    out = []
-    while len(out) < len(calls):
-        q = min((q for q in free if ready[q]), key=lambda q: max(free[q], min(calls[i]["at"] for i in ready[q])))
-        best = max(ready[q], key=lambda i: (calls[i]["way"], -i))
-        fits = [i for i in ready[q] if max(free[q], calls[i]["at"]) + calls[i]["cost"] <= calls[best]["at"] + CFG["fill"]]
-        if fits:
-            now = max(free[q], min(calls[i]["at"] for i in fits))
-            best = max((i for i in fits if calls[i]["at"] <= now), key=lambda i: (calls[i]["way"], -i))
-        c = calls[best]
-        ready[q].remove(best)
-        free[q] = max(free[q], c["at"]) + c["cost"]
-        out.append(c)
-        for j in c["next"]:
-            n = calls[j]
-            n["at"] = max(n["at"], free[q] + c["lag"] + n["dep"][best])
-            n["left"] -= 1
-            if not n["left"]:
-                ready[n["q"]].append(j)
-    return out
+        way[i] = calls[i]["cost"] + max([way[j] + x for j, x in calls[i]["next"].items()], default=calls[i]["lag"])
+    best = None
+    ORDER["log"] = [round(max(way), 2)]
+    for _ in range(CFG["rounds"]):
+        at, seq = place([w + c.get("first", 0.0) for w, c in zip(way, calls)], "dep", "next", False)
+        end = [a + c["cost"] + c["lag"] for a, c in zip(at, calls)]
+        ORDER["log"].append(round(max(end), 2))
+        if best is None or max(end) < best[0]:
+            pos = {i: k for k, i in enumerate(seq)}
+            best = (max(end), sorted(range(len(calls)), key=lambda i: (at[i], pos[i])))
+        back = place(end, "next", "dep", True)[0]
+        way = [a + c["cost"] for a, c in zip(back, calls)]
+    return best[1]
 
 
 def issue(g, T, calls):
@@ -224,7 +245,7 @@ def rank_program(g, core, T, topo):
             kw["accum_out"] = v(acc)
         src = v(a) if offs is None else v(a).indirect(v(offs))
         op("S", lambda e: e.activation(v(out), src, fn, **kw), rw(a, bias, scale, offs), rw(out, acc),
-           cyc(cols(out)) if offs is None else 0.065 + 1.56 * CYCLE * cols(out))
+           cyc(cols(out)) if offs is None else 0.065 + 1.56 * CYCLE * cols(out), line=offs and offs[0])
 
     def mm(out, l, rh, st=True, sp=True, ap=None):
         op("P", lambda e: e.matmul(v(out), v(l), v(rh) if ap is None else ap, start=st, stop=sp), rw(l, rh), rw(out),
@@ -249,8 +270,8 @@ def rank_program(g, core, T, topo):
     def block(name, i):
         return (name, 128 * i, 128 * i + 128)
 
-    for i, (q, out, src, lag) in enumerate((("S", ("xin0",), T.xw, 1.5), ("Y", ("wti",), T.wts, 1.5), ("Y", ("lx", 0, W), T.lex, 5.0),
-                                            ("S", ("thi",), T.th, 1.5), ("Y", ("gin0",), T.gw, 5.5), ("Y", ("lm", 0, W), T.mng, 9.0))):
+    for i, (q, out, src, lag) in enumerate((("S", ("xin0",), T.xw, 1.5), ("Y", ("wti",), T.wts, 1.5), ("Y", ("lx", 0, W), T.lex, 4.0),
+                                            ("S", ("thi",), T.th, 1.5), ("Y", ("gin0",), T.gw, 4.5), ("Y", ("lm", 0, W), T.mng, 7.5))):
         dma(q, v(out), src[:], "ld%d" % i, (), (out,), lag, first=1e4 - 1e3 * i)
 
     small = {"allow_small_or_imprecise_dtypes": True}
@@ -293,10 +314,7 @@ def rank_program(g, core, T, topo):
     for out, src in (("lk", ("e1", 0)), ("lb", bom[0.5])):
         for k in range(16):
             act((out, 128 * k + k, 128 * (k + 1), 16), (src[0], src[1] + k, src[1] + 128, 16), F.Copy)
-    ts(("lb16",), ("lb",), 2.0, A.mult)
     ts(("nlb",), ("lb", 0, 512), -2.0, A.mult)
-    cp(("id16",), ("idn",))
-    cp(("bo16",), ("bo",))
     tt(("c1",), idm[0.5], ("lt",), A.subtract)
     ts(("zb",), ("c1",), 8192.0, A.mult)
     ts(("jcj",), ("jci",), 15, A.bitwise_and)
@@ -304,6 +322,7 @@ def rank_program(g, core, T, topo):
     ts(("md",), ("io16",), ("jc",), A.is_equal)
     for i, c in enumerate((1.0, 2.0, 33088.0)):
         ts(("col", i, i + 1), ("jc",), -8192.0, A.mult, c - 4096.0, A.add)
+        ts(("col", 8 + i, 9 + i), ("jc",), -16384.0, A.mult, c, A.add)
     ts(("col", 3, 4), ("jc",), 4.0, A.mult, 2.0, A.add)
     ts(("col", 4, 5), ("md", 0, 1), -120 * BIG, A.mult)
     ts(("col", 5, 6), ("md", 1, 2), -BIG, A.mult)
@@ -313,7 +332,8 @@ def rank_program(g, core, T, topo):
     ts(("tha", 1, 2), ("thi",), 15, A.bitwise_and)
     cp(("thf",), ("tha",))
     cp(("sel", 0, 8), ("bo", 0, 128, 16))
-    ts(("sel", 8, 16), ("bo", 0, 128, 16), -2.0, A.mult)
+    for i, c in ((1, -2.0), (4, 0.5), (5, -0.5)):
+        ts(("sel", 8 * i, 8 * i + 8), ("bo", 0, 128, 16), c, A.mult)
     for i in (0, 1):
         ts(("sel", 16 + 8 * i, 24 + 8 * i), ("bo", 0, 128, 16), ("thf", i, i + 1), A.mult, 1 / 64.0, A.mult)
     mms(("pwd", 0, 8), ((one, ("sel", 16, 24)), (one, ("sel", 24, 32))))
@@ -338,16 +358,17 @@ def rank_program(g, core, T, topo):
     neng = len(topo.engines(core, nxt))
 
     def send(src, dst, sem):
-        op("G", lambda e: e.remote_dma(T[dst][:], v(src), T.sem[sem], T.sem.loc, pid, rid, mask), (src,), (), 0.3, CFG["far"], sent=sem)
-        op("A", None, (), ((dst,),), 0.0, sem=sem, val=neng)
+        op("G", lambda e: e.remote_dma(v(dst), v(src), T.sem[sem], T.sem.loc, pid, rid, mask), (src,), (), 0.3,
+           CFG["far"] + cols(src) / 400.0, sent=sem)
+        op("A", None, (), (dst,), 0.0, sem=sem, val=neng)
 
     lex, mng = ("lx", 0, W), ("lm", 0, W)
 
-    def words(out, terms, p0, p1):
+    def words(bank, out, terms, p0, p1):
         n = (p1 - p0) // 16
         for hf in range(8 // n):
             r = (128 * hf * n // 8, 128 * (hf + 1) * n // 8)
-            mms(("pwd", out + p0 // 16, out + p1 // 16, 1) + r,
+            mms((bank, K + out + p0 // 16, K + out + p1 // 16, 1) + r,
                 [((l, p0, p1, 1) + r, ("sel", s + n * hf, s + n * hf + n, 1) + r) for l, s in terms])
 
     for t in range(NV):
@@ -380,64 +401,92 @@ def rank_program(g, core, T, topo):
         vs = K - CFG["vs"]
         for c in range(0, vs, CFG["gc"]):
             act(("cg", 16 * c, 16 * min(c + CFG["gc"], vs)), lex, F.Copy, offs=("hu", c, min(c + CFG["gc"], vs)))
-        if vs < K:
-            pick(("cg", 16 * vs, 16 * K), lex, ("hu", vs, K))
+        for c in range(vs, K, CFG["vc"]):
+            pick(("cg", 16 * c, 16 * (c + CFG["vc"])), lex, ("hu", c, c + CFG["vc"]))
+        thin = CFG["thin"]
+        for r in range(2 if thin < K else 0):
+            mm(("pxp", K + r, K + 2 * (K - thin), 2), idm[1], (xi, thin, K))
         for p, (p0, p1) in enumerate(parts):
             n, cnt = p1 - p0, ("pca", "pcb")[p % 2]
             a0, a1 = p0 // 16, p1 // 16
 
             def my(name):
                 return (name, p0, p1)
-            for c in range(p0, p1, CH):
+            for c in range(p0, min(p1, thin), CH):
                 for k in range(16):
                     d = ("d", 16 * c + k * CH, 16 * c + k * CH + CH)
                     tt(d, ("cg", 16 * c + k, 16 * (c + CH), 16), ("pxp", c, c + CH), A.not_equal)
                     mm((cnt, c - p0, c - p0 + CH), block("lk", k), d, k == 0, k == 15)
-            act(my("sg"), (cnt, 0, n), F.Sign, -13.5, -1.0)
+            for c in reversed(range(max(p0, thin), p1, 32)):
+                for k in range(8):
+                    d0 = 16 * c + k * CH
+                    tt(("d", d0, d0 + CH), ("cg", 16 * c + k, 16 * (c + 32), 8), ("pxp", K + 2 * (c - thin), K + 2 * (c - thin) + CH), A.not_equal)
+                    for r in (0, 1):
+                        mm((cnt, c - p0, c - p0 + 32), block("lk", k + 8 * r), ("d", d0 + r, d0 + CH, 2), k + r == 0, k + r == 8)
+            sb, o = ("psb", "pwd")[p % 2], 8 * CFG["sgv"][p]
+            if o:
+                ts(my("sg"), (cnt, 0, n), -13.5, A.is_ge, -2.0, A.mult)
+            else:
+                act(my("sg"), (cnt, 0, n), F.Sign, -13.5, -1.0)
             z = (("zb",), my("sg"))
-            mms(("phv", 0, n), ((("id16",), my("h16")), z))
-            ts(my("eh"), ("phv", 0, n), ("col", 0, 1), A.add, -2048.0, A.max)
-            to_q(("pq", a0, a1), "lb16", my("eh"))
-            ts(("hq", a0, a1), ("pq", a0, a1), 32767.0, A.add)
-            mms(("psb", 0, n), ((idm[1], my(xi)), z))
-            mms(("psb", n, 2 * n), ((idm[64], my(xi)), (idm[-256], my("xq")), z))
-            mms(("psb", 2 * n, 3 * n), ((idm[1], ("cg", 16 * p0 + t, 16 * p1, 16)), (idm[-1], my(xi)), (bom[-64], my("sg"))))
-            act(my("xa"), ("psb", 0, n), F.Relu, ("col", 1, 2))
+            mms(("phv", 0, n), ((idm[1], my("h16")), z))
+            ts(my("eh"), ("phv", 0, n), ("col", o, o + 1), A.add, -2048.0, A.max)
+            to_q(("pq", a0, a1), "lb", my("eh"))
+            ts(("hq", a0, a1), ("pq", a0, a1), 2.0, A.mult, 32767.0, A.add)
+            mms((sb, 0, n), ((idm[1], my(xi)), z))
+            mms((sb, n, 2 * n), ((idm[64], my(xi)), (idm[-256], my("xq")), z))
+            mms((sb, 2 * n, 3 * n), ((idm[1], ("cg", 16 * p0 + t, 16 * p1, 16)), (idm[-1], my(xi)), (bom[-64], my("sg"))))
+            act(my("xa"), (sb, 0, n), F.Relu, ("col", o + 1, o + 2))
             act(my("yy"), my("xa"), F.Relu, 64.0, -64.0)
-            act(my("xl"), ("psb", n, 2 * n), F.Relu, ("col", 2, 3))
-            act(my("nn"), ("psb", 2 * n, 3 * n), F.Relu, -960.0, ("md", t, t + 1))
-            words(0, (("xa", 0),), p0, p1)
-            act(("xw2", a0, a1), ("pwd", a0, a1), F.Copy)
-            xs = a0 + min(CFG["xs"][p], a1 - a0)
-            for a in range(a0, xs):
-                act(("xt", 64 * a, 64 * a + 64), ("io2",), F.Abs, ("xw2", a, a + 1), -1.0)
-            if xs > a0:
-                act(("xh", 64 * a0, 64 * xs), ("xt", 64 * a0, 64 * xs), F.Relu, 1.0, -1.0)
-            for a in range(xs, a1):
-                ts(("xh", 64 * a, 64 * a + 64), ("io2",), ("xw2", a, a + 1), A.is_equal)
+            act(my("xl"), (sb, n, 2 * n), F.Relu, ("col", o + 2, o + 3))
+            act(my("nn"), (sb, 2 * n, 3 * n), F.Relu, -960.0 - 128 * o, ("md", t, t + 1))
+            two = CFG["two"][p]
+
+            def wd(q, b0=a0, b1=a1):
+                return (cnt, K + q + b0, K + q + b1)
+            if not two:
+                words(cnt, 0, (("xa", 0),), p0, p1)
+                act(("xw2", a0, a1), wd(0), F.Copy)
+                xs = a0 + min(CFG["xs"][p], a1 - a0)
+                for a in range(a0, xs):
+                    act(("xt", 64 * a, 64 * a + 64), ("io2",), F.Abs, ("xw2", a, a + 1), -1.0)
+                if xs > a0:
+                    act(("xh", 64 * a0, 64 * xs), ("xt", 64 * a0, 64 * xs), F.Relu, 1.0, -1.0)
+                for a in range(xs, a1):
+                    ts(("xh", 64 * a, 64 * a + 64), ("io2",), ("xw2", a, a + 1), A.is_equal)
             act(my("gs"), mng, F.Copy, offs=("hq", a0, a1))
             early = ((gi, 0), ("yy", 16), ("yy", 24))
             if CFG["mn"][p]:
                 gat(my("mn"), mng, ("hq", a0, a1), my(gi), A.min)
-                words(48, early + (("gs", 0), ("mn", 8)), p0, p1)
+                words(cnt, 48, early + (("gs", 0), ("mn", 8)), p0, p1)
             else:
-                mms((cnt, K, K + n), ((idm[-1], my(gi)), (idm[1], my("gs"))))
-                act(my("mn"), (cnt, K, K + n), F.Abs)
-                words(48, early[1:] + (("mn", 0),), p0, p1)
+                mms((cnt, 128, 128 + n), ((idm[-1], my(gi)), (idm[1], my("gs"))))
+                act(my("mn"), (cnt, 128, 128 + n), F.Abs)
+                words(cnt, 48, early[1:] + (("mn", 0),), p0, p1)
             gat(my("mx"), lex, ("hq", a0, a1), my("yy"), A.max)
-            words(16, (("mx", 0),), p0, p1)
-            tt(("nf", a0, a1), ("pwd", 48 + a0, 48 + a1), ("tsum", 0, 8) if n == 128 else ("tsum", 8, 12), A.is_ge)
-            cw = "pwd" if p1 == K else "xw2"
-            if p1 < K:
-                cp(("xw2", 16 + a0, 16 + a1), ("pwd", 16 + a0, 16 + a1))
+            if two:
+                words(cnt, 0, (("xa", 40), ("mx", 40)), p0, p1)
+                words(cnt, 16, (("xa", 32), ("mx", 40)), p0, p1)
+            else:
+                words(cnt, 16, (("mx", 0),), p0, p1)
+            tt(("nf", a0, a1), wd(48), ("tsum", 0, 8) if n == 128 else ("tsum", 8, 12), A.is_ge)
+            if two:
+                act(("xw2", a0, a1), wd(0), F.Identity, 479.0)
+                act(("xw2", 16 + a0, 16 + a1), wd(16), F.Abs, 479.0)
+                for a in range(a0, a1):
+                    x, c = ("xt", 64 * a, 64 * a + 64), ("chh", 64 * a, 64 * a + 64)
+                    act(x, ("io2",), F.Abs, ("xw2", a, a + 1))
+                    ts(c, x, ("xw2", 16 + a, 17 + a), A.is_equal, ("nf", a, a + 1), A.mult)
+                    mm(("ptb", 0, 64, 1, 0, 64), c, c, a == 0, a == 15)
+                continue
             for a in range(a0, a1):
                 x, c = ("xh", 64 * a, 64 * a + 64), ("chh", 64 * a, 64 * a + 64)
-                ts(c, ("io9",), (cw, 16 + a, 17 + a), A.is_equal, ("nf", a, a + 1), A.mult)
+                ts(c, ("io9",), wd(16, a, a + 1), A.is_equal, ("nf", a, a + 1), A.mult)
                 mm(("ptb", 0, 64, 1, 0, 64), x, c, a == 0, False)
                 mm(("ptb", 0, 64, 1, 0, 64), c, x, False, a == 15)
         mms(("phv", 0, K), ((idm[1], (xi,)), (block("lb", t), ("c120",)), (idm[1], ("nn",)), (block("nlb", t), ("yy",))))
         tt(("xn",), ("phv", 0, K), ("mx",), A.min)
-        ts(("hqf",), ("pq", 0, 16), 32767.0, A.add)
+        ts(("hqf",), ("pq", 0, 16), 2.0, A.mult, 32767.0, A.add)
         to_q(("pq", 16, 32), "lb", ("xl", 0, K), ("mx", 0, K))
         ts(("of",), ("pq", 16, 32), 2.0, A.mult, -1024.0, A.add)
         mms(("psb", 0, K), ((bom[1], ("xa",)), (bom[-1 / 64.0], ("xl",))))
@@ -449,54 +498,66 @@ def rank_program(g, core, T, topo):
         mms(("pcb", 0, K), ((con[-0.25], ("ones", 0, K)), (idm[-0.5], (gi,)), (idm[0.5], ("gs",))))
         act(("dg1",), ("pcb", 0, K), F.Identity, 12582912.0)
         act(("dg",), ("dg1",), F.Identity, -12582912.0)
-        mm(("pwd", K, 2 * K), ("bo16",), ("eh",))
+        mm(("pwd", K, 2 * K), bom[1], ("eh",))
         ts(("hr",), ("pwd", K, 2 * K), 32767.0, A.add)
         gat(("f",), ("tb",), ("of",), ("ms",), A.is_equal)
         mms(("pxp", K, 2 * K), ((con[-64], ("ones", 0, K)), (idm[1], (xi,)), (bom[64], ("f",))))
-        tt(XO, ("pxp", K, 2 * K), ("xn",), A.max)
-        send(XO, "xin%d" % (t + 1), "ax%d" % (t + 1))
+        for c0, c1, sem in ((0, CH, "ax"), (CH, K, "bx")) if CFG["cut"] and t < NV - 1 else ((0, K, "ax"),):
+            tt(("xo", K * t + c0, K * t + c1), ("pxp", K + c0, K + c1), ("xn", c0, c1), A.max)
+            send(("xo", K * t + c0, K * t + c1), ("xin%d" % (t + 1), c0, c1), "%s%d" % (sem, t + 1))
         to_q(("pq", 32, 48), "lb", ("f", 0, K))
         tt(("sq",), ("pq", 32, 48), ("hqf",), A.add)
-        nv = 16 - CFG["eqs"]
-        if nv < 16:
-            ts(("hqs", nv, 16), ("sq", nv, 16), -32767.0, A.add)
+        step = 16 // CFG["nsc"]
+        if CFG["eqs"]:
+            ts(("hqs",), ("sq",), -32767.0, A.add)
         bad = ("ptb", K, 2 * K)
         mm(bad, bom[1], ("thr",), True, False)
         mm(bad, bom[BIG / 8], ("yy",), False, False)
         mm(bad, bom[64 * BIG], ("f",), False, False)
         for a in range(16):
-            row = ("eq", 272 * a, 256 * a + 256)
-            if a < nv:
-                ts(row, ("hr", 16 * a, K), ("sq", a, a + 1), A.is_equal)
+            end = 16 * (a // step + 1) * step
+            n = end - 16 * a
+            row = ("eq", 272 * a, 272 * a + n)
+            if step - a % step > CFG["eqs"]:
+                ts(row, ("hr", 16 * a, end), ("sq", a, a + 1), A.is_equal)
             else:
-                e0 = 128 * (a - 8)
-                act(("ea", e0, e0 + K - 16 * a), ("pwd", K + 16 * a, 2 * K), F.Abs, ("hqs", a, a + 1), -1.0)
-                act(row, ("ea", e0, e0 + K - 16 * a), F.Relu, 1.0, -2.0)
-            if a < 15:
-                mm(("ptb", K + 16 * a + 16, 2 * K), bom[64 * BIG], ("eq", 272 * a + 16, 256 * a + 256), False, False)
+                act(("ea", 128 * a, 128 * a + n), ("pwd", K + 16 * a, K + end), F.Abs, ("hqs", a, a + 1), -1.0)
+                act(row, ("ea", 128 * a, 128 * a + n), F.Relu, 1.0, -2.0)
+            if n > 16:
+                mm(("ptb", K + 16 * a + 16, K + end), bom[64 * BIG], ("eq", 272 * a + 16, 272 * a + n), False, False)
         mm(bad, ("bow",), ("eq", 0, 16 * 272), False, True, ap=T.eq[:, :, 0:16])
         tt(("ls",), bad, ("drow",), A.min)
         to_q(("pq", 48, 64), "lb", ("ls", 0, K))
         tt(("lq",), ("pq", 48, 64), ("hqf",), A.max)
         cp(("so",), ("lq",))
-        step = 16 // CFG["nsc"]
-        for a in range(0, 16, step):
+        for a in reversed(range(0, 16, step)):
             scat(("lx",), ("so", a, a + step), ("xo", K * t + 16 * a, K * t + 16 * (a + step)))
         mms(("pcb", K, 2 * K), ((con[16], ("ones", 0, K)), (bom[-1 / 64.0], ("yy",)), (bom[-1], ("f",))))
         tt(("gm",), ("dg",), ("pcb", K, 2 * K), A.mult)
         mms(("pca", K, 2 * K), ((idm[1], (gi,)), (idm[1], ("gm",))))
         act(GO, ("pca", K, 2 * K), F.Copy)
-        send(GO, "gin%d" % (t + 1), "ag%d" % (t + 1))
-        for a in range(0, 16, step):
+        send(GO, ("gin%d" % (t + 1),), "ag%d" % (t + 1))
+        for a in reversed(range(0, 16, step) if t < NV - 1 else ()):
             scat(("lm",), ("so", a, a + step), ("go", K * t + 16 * a, K * t + 16 * (a + step)))
 
-    h = W // 2
-    op("V", lambda e: e.tensor_reduce(T.sm[:, 0:1], T.lm[:, 0:h], X.X, A.add), (("lm", 0, h),), (("sm", 0, 1),), cyc(h))
-    act(("cg", 0, h), ("lm", h, W), F.Copy, acc=("sm", 1, 2))
-    tt(("sm", 2, 3), ("sm", 0, 1), ("sm", 1, 2), A.add)
-    for q, y, a, sem in (("Y", T.yl, lex, "st0"), ("Y", T.yx, ("xin%d" % NV,), "st1"), ("Y", T.yg, ("gin%d" % NV,), "st2"), ("S", T.ym, ("sm", 2, 3), "st3")):
-        dma(q, y[:], v(a), sem, (a,), (), 1.3 + cols(a) / 1.0e3)
-    issue(g, T, order(calls))
+    for i in range(8):
+        act(("xh", 512 * (i % 2), 512 * (i % 2) + 512), ("lm", 512 * i, 512 * i + 512), F.Copy, acc=("sm", i, i + 1))
+    over = ("psb", 0, K)
+    mm(over, bom[1], ("zero",), True, False)
+    for a in range(16 - step):
+        end = 16 * (a // step + 1) * step
+        ts(("d", K * a + end, K * a + K), ("hr", end, K), ("sq", a, a + 1), A.is_equal, -1.0, A.mult)
+        mm(("psb", end, K), bom[64 * BIG], ("d", K * a + end, K * a + K), False, a == 15 - step)
+    tt(("ms",), over, ("ls",), A.is_gt)
+    mms(("phv", 0, K), ((idm[1], GO), (idm[-1], ("gs",))))
+    tt(("mn",), ("phv", 0, K), ("ms",), A.mult)
+    act(("mx",), ("mn",), F.Copy, acc=("sm", 8, 9))
+    op("V", lambda e: e.tensor_reduce(T.sm[:, 9:10], T.sm[:, 0:9], X.X, A.add), (("sm", 0, 9),), (("sm", 9, 10),), cyc(64))
+    for q, y, a, sem in (("Y", T.yl, lex, "st0"), ("Y", T.yx, ("xin%d" % NV,), "st1"), ("Y", T.yg, ("gin%d" % NV,), "st2"), ("S", T.ym, ("sm", 9, 10), "st3")):
+        dma(q, y[:], v(a), sem, (a,), (), 1.3 + cols(a) / 1.5e3)
+    if "calls" not in ORDER:
+        ORDER["calls"] = order(calls)
+    issue(g, T, [calls[i] for i in ORDER["calls"]])
     for i in range(4):
         g.wait_ge(T.sem["st%d" % i], 16)
-    g.wait_ge(T.sem.loc, 2 * NV * neng)
+    g.wait_ge(T.sem.loc, neng * sum("sent" in c for c in calls))

@@ -5,9 +5,11 @@ K = 256
 W = 4096
 NV = 4
 CH = 64
-CFG = {"parts": ((0, 128), (128, 256)), "vs": 32, "eqs": 2, "nsc": 2, "xs": (0, 4, 0, 0), "mn": (1, 1, 1, 1), "xq": 0, "gc": 64, "wait": 0.18,
-       "sgv": (1, 0, 0, 0), "far": 1.5, "cut": 1, "pe": 0.5, "hs": 64, "rounds": 2, "vc": 16,
-       "two": (1, 0, 0, 0), "us": 0, "thin": 192}
+CFG = {"parts": ((0, 128), (128, 256)), "lines": (), "gb": ("lk", "lb"), "vf": 1, "aw": 64, "gm": 1, "us": 0, "xo": 0, "rs": 0, "vp": (128, 160),
+       "gather": ((0, 64), (64, 128), (160, 224), (224, 256)), "compare": ((0, 64), (64, 128), (128, 224), (224, 256)), "nsc": 2, "xs": (0, 4, 0, 0), "mn": (1, 1, 1, 1), "xq": 0, "wait": 0.17,
+       "sgv": (0, 0, 0, 0), "far": 1.6, "cut": 1, "pe": 0.6, "hs": 64, "rounds": 1, "vc": 32,
+       "two": (1, 0, 0, 0), "thin": 224, "dv": 0}
+SHIFT = {'V hin h': -4.5, 'V lm g': 1.0, 'P pxp h': -3.5, 'V lm e': -14.5, 'P pcb h': -4.5, 'P pxp f': -4.5, 'V hqs f': -6.5, 'V win c': -6.5, 'S nn 1': -2.0, 'P phv f': -2.5, 'P pcb f': -4.0, 'P pxp n': -1, 'P pq f': -1}
 ORDER = {}
 
 SCRATCH = {}
@@ -23,28 +25,26 @@ for _t in range(NV + 1):
 for _d, _l in (
         ("bfloat16", (("xo", NV * K), ("go", NV * K), ("lx", W + K), ("lm", W + K), ("ones", 512),
                       ("bo1", 128), ("bo", 128), ("idn", 128), ("lt", 128), ("c1", 128), ("e1", 128), ("bd", 128), ("w1", 256), ("w2", 128),
-                      ("lk", 2048), ("lb", 2048), ("nlb", 512), ("ids", 6 * 128), ("bos", 7 * 128), ("zb", 128), ("cb", 3 * 128), ("cbr", 384),
-                      ("c120", K), ("bow", 128), ("thl", K), ("thr", K), ("drow", K), ("ia", K), ("ib", K), ("ra", 512), ("io2", 64),
+                      ("lk", 2048), ("lb", 2048), ("nlb", 512), ("ids", 6 * 128), ("bos", 13 * 128), ("cr", K), ("xc", 128), ("zb", 128), ("cb", 3 * 128), ("cbr", 384),
+                      ("c120", K), ("ia", K), ("ra", 512), ("io2", 64),
                       ("sel", 48), ("fb", 2 * K), ("cg", 16 * K), ("d", 16 * K), ("sg", K), ("xq", K), ("xa", K), ("xl", K), ("nn", K), ("yy", K),
                       ("gs", K), ("mn", K), ("mx", K), ("xn", K), ("ms", K), ("dg", K), ("gm", K), ("xh", 1024), ("chh", 1024), ("xt", 1024),
-                      ("h1", 64), ("tb", K), ("f", K), ("ea", 2048), ("ls", K), ("zero", K))),
-        ("float16", (("h16", K), ("eh", K), ("io9", 64))),
+                      ("h1", 64), ("tb", K), ("f", K), ("ea", 2048))),
+        ("float16", (("hh", 2 * K), ("dh", K), ("eh", K), ("io9", 64))),
         ("int32", (("wti", 2), ("thi", 1), ("tha", 2), ("jci", 1), ("jcj", 1), ("pr", K), ("p2", K), ("h", K))),
-        ("uint16", (("hu", K), ("hq", 16), ("of", 16), ("hr", K), ("so", 16))),
-        ("float32", (("wf", 2), ("thf", 2), ("jc", 1), ("io16", 16), ("md", 16), ("pw", 16), ("col", 11), ("u2s", K), ("hqf", 16), ("tsum", 12),
-                     ("nf", 16), ("xw2", 32), ("sq", 16), ("hqs", 16), ("dg1", K), ("lq", 16), ("sm", 10)))):
+        ("uint16", (("ho", NV * K), ("hin0", K), ("hin1", K), ("hin2", K), ("hin3", K), ("hq", 16), ("of", 16), ("so", 16))),
+        ("float32", (("wf", 2), ("thf", 2), ("jc", 1), ("io16", 16), ("md", 16), ("cv", 16), ("dm", 16), ("col", 11), ("u2s", K), ("hd", 32), ("win", 32), ("tsum", 12),
+                     ("nf", 16), ("xw2", 32), ("sq", 32), ("hqs", 16), ("lq", 16), ("sm", 16), ("vb", 128), ("id32", 128)))):
     for _n, _c in _l:
         _buf(_n, _c, _d)
-SCRATCH["eq"] = ("sbuf", [128, 16, 272], "bfloat16")
 for _n in ("pxp", "pca", "pcb", "psb", "phv", "pq", "pwd", "ptb"):
     _buf(_n, 512, "float32", "psum")
 
 SEMAPHORES = ["v", "s", "p", "gc", "loc"]
 SEMAPHORES += ["ld%d" % _i for _i in range(6)] + ["st%d" % _i for _i in range(4)]
-SEMAPHORES += ["%s%d" % (_n, _i) for _n in ("ax", "bx", "ag") for _i in range(1, NV + 1)]
+SEMAPHORES += ["%s%d" % (_n, _i) for _n in ("ax", "ah", "bh", "ag") for _i in range(1, NV + 1)]
 
 CYCLE = 0.83e-3
-BIG = 2.0 ** 27
 
 
 def span(a):
@@ -122,7 +122,7 @@ def order(calls):
     best = None
     ORDER["log"] = [round(max(way), 2)]
     for _ in range(CFG["rounds"]):
-        at, seq = place([w + c.get("first", 0.0) for w, c in zip(way, calls)], "dep", "next", False)
+        at, seq = place([w + c.get("first", 0.0) + SHIFT.get(c["tag"], 0.0) for w, c in zip(way, calls)], "dep", "next", False)
         end = [a + c["cost"] + c["lag"] for a, c in zip(at, calls)]
         ORDER["log"].append(round(max(end), 2))
         if best is None or max(end) < best[0]:
@@ -187,14 +187,16 @@ def rank_program(g, core, T, topo):
     if rank is None:
         return
     calls = []
-    parts = CFG["parts"]
+    parts, AW = CFG["parts"], CFG["aw"]
+    part = [""]
 
     def op(q, call, reads, writes, cost, lag=0.0, **more):
-        calls.append(dict(more, q=q, call=call, r=tuple(reads), w=tuple(writes), cost=cost, lag=lag))
+        tag = q + " " + (writes or reads)[0][0].rstrip("01234") + part[0]
+        if tag[:-2] in CFG["lines"]:
+            more["line"] = tag[:-2]
+        calls.append(dict(more, q=q, call=call, r=tuple(reads), w=tuple(writes), cost=cost, lag=lag, tag=tag))
 
     def v(a):
-        if a[0] == "eq" and len(a) > 1:
-            return T.eq[:, a[1] // 272, a[1] % 272:a[1] % 272 + a[2] - a[1]]
         if len(a) == 6:
             return T[a[0]][a[4]:a[5], a[1]:a[2]:a[3]]
         return T[a[0]][:] if len(a) == 1 else T[a[0]][:, a[1]:a[2]] if len(a) == 3 else T[a[0]][:, a[1]:a[2]:a[3]]
@@ -221,7 +223,7 @@ def rank_program(g, core, T, topo):
         op("V", lambda e: e.tensor_tensor(v(out), v(a), v(b), o), rw(a, b), rw(out), cyc(cols(out) * (2 if both else 1)))
 
     def gat(out, win, offs, b, o):
-        op("V", lambda e: e.tensor_tensor(v(out), v(win).indirect(v(offs)), v(b), o), rw(win, offs, b), rw(out), 0.05 + 1.56 * CYCLE * cols(out))
+        op("V", lambda e: e.tensor_tensor(v(out), v(win).indirect(v(offs)), v(b), o), rw(win, offs, b), rw(out), 0.05 + 2.2 * CYCLE * cols(out))
 
     def pick(out, win, offs):
         op("V", lambda e: e.tensor_copy(v(out), v(win).indirect(v(offs))), rw(win, offs), rw(out), 0.05 + 1.56 * CYCLE * cols(out))
@@ -231,6 +233,15 @@ def rank_program(g, core, T, topo):
 
     def scat(win, offs, a):
         op("V", lambda e: e.tensor_copy(v(win).indirect(v(offs)), v(a)), rw(offs, a), rw(win), 0.05 + 3.8 * CYCLE * cols(a))
+
+    def total(out, a):
+        op("V", lambda e: e.tensor_reduce(v(out), v(a), X.X, A.add), rw(a), rw(out), cyc(cols(a)))
+
+    def least(out, a):
+        op("V", lambda e: e.tensor_reduce(v(out), v(a), X.X, A.min), rw(a), rw(out), cyc(cols(a)))
+
+    def scan(out, a, b):
+        op("V", lambda e: e.tensor_tensor_scan(v(out), v(a), v(b), 0.0, A.mult, A.add), rw(a, b), rw(out), cyc(cols(a)))
 
     def fill(out, c):
         op("V", lambda e: e.memset(v(out), c), (), rw(out), cyc(cols(out), out))
@@ -245,11 +256,11 @@ def rank_program(g, core, T, topo):
             kw["accum_out"] = v(acc)
         src = v(a) if offs is None else v(a).indirect(v(offs))
         op("S", lambda e: e.activation(v(out), src, fn, **kw), rw(a, bias, scale, offs), rw(out, acc),
-           cyc(cols(out)) if offs is None else 0.065 + 1.56 * CYCLE * cols(out), line=offs and offs[0])
+           cyc(cols(out)) if offs is None else 0.065 + 1.56 * CYCLE * cols(out), line=offs and out[0])
 
     def mm(out, l, rh, st=True, sp=True, ap=None):
         op("P", lambda e: e.matmul(v(out), v(l), v(rh) if ap is None else ap, start=st, stop=sp), rw(l, rh), rw(out),
-           CFG["pe"] * CYCLE * max(min(64, cols(l)), cols(out)))
+           CFG["pe"] * CYCLE * max(min(64, cols(l)), cols(out)) * (4 if SCRATCH[l[0]][2] == "float32" else 1))
 
     def mms(out, terms):
         for i, (l, rh) in enumerate(terms):
@@ -284,22 +295,19 @@ def rank_program(g, core, T, topo):
     iota("io16", [[1, 16]], 0, 0, **small)
     sel(("lt",), ("bo",), [[1, 128]], A.is_gt, 0, -1)
     iota("io2", [[1, 64]], 2, 0, **small)
-    iota("ia", [[32, 16], [0, 16]], 0, 0, **small)
-    iota("ib", [[0, 16], [2, 16]], 0, 0, **small)
     sel(("ra", 0, 512, 1, 0, 64), ("ones", 0, 512, 1, 0, 64), [[-1, 4], [0, 8], [-4, 16]], A.is_equal, 0, 1)
 
     fill(("cbr", 0, 192), 4160.0)
-    fill(("cbr", 192, 384), 67584.0)
-    fill(("zero",), 0.0)
+    fill(("cbr", 192, 384), -65536.0)
     fill(("c120",), 120.0)
     idm, bom, con = {1: ("idn",)}, {1: ("bo",)}, {}
     for i, c in enumerate((-1, -32, 64, -256, 0.5, -0.5)):
         idm[c] = block("ids", i)
         ts(idm[c], ("idn",), float(c), A.mult)
-    for i, c in enumerate((-64, 64, -1 / 64.0, -1, 64 * BIG, BIG / 8, 0.5)):
+    for i, c in enumerate((-64, 64, -1 / 64.0, -1, 512, 128, 0.5, 8192, -8192, -8, -512, 2, -4096)):
         bom[c] = block("bos", i)
         ts(bom[c], ("bo",), float(c), A.mult)
-    for i, c in enumerate((16, -64, -0.25)):
+    for i, c in enumerate((16, -0.25, -64)):
         con[c] = block("cb", i)
         fill(con[c], c / 128.0)
     tt(("bd",), ("bo",), ("idn",), A.subtract)
@@ -313,8 +321,13 @@ def rank_program(g, core, T, topo):
     fill(("lb",), 0.0)
     for out, src in (("lk", ("e1", 0)), ("lb", bom[0.5])):
         for k in range(16):
-            act((out, 128 * k + k, 128 * (k + 1), 16), (src[0], src[1] + k, src[1] + 128, 16), F.Copy)
+            if out in CFG["gb"]:
+                sel((out, 128 * k + k, 128 * (k + 1), 16), (src[0], src[1] + k, src[1] + 128, 16), [[0, 8]], A.is_ge, 0, 0)
+            else:
+                act((out, 128 * k + k, 128 * (k + 1), 16), (src[0], src[1] + k, src[1] + 128, 16), F.Copy)
     ts(("nlb",), ("lb", 0, 512), -2.0, A.mult)
+    if CFG["vf"]:
+        act(("id32",), ("idn",), F.Copy)
     tt(("c1",), idm[0.5], ("lt",), A.subtract)
     ts(("zb",), ("c1",), 8192.0, A.mult)
     ts(("jcj",), ("jci",), 15, A.bitwise_and)
@@ -324,9 +337,7 @@ def rank_program(g, core, T, topo):
         ts(("col", i, i + 1), ("jc",), -8192.0, A.mult, c - 4096.0, A.add)
         ts(("col", 8 + i, 9 + i), ("jc",), -16384.0, A.mult, c, A.add)
     ts(("col", 3, 4), ("jc",), 4.0, A.mult, 2.0, A.add)
-    ts(("col", 4, 5), ("md", 0, 1), -120 * BIG, A.mult)
-    ts(("col", 5, 6), ("md", 1, 2), -BIG, A.mult)
-    ts(("col", 6, 7), ("md", 0, 1), 8192.0, A.mult)
+    ts(("col", 4, 8), ("md", 0, NV), 960.0, A.mult)
     ts(("io9",), ("io2",), 958.0, A.add)
     ts(("tha", 0, 1), ("thi",), 0xFF0, A.bitwise_and)
     ts(("tha", 1, 2), ("thi",), 15, A.bitwise_and)
@@ -340,17 +351,14 @@ def rank_program(g, core, T, topo):
     ts(("tsum", 0, 8), ("pwd", 0, 8), 64.0, A.mult)
     for hf in (0, 1):
         cp(("tsum", 8, 12, 1, 64 * hf, 64 * hf + 64), ("tsum", 4 * hf, 4 * hf + 4, 1, 64 * hf, 64 * hf + 64))
-    fill(("ms",), 0.5)
-    fill(("ms", 0, K, 16), 32768.0)
-    op("V", lambda e: e.tensor_tensor_scan(v(("thl",)), v(("ms",)), v(("zero",)), 2.0 ** -13, A.mult, A.add),
-       (("ms",), ("zero",)), (("thl",),), cyc(128))
-    tt(("pw",), ("md",), ("thl", 0, 16), A.mult)
-    op("V", lambda e: e.tensor_reduce(v(("col", 7, 8)), v(("pw",)), X.X, A.add), (("pw",),), (("col", 7, 8),), cyc(64))
-    ts(("bow",), ("bo",), ("col", 7, 8), A.mult, BIG / 2, A.mult)
-    ts(("thr",), ("thl",), ("col", 5, 6), A.mult, ("col", 4, 5), A.add)
-    ts(("ia",), ("ia",), ("md", 1, 2), A.mult, ("col", 6, 7), A.add)
-    ts(("ib",), ("ib",), ("md", 2, 3), A.mult)
-    tt(("drow",), ("ia",), ("ib",), A.add)
+    step = 16 // CFG["nsc"]
+    iota("ia", [[0, CFG["nsc"]], [1, 16 * step]], 128, 0, **small)
+    iota("cv", [[0, CFG["nsc"]], [16, step]], 64, 0, **small)
+    iota("dm", [[16, 16]], W, 0, **small)
+    ts(("cv",), ("cv",), ("jc",), A.add)
+    ts(("hd", 1, 32, 2), ("dm",), ("jc",), A.add, 0.5, A.mult)
+    ts(("dm",), ("hd", 1, 32, 2), -16383.5, A.add)
+    fill(("win",), 0.0)
 
     nxt = T.cores[(rank + 1) % len(T.cores)]
     rid, pid = topo.addr(nxt)[0], topo.addr(nxt)[1]
@@ -371,56 +379,76 @@ def rank_program(g, core, T, topo):
             mms((bank, K + out + p0 // 16, K + out + p1 // 16, 1) + r,
                 [((l, p0, p1, 1) + r, ("sel", s + n * hf, s + n * hf + n, 1) + r) for l, s in terms])
 
+    def places(src, c0, c1, raw, un, out):
+        n, x = c1 - c0, (src, c0, c1)
+
+        def half(bank, i, e0=c0, e1=c1):
+            return (bank[0], bank[1] + n * i + e0 - c0, bank[1] + n * i + e1 - c0)
+        mms(half(raw, 0), ((one, ("cbr", 0, n)), (("w2",), x)))
+        mm(half(raw, 1), block("w1", 0), x)
+        act(("fb", c0, c1), half(raw, 0), F.Identity, -2047.5)
+        act(("fb", K + c0, K + c1), half(raw, 1), F.Identity, 530432.5)
+        mm((un[0], un[1], un[1] + 2 * n), one, ("cbr", 192 - n, 192 + n), True, False)
+        mm(half(un, 0), block("w1", 0), x, False, False)
+        mm(half(un, 1), block("w1", 1), x, False, False)
+        mm(half(un, 0), idm[-1], ("fb", K + c0, K + c1), False, True)
+        us = CFG["us"] and not out
+        if us:
+            mms(half(raw, 1), ((one, ("cbr", 0, n)), (("w2",), x), (idm[-1], ("fb", c0, c1))))
+            act(("u2s", c0, c1), half(raw, 1), F.Copy)
+        for e0 in range(c0, c1, CFG["hs"] if out else n):
+            e1 = min(c1, e0 + (CFG["hs"] if out else n))
+            if not us:
+                tt(("u2s", e0, e1), half(raw, 0, e0, e1), ("fb", e0, e1), A.subtract)
+            tt(("pr", e0, e1), ("u2s", e0, e1), half(un, 0, e0, e1), A.mult)
+            tt(("p2", e0, e1), ("pr", e0, e1), half(un, 1, e0, e1), A.add)
+            ts(("h", e0, e1), ("p2", e0, e1), 5, A.arith_shift_right, 4095, A.bitwise_and)
+            if out:
+                cp((out, e0, e1), ("h", e0, e1))
+            else:
+                ts(("hh", e0, e1), ("h", e0, e1), -2048.0, A.add)
+
     for t in range(NV):
         xi, gi = "xin%d" % t, "gin%d" % t
         XO, GO = ("xo", K * t, K * t + K), ("go", K * t, K * t + K)
-        for c0, c1, raw, un in ((0, CH, "pca", "psb"), (CH, K, "pcb", "phv")):
-            n, x = c1 - c0, (xi, c0, c1)
-            mms((raw, 0, n), ((one, ("cbr", 0, n)), (("w2",), x)))
-            mm((raw, n, 2 * n), block("w1", 0), x)
-            act(("fb", c0, c1), (raw, 0, n), F.Identity, -2047.5)
-            act(("fb", K + c0, K + c1), (raw, n, 2 * n), F.Identity, 530432.5)
-            mm((un, 0, 2 * n), one, ("cbr", 192 - n, 192 + n), True, False)
-            mm((un, 0, n), block("w1", 0), x, False, False)
-            mm((un, n, 2 * n), block("w1", 1), x, False, False)
-            mm((un, 0, n), idm[-1], ("fb", K + c0, K + c1), False, False)
-            mm((un, n, 2 * n), idm[-32], ("fb", K + c0, K + c1), False, True)
-            for e0 in range(c0, c1, CFG["hs"]):
-                e1 = min(c1, e0 + CFG["hs"])
-                tt(("u2s", e0, e1), (raw, e0 - c0, e1 - c0), ("fb", e0, e1), A.subtract)
-                tt(("pr", e0, e1), ("u2s", e0, e1), (un, e0 - c0, e1 - c0), A.mult)
-                tt(("p2", e0, e1), ("pr", e0, e1), (un, n + e0 - c0, n + e1 - c0), A.add)
-                ts(("h", e0, e1), ("p2", e0, e1), 5, A.arith_shift_right, 4095, A.bitwise_and)
-                cp(("hu", e0, e1), ("h", e0, e1))
-        mm(("pxp", 0, K), idm[1], (xi,))
-        ts(("h16",), ("hu",), -2048.0, A.add)
+        hu, ahead = "hin%d" % t, AW if t < NV - 1 else 0
+        part[0] = " h"
+        if t == 0:
+            places(xi, 0, CH, ("psb", 0), ("phv", 0), hu)
+        places(xi, AW if t else CH, K, ("pwd", 0), ("pcb", 0), hu)
+        thin = CFG["thin"]
+        mm(("pxp", 0, thin), idm[1], (xi, 0, thin))
+        for r in range(2):
+            mm(("pxp", thin + r, thin + 2 * (K - thin), 2), idm[1], (xi, thin, K))
+        for p0, p1 in parts:
+            ts(("hh", K + p0, K + p1), (hu, p0, p1), -2048.0, A.add)
         if CFG["xq"]:
             act(("xq",), (xi,), F.Identity, 128.625, 0.25)
         else:
             ts(("xq",), (xi,), 0.25, A.mult, 128.625, A.add)
-        vs = K - CFG["vs"]
-        for c in range(0, vs, CFG["gc"]):
-            act(("cg", 16 * c, 16 * min(c + CFG["gc"], vs)), lex, F.Copy, offs=("hu", c, min(c + CFG["gc"], vs)))
-        for c in range(vs, K, CFG["vc"]):
-            pick(("cg", 16 * c, 16 * (c + CFG["vc"])), lex, ("hu", c, c + CFG["vc"]))
-        thin = CFG["thin"]
-        for r in range(2 if thin < K else 0):
-            mm(("pxp", K + r, K + 2 * (K - thin), 2), idm[1], (xi, thin, K))
+        if t == NV - 1:
+            mms(("ptb", 128, 256), [(idm[1], ("lm", c, c + 128)) for c in range(0, W, 128)])
+            total(("sm", 0, 1), ("ptb", 128, 256))
+        v0, v1 = CFG["vp"]
+        for c, e in CFG["gather"]:
+            act(("cg", 16 * c, 16 * e), lex, F.Copy, offs=(hu, c, e))
+        for c in range(v0, v1, 16):
+            pick(("cg", 16 * c, 16 * c + 256), lex, (hu, c, c + 16))
         for p, (p0, p1) in enumerate(parts):
             n, cnt = p1 - p0, ("pca", "pcb")[p % 2]
             a0, a1 = p0 // 16, p1 // 16
+            part[0] = " %d" % p
 
             def my(name):
                 return (name, p0, p1)
-            for c in range(p0, min(p1, thin), CH):
-                for k in range(16):
-                    d = ("d", 16 * c + k * CH, 16 * c + k * CH + CH)
-                    tt(d, ("cg", 16 * c + k, 16 * (c + CH), 16), ("pxp", c, c + CH), A.not_equal)
-                    mm((cnt, c - p0, c - p0 + CH), block("lk", k), d, k == 0, k == 15)
-            for c in reversed(range(max(p0, thin), p1, 32)):
-                for k in range(8):
+            for c, e in (x for x in CFG["compare"] if p0 <= x[0] < p1):
+                for k in range(16 if c < thin else 0):
+                    d = ("d", 16 * c + k * (e - c), 16 * c + (k + 1) * (e - c))
+                    tt(d, ("cg", 16 * c + k, 16 * e, 16), ("pxp", c, e), A.not_equal)
+                    mm((cnt, c - p0, e - p0), block("lk", k), d, k == 0, k == 15)
+                for k in range(0 if c < thin else 8):
                     d0 = 16 * c + k * CH
-                    tt(("d", d0, d0 + CH), ("cg", 16 * c + k, 16 * (c + 32), 8), ("pxp", K + 2 * (c - thin), K + 2 * (c - thin) + CH), A.not_equal)
+                    tt(("d", d0, d0 + CH), ("cg", 16 * c + k, 16 * (c + 32), 8), ("pxp", 2 * c - thin, 2 * c - thin + CH), A.not_equal)
                     for r in (0, 1):
                         mm((cnt, c - p0, c - p0 + 32), block("lk", k + 8 * r), ("d", d0 + r, d0 + CH, 2), k + r == 0, k + r == 8)
             sb, o = ("psb", "pwd")[p % 2], 8 * CFG["sgv"][p]
@@ -429,13 +457,13 @@ def rank_program(g, core, T, topo):
             else:
                 act(my("sg"), (cnt, 0, n), F.Sign, -13.5, -1.0)
             z = (("zb",), my("sg"))
-            mms(("phv", 0, n), ((idm[1], my("h16")), z))
+            mms(("phv", 0, n), ((idm[1], ("hh", K + p0, K + p1)), z))
             ts(my("eh"), ("phv", 0, n), ("col", o, o + 1), A.add, -2048.0, A.max)
             to_q(("pq", a0, a1), "lb", my("eh"))
             ts(("hq", a0, a1), ("pq", a0, a1), 2.0, A.mult, 32767.0, A.add)
             mms((sb, 0, n), ((idm[1], my(xi)), z))
             mms((sb, n, 2 * n), ((idm[64], my(xi)), (idm[-256], my("xq")), z))
-            mms((sb, 2 * n, 3 * n), ((idm[1], ("cg", 16 * p0 + t, 16 * p1, 16)), (idm[-1], my(xi)), (bom[-64], my("sg"))))
+            mms((sb, 2 * n, 3 * n), ((idm[-1], my(xi)), (idm[1], ("cg", 16 * p0 + t, 16 * p1, 16)), (bom[-64], my("sg"))))
             act(my("xa"), (sb, 0, n), F.Relu, ("col", o + 1, o + 2))
             act(my("yy"), my("xa"), F.Relu, 64.0, -64.0)
             act(my("xl"), (sb, n, 2 * n), F.Relu, ("col", o + 2, o + 3))
@@ -456,23 +484,32 @@ def rank_program(g, core, T, topo):
                     ts(("xh", 64 * a, 64 * a + 64), ("io2",), ("xw2", a, a + 1), A.is_equal)
             act(my("gs"), mng, F.Copy, offs=("hq", a0, a1))
             early = ((gi, 0), ("yy", 16), ("yy", 24))
-            if CFG["mn"][p]:
+            if CFG["mn"][p] == 2:
+                act(my("cr"), lex, F.Copy, offs=("hq", a0, a1))
+                mm((cnt, 128, 128 + n), idm[1], my(gi))
+                mm((cnt, 0, n), idm[1], my("yy"))
+                tt(my("mn"), (cnt, 128, 128 + n), my("gs"), A.min)
+                tt(my("mx"), (cnt, 0, n), my("cr"), A.max)
+                words(cnt, 48, early + (("gs", 0), ("mn", 8)), p0, p1)
+            elif CFG["mn"][p]:
                 gat(my("mn"), mng, ("hq", a0, a1), my(gi), A.min)
                 words(cnt, 48, early + (("gs", 0), ("mn", 8)), p0, p1)
             else:
                 mms((cnt, 128, 128 + n), ((idm[-1], my(gi)), (idm[1], my("gs"))))
                 act(my("mn"), (cnt, 128, 128 + n), F.Abs)
                 words(cnt, 48, early[1:] + (("mn", 0),), p0, p1)
-            gat(my("mx"), lex, ("hq", a0, a1), my("yy"), A.max)
+            if CFG["mn"][p] < 2:
+                gat(my("mx"), lex, ("hq", a0, a1), my("yy"), A.max)
             if two:
                 words(cnt, 0, (("xa", 40), ("mx", 40)), p0, p1)
                 words(cnt, 16, (("xa", 32), ("mx", 40)), p0, p1)
             else:
                 words(cnt, 16, (("mx", 0),), p0, p1)
-            tt(("nf", a0, a1), wd(48), ("tsum", 0, 8) if n == 128 else ("tsum", 8, 12), A.is_ge)
             if two:
                 act(("xw2", a0, a1), wd(0), F.Identity, 479.0)
                 act(("xw2", 16 + a0, 16 + a1), wd(16), F.Abs, 479.0)
+            tt(("nf", a0, a1), wd(48), ("tsum", 0, 8) if n == 128 else ("tsum", 8, 12), A.is_ge)
+            if two:
                 for a in range(a0, a1):
                     x, c = ("xt", 64 * a, 64 * a + 64), ("chh", 64 * a, 64 * a + 64)
                     act(x, ("io2",), F.Abs, ("xw2", a, a + 1))
@@ -484,77 +521,76 @@ def rank_program(g, core, T, topo):
                 ts(c, ("io9",), wd(16, a, a + 1), A.is_equal, ("nf", a, a + 1), A.mult)
                 mm(("ptb", 0, 64, 1, 0, 64), x, c, a == 0, False)
                 mm(("ptb", 0, 64, 1, 0, 64), c, x, False, a == 15)
-        mms(("phv", 0, K), ((idm[1], (xi,)), (block("lb", t), ("c120",)), (idm[1], ("nn",)), (block("nlb", t), ("yy",))))
-        tt(("xn",), ("phv", 0, K), ("mx",), A.min)
-        ts(("hqf",), ("pq", 0, 16), 2.0, A.mult, 32767.0, A.add)
+        def unmerged(bank, o, n):
+            mms((bank, o, o + n), ((idm[1], (xi, 0, n)), (block("lb", t), ("c120", 0, n)), (idm[1], ("nn", 0, n)), (block("nlb", t), ("yy", 0, n))))
+        if ahead:
+            part[0] = " n"
+            unmerged("psb", K, AW)
+            tt(("xc", 0, AW), ("psb", K, K + AW), ("mx", 0, AW), A.min)
+            places("xc", 0, AW, ("psb", 0), ("pxp", 0), None)
+        part[0] = " f"
+        mms(("phv", 0, K), ((idm[1], (xi,)), (idm[1], ("nn",)), (block("nlb", t), ("yy",))))
+        act(("xn",), ("phv", 0, K), F.Identity, ("col", 4 + t, 5 + t))
         to_q(("pq", 16, 32), "lb", ("xl", 0, K), ("mx", 0, K))
         ts(("of",), ("pq", 16, 32), 2.0, A.mult, -1024.0, A.add)
-        mms(("psb", 0, K), ((bom[1], ("xa",)), (bom[-1 / 64.0], ("xl",))))
-        act(("ms",), ("psb", 0, K), F.Copy)
+        tt(("hd", 0, 32, 2), ("pq", 0, 16), ("dm",), A.subtract)
+        ts(("hqs",), ("pq", 0, 16), -1024.0, A.mult, 2.0 ** 24 - 1, A.min)
+        tt(("hqs",), ("hqs",), ("cv",), A.subtract)
+        mms(("pca", K, 2 * K), ((bom[1], ("xa",)), (bom[-1 / 64.0], ("xl",))))
+        act(("ms",), ("pca", K, 2 * K), F.Copy)
         ts(("h1", 0, 64, 1, 0, 64), ("ptb", 0, 64, 1, 0, 64), 1.0, A.min)
         for q in range(4):
             mm(("pca", 64 * q, 64 * q + 64), ("ra", 128 * q, 128 * q + 128, 1, 0, 64), ("h1", 0, 64, 1, 0, 64))
         act(("tb",), ("pca", 0, K), F.Identity, -1.0, ("col", 3, 4))
-        mms(("pcb", 0, K), ((con[-0.25], ("ones", 0, K)), (idm[-0.5], (gi,)), (idm[0.5], ("gs",))))
-        act(("dg1",), ("pcb", 0, K), F.Identity, 12582912.0)
-        act(("dg",), ("dg1",), F.Identity, -12582912.0)
-        mm(("pwd", K, 2 * K), bom[1], ("eh",))
-        ts(("hr",), ("pwd", K, 2 * K), 32767.0, A.add)
+        if CFG["dv"]:
+            mms(("pcb", 0, K), ((idm[-0.5], (gi,)), (idm[0.5], ("gs",))))
+            ts(("dh",), ("pcb", 0, K), 1535.75, A.add)
+        else:
+            mms(("pcb", 0, K), ((idm[0.5], (gi,)), (idm[0.5], ("gs",)), (idm[-1], ("mn",))))
+            act(("dg",), ("pcb", 0, K), F.Identity, 127.75)
         gat(("f",), ("tb",), ("of",), ("ms",), A.is_equal)
-        mms(("pxp", K, 2 * K), ((con[-64], ("ones", 0, K)), (idm[1], (xi,)), (bom[64], ("f",))))
-        for c0, c1, sem in ((0, CH, "ax"), (CH, K, "bx")) if CFG["cut"] and t < NV - 1 else ((0, K, "ax"),):
-            tt(("xo", K * t + c0, K * t + c1), ("pxp", K + c0, K + c1), ("xn", c0, c1), A.max)
-            send(("xo", K * t + c0, K * t + c1), ("xin%d" % (t + 1), c0, c1), "%s%d" % (sem, t + 1))
-        to_q(("pq", 32, 48), "lb", ("f", 0, K))
-        tt(("sq",), ("pq", 32, 48), ("hqf",), A.add)
-        step = 16 // CFG["nsc"]
-        if CFG["eqs"]:
-            ts(("hqs",), ("sq",), -32767.0, A.add)
-        bad = ("ptb", K, 2 * K)
-        mm(bad, bom[1], ("thr",), True, False)
-        mm(bad, bom[BIG / 8], ("yy",), False, False)
-        mm(bad, bom[64 * BIG], ("f",), False, False)
-        for a in range(16):
-            end = 16 * (a // step + 1) * step
-            n = end - 16 * a
-            row = ("eq", 272 * a, 272 * a + n)
-            if step - a % step > CFG["eqs"]:
-                ts(row, ("hr", 16 * a, end), ("sq", a, a + 1), A.is_equal)
-            else:
-                act(("ea", 128 * a, 128 * a + n), ("pwd", K + 16 * a, K + end), F.Abs, ("hqs", a, a + 1), -1.0)
-                act(row, ("ea", 128 * a, 128 * a + n), F.Relu, 1.0, -2.0)
-            if n > 16:
-                mm(("ptb", K + 16 * a + 16, K + end), bom[64 * BIG], ("eq", 272 * a + 16, 272 * a + n), False, False)
-        mm(bad, ("bow",), ("eq", 0, 16 * 272), False, True, ap=T.eq[:, :, 0:16])
-        tt(("ls",), bad, ("drow",), A.min)
-        to_q(("pq", 48, 64), "lb", ("ls", 0, K))
-        tt(("lq",), ("pq", 48, 64), ("hqf",), A.max)
-        cp(("so",), ("lq",))
-        for a in reversed(range(0, 16, step)):
-            scat(("lx",), ("so", a, a + step), ("xo", K * t + 16 * a, K * t + 16 * (a + step)))
-        mms(("pcb", K, 2 * K), ((con[16], ("ones", 0, K)), (bom[-1 / 64.0], ("yy",)), (bom[-1], ("f",))))
-        tt(("gm",), ("dg",), ("pcb", K, 2 * K), A.mult)
-        mms(("pca", K, 2 * K), ((idm[1], (gi,)), (idm[1], ("gm",))))
-        act(GO, ("pca", K, 2 * K), F.Copy)
+        if ahead:
+            part[0] = " s"
+            mms(("psb", 0, AW), ((idm[1], ("hh", K, K + AW)), (idm[-1], ("hh", 0, AW)), (bom[8192], ("f", 0, AW))))
+            act(("vb", 0, AW), ("psb", 0, AW), F.Relu, -4096.0)
+            mms(("phv", 0, AW), ((idm[1], ("hh", 0, AW)), (bom[-4096], ("f", 0, AW)), (("id32",), ("vb", 0, AW))))
+            ts(("ho", K * t, K * t + AW), ("phv", 0, AW), 2048.0, A.add)
+            send(("ho", K * t, K * t + AW), ("hin%d" % (t + 1), 0, AW), "ah%d" % (t + 1))
+            part[0] = " f"
+        mms(("pxp", K, 2 * K), ((idm[1], ("mx",)), (bom[64], ("f",))))
+        tt(XO, ("pxp", K, 2 * K), ("xn",), A.min)
+        send(XO, ("xin%d" % (t + 1),), "ax%d" % (t + 1))
+        mms(("pwd", K, 2 * K), ((bom[512], ("eh",)), (idm[1], ("ia",)), (bom[128], ("f",))))
+        part[0] = " c"
+        for a0 in reversed(range(0, 16, step)):
+            a1 = a0 + step
+            for a in reversed(range(a0, a1)):
+                row = ("ea", 128 * a, 128 * a + 16 * (a + 1 - a0))
+                act(row, ("pwd", K + 16 * a0, K + 16 * a + 16), F.Abs, ("hqs", a, a + 1))
+                least(("lq", a, a + 1), row)
+            ts(("win", 2 * a0 + 1, 2 * a1, 2), ("lq", a0, a1), 64.0, A.is_equal)
+            scan(("sq", 2 * a0, 2 * a1), ("win", 2 * a0, 2 * a1), ("hd", 2 * a0, 2 * a1))
+            ts(("so", a0, a1), ("sq", 2 * a0 + 1, 2 * a1, 2), 2.0, A.mult)
+            scat(("lx",), ("so", a0, a1), ("xo", K * t + 16 * a0, K * t + 16 * a1))
+        part[0] = " g"
+        step_ = ((idm[1], ("dh",)),) if CFG["dv"] else ((idm[1], ("dg",)), (idm[1], ("mn",)), (idm[-1], (gi,)))
+        mms(("pcb", K, 2 * K), step_ + ((bom[-8], ("yy",)), (bom[-512], ("f",))))
+        act(("gm",), ("pcb", K, 2 * K), F.Relu, 7680.0 - 1408 * CFG["dv"])
+        mms(("pca", K, 2 * K), ((idm[1], (gi,)), (bom[2], ("yy",)), (bom[128], ("f",)), (idm[1], ("gm",))))
+        act(GO, ("pca", K, 2 * K), F.Identity, -2048.0)
         send(GO, ("gin%d" % (t + 1),), "ag%d" % (t + 1))
-        for a in reversed(range(0, 16, step) if t < NV - 1 else ()):
-            scat(("lm",), ("so", a, a + step), ("go", K * t + 16 * a, K * t + 16 * (a + step)))
+        if t == NV - 1:
+            part[0] = " e"
+            act(("lm", W, W + K), GO, F.Copy, acc=("sm", 1, 2))
+        for a in reversed(range(0, 16, step)):
+            if t == NV - 1:
+                act(("gs", 16 * a, 16 * (a + step)), ("lm",), F.Identity, None, -1.0, ("so", a, a + step), ("sm", 2 + a // step, 3 + a // step))
+            if a or t < NV - 1:
+                scat(("lm",), ("so", a, a + step), ("go", K * t + 16 * a, K * t + 16 * (a + step)))
 
-    for i in range(8):
-        act(("xh", 512 * (i % 2), 512 * (i % 2) + 512), ("lm", 512 * i, 512 * i + 512), F.Copy, acc=("sm", i, i + 1))
-    over = ("psb", 0, K)
-    mm(over, bom[1], ("zero",), True, False)
-    for a in range(16 - step):
-        end = 16 * (a // step + 1) * step
-        ts(("d", K * a + end, K * a + K), ("hr", end, K), ("sq", a, a + 1), A.is_equal, -1.0, A.mult)
-        mm(("psb", end, K), bom[64 * BIG], ("d", K * a + end, K * a + K), False, a == 15 - step)
-    tt(("ms",), over, ("ls",), A.is_gt)
-    mms(("phv", 0, K), ((idm[1], GO), (idm[-1], ("gs",))))
-    tt(("mn",), ("phv", 0, K), ("ms",), A.mult)
-    act(("mx",), ("mn",), F.Copy, acc=("sm", 8, 9))
-    op("V", lambda e: e.tensor_reduce(T.sm[:, 9:10], T.sm[:, 0:9], X.X, A.add), (("sm", 0, 9),), (("sm", 9, 10),), cyc(64))
-    for q, y, a, sem in (("Y", T.yl, lex, "st0"), ("Y", T.yx, ("xin%d" % NV,), "st1"), ("Y", T.yg, ("gin%d" % NV,), "st2"), ("S", T.ym, ("sm", 9, 10), "st3")):
-        dma(q, y[:], v(a), sem, (a,), (), 1.3 + cols(a) / 1.5e3)
+    total(("sm", 15, 16), ("sm", 0, 2 + CFG["nsc"]))
+    for q, y, a, sem in (("Y", T.yl, lex, "st0"), ("Y", T.yx, ("xin%d" % NV,), "st1"), ("Y", T.yg, ("gin%d" % NV,), "st2"), ("S", T.ym, ("sm", 15, 16), "st3")):
+        dma(q, y[:], v(a), sem, (a,), (), 1.3 + cols(a) / 2.5e3)
     if "calls" not in ORDER:
         ORDER["calls"] = order(calls)
     issue(g, T, [calls[i] for i in ORDER["calls"]])

import numpy as np
from concourse.mybir import AluOpType as A, ActivationFunctionType as F, AxisListType as X

K = 256
W = 4096
NV = 4
CH = 64
CFG = {"parts": ((0, 128), (128, 256)), "lines": (), "gb": ("lk", "lb"), "vf": 1, "aw": 64, "gm": 1, "us": 0, "xo": 0, "rs": 0, "vp": (128, 160),
       "gather": ((0, 64), (64, 128), (160, 224), (224, 256)), "compare": ((0, 64), (64, 128), (128, 224), (224, 256)), "nsc": 2, "xs": (0, 4, 0, 0), "mn": (1, 1, 1, 1), "xq": 0, "wait": 0.17,
       "sgv": (0, 0, 0, 0), "far": 1.6, "cut": 1, "pe": 0.6, "hs": 64, "rounds": 1, "vc": 32,
       "two": (1, 0, 0, 0), "thin": 224, "dv": 0}
SHIFT = {'V hin h': -4.5, 'V lm g': 1.0, 'P pxp h': -3.5, 'V lm e': -14.5, 'P pcb h': -4.5, 'P pxp f': -4.5, 'V hqs f': -6.5, 'V win c': -6.5, 'S nn 1': -2.0, 'P phv f': -2.5, 'P pcb f': -4.0, 'P pxp n': -1, 'P pq f': -1}
ORDER = {}

SCRATCH = {}


def _buf(name, cols, dtype, where="sbuf", rows=128):
    SCRATCH[name] = (where, [rows, cols], dtype)


for _t in range(NV + 1):
    _buf("xin%d" % _t, K, "bfloat16")
    _buf("gin%d" % _t, K, "bfloat16")
for _d, _l in (
        ("bfloat16", (("xo", NV * K), ("go", NV * K), ("lx", W + K), ("lm", W + K), ("ones", 512),
                      ("bo1", 128), ("bo", 128), ("idn", 128), ("lt", 128), ("c1", 128), ("e1", 128), ("bd", 128), ("w1", 256), ("w2", 128),
                      ("lk", 2048), ("lb", 2048), ("nlb", 512), ("ids", 6 * 128), ("bos", 13 * 128), ("cr", K), ("xc", 128), ("zb", 128), ("cb", 3 * 128), ("cbr", 384),
                      ("c120", K), ("ia", K), ("ra", 512), ("io2", 64),
                      ("sel", 48), ("fb", 2 * K), ("cg", 16 * K), ("d", 16 * K), ("sg", K), ("xq", K), ("xa", K), ("xl", K), ("nn", K), ("yy", K),
                      ("gs", K), ("mn", K), ("mx", K), ("xn", K), ("ms", K), ("dg", K), ("gm", K), ("xh", 1024), ("chh", 1024), ("xt", 1024),
                      ("h1", 64), ("tb", K), ("f", K), ("ea", 2048))),
        ("float16", (("hh", 2 * K), ("dh", K), ("eh", K), ("io9", 64))),
        ("int32", (("wti", 2), ("thi", 1), ("tha", 2), ("jci", 1), ("jcj", 1), ("pr", K), ("p2", K), ("h", K))),
        ("uint16", (("ho", NV * K), ("hin0", K), ("hin1", K), ("hin2", K), ("hin3", K), ("hq", 16), ("of", 16), ("so", 16))),
        ("float32", (("wf", 2), ("thf", 2), ("jc", 1), ("io16", 16), ("md", 16), ("cv", 16), ("dm", 16), ("col", 11), ("u2s", K), ("hd", 32), ("win", 32), ("tsum", 12),
                     ("nf", 16), ("xw2", 32), ("sq", 32), ("hqs", 16), ("lq", 16), ("sm", 16), ("vb", 128), ("id32", 128)))):
    for _n, _c in _l:
        _buf(_n, _c, _d)
for _n in ("pxp", "pca", "pcb", "psb", "phv", "pq", "pwd", "ptb"):
    _buf(_n, 512, "float32", "psum")

SEMAPHORES = ["v", "s", "p", "gc", "loc"]
SEMAPHORES += ["ld%d" % _i for _i in range(6)] + ["st%d" % _i for _i in range(4)]
SEMAPHORES += ["%s%d" % (_n, _i) for _n in ("ax", "ah", "bh", "ag") for _i in range(1, NV + 1)]

CYCLE = 0.83e-3


def span(a):
    return (a[0], 0, SCRATCH[a[0]][1][1]) if len(a) == 1 else a[:3]


def order(calls):
    log, banks, sent = {}, {}, {}
    for i, c in enumerate(calls):
        dep = {}
        for wr, accs in ((False, c["r"]), (True, c["w"])):
            for a in accs:
                name, lo, hi = span(a)
                for j, l, h, w in log.get(name, ()):
                    if l < hi and lo < h and (w or wr):
                        dep[j] = CFG["wait"]
        for name in {span(a)[0] for a in c["r"] + c["w"] if SCRATCH[a[0]][0] == "psum"}:
            b = banks.setdefault(name, {"q": None, "now": [], "before": []})
            if b["q"] != c["q"]:
                b["q"], b["before"], b["now"] = c["q"], b["now"], []
            for j in b["before"]:
                dep[j] = CFG["wait"]
            if c["q"] == "P":
                for j in b["now"]:
                    dep[j] = 0.0
                b["now"] = b["now"][-1:]
            b["now"].append(i)
        if c["q"] == "A":
            dep[sent[c["sem"]]] = 0.0
        if c.get("line"):
            dep.setdefault(sent.get(c["line"], i), 0.0)
            sent[c["line"]] = i
        if "sent" in c:
            sent[c["sent"]] = i
        for wr, accs in ((True, c["w"]), (False, c["r"])):
            for a in accs:
                name, lo, hi = span(a)
                rows = log.setdefault(name, [])
                if wr:
                    rows[:] = [r for r in rows if not (lo <= r[1] and r[2] <= hi)]
                rows.append((i, lo, hi, wr))
        dep.pop(i, None)
        c["dep"], c["next"] = {j: x + calls[j]["lag"] for j, x in dep.items()}, {}
        for j, x in c["dep"].items():
            calls[j]["next"][i] = x

    def place(rank, before, after, tail):
        left = [len(c[before]) for c in calls]
        at = [c["lag"] if tail else 0.0 for c in calls]
        busy = {q: ([], []) for q in "VSPGYA"}
        ready = {i for i in range(len(calls)) if not left[i]}
        seq = []
        while ready:
            i = max(ready, key=lambda i: (rank[i], -i))
            ready.remove(i)
            c = calls[i]
            starts, ends = busy[c["q"]]
            k = int(np.searchsorted(ends, at[i], side="right")) if ends else 0
            while k < len(starts) and starts[k] < at[i] + c["cost"] - 1e-9:
                at[i] = max(at[i], ends[k])
                k += 1
            starts.insert(k, at[i])
            ends.insert(k, at[i] + c["cost"])
            seq.append(i)
            for j, x in c[after].items():
                at[j] = max(at[j], at[i] + c["cost"] + x)
                left[j] -= 1
                if not left[j]:
                    ready.add(j)
        return at, seq

    way = [0.0] * len(calls)
    for i in reversed(range(len(calls))):
        way[i] = calls[i]["cost"] + max([way[j] + x for j, x in calls[i]["next"].items()], default=calls[i]["lag"])
    best = None
    ORDER["log"] = [round(max(way), 2)]
    for _ in range(CFG["rounds"]):
        at, seq = place([w + c.get("first", 0.0) + SHIFT.get(c["tag"], 0.0) for w, c in zip(way, calls)], "dep", "next", False)
        end = [a + c["cost"] + c["lag"] for a, c in zip(at, calls)]
        ORDER["log"].append(round(max(end), 2))
        if best is None or max(end) < best[0]:
            pos = {i: k for k, i in enumerate(seq)}
            best = (max(end), sorted(range(len(calls)), key=lambda i: (at[i], pos[i])))
        back = place(end, "next", "dep", True)[0]
        way = [a + c["cost"] for a, c in zip(back, calls)]
    return best[1]


def issue(g, T, calls):
    queue = {"V": g.vector, "S": g.scalar, "P": g.tensor, "G": g, "Y": g.sync}
    own = {"V": "v", "S": "s", "P": "p", "G": "gc"}
    total, log = {}, {}
    know = {q: {} for q in queue}
    for seq, c in enumerate(calls):
        q, sem = c["q"], c.get("sem")
        if q == "A":
            val, clock = c["val"], {sem: c["val"]}
        else:
            found = []
            for wr, accs in ((False, c["r"]), (True, c["w"])):
                for a in accs:
                    name, lo, hi = span(a)
                    bank = SCRATCH[name][0] == "psum"
                    for r in log.get(name, ()):
                        if bank and r["q"] != q:
                            found.append(r)
                        elif r["lo"] < hi and lo < r["hi"] and (r["wr"] or wr) and not (bank and q == "P"):
                            found.append(r)
            for r in sorted(found, key=lambda r: -r["seq"]):
                if know[q].get(r["sem"], 0) < r["val"]:
                    queue[q].wait_ge(T.sem[r["sem"]], r["val"])
                    for s, x in r["clock"].items():
                        know[q][s] = max(know[q].get(s, 0), x)
            if "sent" in c:
                c["call"](g)
                continue
            if sem:
                val = 16
                c["call"](queue[q]).then_inc(T.sem[sem], 16)
            else:
                sem = own[q]
                c["call"](queue[q]).then_inc(T.sem[sem], 1)
                val = total[sem] = total.get(sem, 0) + 1
            clock = dict(know[q])
            clock[sem] = val
        for wr, accs in ((True, c["w"]), (False, c["r"])):
            for a in accs:
                name, lo, hi = span(a)
                rows = log.setdefault(name, [])
                if wr:
                    rows[:] = [r for r in rows if not (lo <= r["lo"] and r["hi"] <= hi)]
                rows.append({"q": "dma" if c.get("sem") else q, "sem": sem, "val": val, "clock": clock, "lo": lo, "hi": hi, "wr": wr, "seq": seq})
    for sem, q in (("v", "G"), ("s", "G"), ("p", "G"), ("gc", "V")):
        if know[q].get(sem, 0) < total[sem]:
            queue[q].wait_ge(T.sem[sem], total[sem])


def rank_program(g, core, T, topo):
    rank = T.rank_of(core)
    if rank is None:
        return
    calls = []
    parts, AW = CFG["parts"], CFG["aw"]
    part = [""]

    def op(q, call, reads, writes, cost, lag=0.0, **more):
        tag = q + " " + (writes or reads)[0][0].rstrip("01234") + part[0]
        if tag[:-2] in CFG["lines"]:
            more["line"] = tag[:-2]
        calls.append(dict(more, q=q, call=call, r=tuple(reads), w=tuple(writes), cost=cost, lag=lag, tag=tag))

    def v(a):
        if len(a) == 6:
            return T[a[0]][a[4]:a[5], a[1]:a[2]:a[3]]
        return T[a[0]][:] if len(a) == 1 else T[a[0]][:, a[1]:a[2]] if len(a) == 3 else T[a[0]][:, a[1]:a[2]:a[3]]

    def rw(*a):
        return tuple(x[:3] for x in a if isinstance(x, tuple))

    def sc(x):
        return v(x) if isinstance(x, tuple) else x

    def cols(a):
        return len(range(span(a)[1], span(a)[2], a[3] if len(a) > 3 else 1))

    def cyc(n, *sides):
        narrow = all(SCRATCH[a[0]][2] in ("bfloat16", "float16", "uint16") for a in sides)
        return CYCLE * max(64, n / 2 if sides and narrow else n)

    def ts(out, i0, s1, o0, s2=None, o1=None):
        more = (None, o0) if o1 is None else (sc(s2), o0, o1)
        op("V", lambda e: e.tensor_scalar(v(out), v(i0), sc(s1), *more), rw(i0, s1, s2), rw(out), cyc(cols(out), out, i0))

    def tt(out, a, b, o):
        both = SCRATCH[a[0]][0] == SCRATCH[b[0]][0]
        op("V", lambda e: e.tensor_tensor(v(out), v(a), v(b), o), rw(a, b), rw(out), cyc(cols(out) * (2 if both else 1)))

    def gat(out, win, offs, b, o):
        op("V", lambda e: e.tensor_tensor(v(out), v(win).indirect(v(offs)), v(b), o), rw(win, offs, b), rw(out), 0.05 + 2.2 * CYCLE * cols(out))

    def pick(out, win, offs):
        op("V", lambda e: e.tensor_copy(v(out), v(win).indirect(v(offs))), rw(win, offs), rw(out), 0.05 + 1.56 * CYCLE * cols(out))

    def cp(out, a):
        op("V", lambda e: e.tensor_copy(v(out), v(a)), rw(a), rw(out), cyc(cols(out), out, a))

    def scat(win, offs, a):
        op("V", lambda e: e.tensor_copy(v(win).indirect(v(offs)), v(a)), rw(offs, a), rw(win), 0.05 + 3.8 * CYCLE * cols(a))

    def total(out, a):
        op("V", lambda e: e.tensor_reduce(v(out), v(a), X.X, A.add), rw(a), rw(out), cyc(cols(a)))

    def least(out, a):
        op("V", lambda e: e.tensor_reduce(v(out), v(a), X.X, A.min), rw(a), rw(out), cyc(cols(a)))

    def scan(out, a, b):
        op("V", lambda e: e.tensor_tensor_scan(v(out), v(a), v(b), 0.0, A.mult, A.add), rw(a, b), rw(out), cyc(cols(a)))

    def fill(out, c):
        op("V", lambda e: e.memset(v(out), c), (), rw(out), cyc(cols(out), out))

    def act(out, a, fn, bias=None, scale=None, offs=None, acc=None):
        kw = {}
        if bias is not None:
            kw["bias"] = sc(bias)
        if scale is not None:
            kw["scale"] = sc(scale)
        if acc is not None:
            kw["accum_out"] = v(acc)
        src = v(a) if offs is None else v(a).indirect(v(offs))
        op("S", lambda e: e.activation(v(out), src, fn, **kw), rw(a, bias, scale, offs), rw(out, acc),
           cyc(cols(out)) if offs is None else 0.065 + 1.56 * CYCLE * cols(out), line=offs and out[0])

    def mm(out, l, rh, st=True, sp=True, ap=None):
        op("P", lambda e: e.matmul(v(out), v(l), v(rh) if ap is None else ap, start=st, stop=sp), rw(l, rh), rw(out),
           CFG["pe"] * CYCLE * max(min(64, cols(l)), cols(out)) * (4 if SCRATCH[l[0]][2] == "float32" else 1))

    def mms(out, terms):
        for i, (l, rh) in enumerate(terms):
            mm(out, l, rh, i == 0, i == len(terms) - 1)

    def to_q(out, lname, *srcs):
        mms(out, [((lname, 128 * b, 128 * b + 128), (s[0], s[1] + b, s[2], 16)) for s in srcs for b in range(16)])

    def dma(q, out, src, sem, reads, writes, lag, **more):
        op(q, lambda e: e.dma_start(out, src), reads, writes, 0.05, lag, sem=sem, **more)

    def sel(out, i, pat, o, base, cm):
        op("G", lambda e: e.affine_select(v(out), v(i), pat, o, 0.0, base, cm), rw(i), rw(out), 0.17 + 2 * CYCLE * cols(out))

    def iota(out, pat, base, cm, **kw):
        op("G", lambda e: e.iota(T[out][:], pat, base, cm, **kw), (), ((out,),), 0.13 + 2 * CYCLE * cols((out,)))

    def block(name, i):
        return (name, 128 * i, 128 * i + 128)

    for i, (q, out, src, lag) in enumerate((("S", ("xin0",), T.xw, 1.5), ("Y", ("wti",), T.wts, 1.5), ("Y", ("lx", 0, W), T.lex, 4.0),
                                            ("S", ("thi",), T.th, 1.5), ("Y", ("gin0",), T.gw, 4.5), ("Y", ("lm", 0, W), T.mng, 7.5))):
        dma(q, v(out), src[:], "ld%d" % i, (), (out,), lag, first=1e4 - 1e3 * i)

    small = {"allow_small_or_imprecise_dtypes": True}
    one = ("ones", 0, 128)
    fill(("ones",), 1.0)
    sel(("bo1",), one, [[-16, 8], [0, 16]], A.is_ge, 0, 1)
    sel(("bo",), ("bo1",), [[16, 8], [0, 16]], A.is_ge, 15, -1)
    sel(("idn",), one, [[-1, 128]], A.is_equal, 0, 1)
    iota("jci", [[0, 1]], 0, 1)
    iota("io16", [[1, 16]], 0, 0, **small)
    sel(("lt",), ("bo",), [[1, 128]], A.is_gt, 0, -1)
    iota("io2", [[1, 64]], 2, 0, **small)
    sel(("ra", 0, 512, 1, 0, 64), ("ones", 0, 512, 1, 0, 64), [[-1, 4], [0, 8], [-4, 16]], A.is_equal, 0, 1)

    fill(("cbr", 0, 192), 4160.0)
    fill(("cbr", 192, 384), -65536.0)
    fill(("c120",), 120.0)
    idm, bom, con = {1: ("idn",)}, {1: ("bo",)}, {}
    for i, c in enumerate((-1, -32, 64, -256, 0.5, -0.5)):
        idm[c] = block("ids", i)
        ts(idm[c], ("idn",), float(c), A.mult)
    for i, c in enumerate((-64, 64, -1 / 64.0, -1, 512, 128, 0.5, 8192, -8192, -8, -512, 2, -4096)):
        bom[c] = block("bos", i)
        ts(bom[c], ("bo",), float(c), A.mult)
    for i, c in enumerate((16, -0.25, -64)):
        con[c] = block("cb", i)
        fill(con[c], c / 128.0)
    tt(("bd",), ("bo",), ("idn",), A.subtract)
    cp(("wf",), ("wti",))
    ts(("w1", 0, 128), ("bd",), ("wf", 0, 1), A.mult)
    ts(("w2",), ("bd",), ("wf", 1, 2), A.mult)
    ts(("w1", 128, 256), ("bd",), ("wf", 0, 1), A.mult, 32.0, A.mult)
    ts(("c1",), ("idn",), -17.0, A.mult)
    tt(("e1",), ("bo",), ("c1",), A.add)
    fill(("lk",), 0.0)
    fill(("lb",), 0.0)
    for out, src in (("lk", ("e1", 0)), ("lb", bom[0.5])):
        for k in range(16):
            if out in CFG["gb"]:
                sel((out, 128 * k + k, 128 * (k + 1), 16), (src[0], src[1] + k, src[1] + 128, 16), [[0, 8]], A.is_ge, 0, 0)
            else:
                act((out, 128 * k + k, 128 * (k + 1), 16), (src[0], src[1] + k, src[1] + 128, 16), F.Copy)
    ts(("nlb",), ("lb", 0, 512), -2.0, A.mult)
    if CFG["vf"]:
        act(("id32",), ("idn",), F.Copy)
    tt(("c1",), idm[0.5], ("lt",), A.subtract)
    ts(("zb",), ("c1",), 8192.0, A.mult)
    ts(("jcj",), ("jci",), 15, A.bitwise_and)
    cp(("jc",), ("jcj",))
    ts(("md",), ("io16",), ("jc",), A.is_equal)
    for i, c in enumerate((1.0, 2.0, 33088.0)):
        ts(("col", i, i + 1), ("jc",), -8192.0, A.mult, c - 4096.0, A.add)
        ts(("col", 8 + i, 9 + i), ("jc",), -16384.0, A.mult, c, A.add)
    ts(("col", 3, 4), ("jc",), 4.0, A.mult, 2.0, A.add)
    ts(("col", 4, 8), ("md", 0, NV), 960.0, A.mult)
    ts(("io9",), ("io2",), 958.0, A.add)
    ts(("tha", 0, 1), ("thi",), 0xFF0, A.bitwise_and)
    ts(("tha", 1, 2), ("thi",), 15, A.bitwise_and)
    cp(("thf",), ("tha",))
    cp(("sel", 0, 8), ("bo", 0, 128, 16))
    for i, c in ((1, -2.0), (4, 0.5), (5, -0.5)):
        ts(("sel", 8 * i, 8 * i + 8), ("bo", 0, 128, 16), c, A.mult)
    for i in (0, 1):
        ts(("sel", 16 + 8 * i, 24 + 8 * i), ("bo", 0, 128, 16), ("thf", i, i + 1), A.mult, 1 / 64.0, A.mult)
    mms(("pwd", 0, 8), ((one, ("sel", 16, 24)), (one, ("sel", 24, 32))))
    ts(("tsum", 0, 8), ("pwd", 0, 8), 64.0, A.mult)
    for hf in (0, 1):
        cp(("tsum", 8, 12, 1, 64 * hf, 64 * hf + 64), ("tsum", 4 * hf, 4 * hf + 4, 1, 64 * hf, 64 * hf + 64))
    step = 16 // CFG["nsc"]
    iota("ia", [[0, CFG["nsc"]], [1, 16 * step]], 128, 0, **small)
    iota("cv", [[0, CFG["nsc"]], [16, step]], 64, 0, **small)
    iota("dm", [[16, 16]], W, 0, **small)
    ts(("cv",), ("cv",), ("jc",), A.add)
    ts(("hd", 1, 32, 2), ("dm",), ("jc",), A.add, 0.5, A.mult)
    ts(("dm",), ("hd", 1, 32, 2), -16383.5, A.add)
    fill(("win",), 0.0)

    nxt = T.cores[(rank + 1) % len(T.cores)]
    rid, pid = topo.addr(nxt)[0], topo.addr(nxt)[1]
    mask = topo.mask(core, nxt)
    neng = len(topo.engines(core, nxt))

    def send(src, dst, sem):
        op("G", lambda e: e.remote_dma(v(dst), v(src), T.sem[sem], T.sem.loc, pid, rid, mask), (src,), (), 0.3,
           CFG["far"] + cols(src) / 400.0, sent=sem)
        op("A", None, (), (dst,), 0.0, sem=sem, val=neng)

    lex, mng = ("lx", 0, W), ("lm", 0, W)

    def words(bank, out, terms, p0, p1):
        n = (p1 - p0) // 16
        for hf in range(8 // n):
            r = (128 * hf * n // 8, 128 * (hf + 1) * n // 8)
            mms((bank, K + out + p0 // 16, K + out + p1 // 16, 1) + r,
                [((l, p0, p1, 1) + r, ("sel", s + n * hf, s + n * hf + n, 1) + r) for l, s in terms])

    def places(src, c0, c1, raw, un, out):
        n, x = c1 - c0, (src, c0, c1)

        def half(bank, i, e0=c0, e1=c1):
            return (bank[0], bank[1] + n * i + e0 - c0, bank[1] + n * i + e1 - c0)
        mms(half(raw, 0), ((one, ("cbr", 0, n)), (("w2",), x)))
        mm(half(raw, 1), block("w1", 0), x)
        act(("fb", c0, c1), half(raw, 0), F.Identity, -2047.5)
        act(("fb", K + c0, K + c1), half(raw, 1), F.Identity, 530432.5)
        mm((un[0], un[1], un[1] + 2 * n), one, ("cbr", 192 - n, 192 + n), True, False)
        mm(half(un, 0), block("w1", 0), x, False, False)
        mm(half(un, 1), block("w1", 1), x, False, False)
        mm(half(un, 0), idm[-1], ("fb", K + c0, K + c1), False, True)
        us = CFG["us"] and not out
        if us:
            mms(half(raw, 1), ((one, ("cbr", 0, n)), (("w2",), x), (idm[-1], ("fb", c0, c1))))
            act(("u2s", c0, c1), half(raw, 1), F.Copy)
        for e0 in range(c0, c1, CFG["hs"] if out else n):
            e1 = min(c1, e0 + (CFG["hs"] if out else n))
            if not us:
                tt(("u2s", e0, e1), half(raw, 0, e0, e1), ("fb", e0, e1), A.subtract)
            tt(("pr", e0, e1), ("u2s", e0, e1), half(un, 0, e0, e1), A.mult)
            tt(("p2", e0, e1), ("pr", e0, e1), half(un, 1, e0, e1), A.add)
            ts(("h", e0, e1), ("p2", e0, e1), 5, A.arith_shift_right, 4095, A.bitwise_and)
            if out:
                cp((out, e0, e1), ("h", e0, e1))
            else:
                ts(("hh", e0, e1), ("h", e0, e1), -2048.0, A.add)

    for t in range(NV):
        xi, gi = "xin%d" % t, "gin%d" % t
        XO, GO = ("xo", K * t, K * t + K), ("go", K * t, K * t + K)
        hu, ahead = "hin%d" % t, AW if t < NV - 1 else 0
        part[0] = " h"
        if t == 0:
            places(xi, 0, CH, ("psb", 0), ("phv", 0), hu)
        places(xi, AW if t else CH, K, ("pwd", 0), ("pcb", 0), hu)
        thin = CFG["thin"]
        mm(("pxp", 0, thin), idm[1], (xi, 0, thin))
        for r in range(2):
            mm(("pxp", thin + r, thin + 2 * (K - thin), 2), idm[1], (xi, thin, K))
        for p0, p1 in parts:
            ts(("hh", K + p0, K + p1), (hu, p0, p1), -2048.0, A.add)
        if CFG["xq"]:
            act(("xq",), (xi,), F.Identity, 128.625, 0.25)
        else:
            ts(("xq",), (xi,), 0.25, A.mult, 128.625, A.add)
        if t == NV - 1:
            mms(("ptb", 128, 256), [(idm[1], ("lm", c, c + 128)) for c in range(0, W, 128)])
            total(("sm", 0, 1), ("ptb", 128, 256))
        v0, v1 = CFG["vp"]
        for c, e in CFG["gather"]:
            act(("cg", 16 * c, 16 * e), lex, F.Copy, offs=(hu, c, e))
        for c in range(v0, v1, 16):
            pick(("cg", 16 * c, 16 * c + 256), lex, (hu, c, c + 16))
        for p, (p0, p1) in enumerate(parts):
            n, cnt = p1 - p0, ("pca", "pcb")[p % 2]
            a0, a1 = p0 // 16, p1 // 16
            part[0] = " %d" % p

            def my(name):
                return (name, p0, p1)
            for c, e in (x for x in CFG["compare"] if p0 <= x[0] < p1):
                for k in range(16 if c < thin else 0):
                    d = ("d", 16 * c + k * (e - c), 16 * c + (k + 1) * (e - c))
                    tt(d, ("cg", 16 * c + k, 16 * e, 16), ("pxp", c, e), A.not_equal)
                    mm((cnt, c - p0, e - p0), block("lk", k), d, k == 0, k == 15)
                for k in range(0 if c < thin else 8):
                    d0 = 16 * c + k * CH
                    tt(("d", d0, d0 + CH), ("cg", 16 * c + k, 16 * (c + 32), 8), ("pxp", 2 * c - thin, 2 * c - thin + CH), A.not_equal)
                    for r in (0, 1):
                        mm((cnt, c - p0, c - p0 + 32), block("lk", k + 8 * r), ("d", d0 + r, d0 + CH, 2), k + r == 0, k + r == 8)
            sb, o = ("psb", "pwd")[p % 2], 8 * CFG["sgv"][p]
            if o:
                ts(my("sg"), (cnt, 0, n), -13.5, A.is_ge, -2.0, A.mult)
            else:
                act(my("sg"), (cnt, 0, n), F.Sign, -13.5, -1.0)
            z = (("zb",), my("sg"))
            mms(("phv", 0, n), ((idm[1], ("hh", K + p0, K + p1)), z))
            ts(my("eh"), ("phv", 0, n), ("col", o, o + 1), A.add, -2048.0, A.max)
            to_q(("pq", a0, a1), "lb", my("eh"))
            ts(("hq", a0, a1), ("pq", a0, a1), 2.0, A.mult, 32767.0, A.add)
            mms((sb, 0, n), ((idm[1], my(xi)), z))
            mms((sb, n, 2 * n), ((idm[64], my(xi)), (idm[-256], my("xq")), z))
            mms((sb, 2 * n, 3 * n), ((idm[-1], my(xi)), (idm[1], ("cg", 16 * p0 + t, 16 * p1, 16)), (bom[-64], my("sg"))))
            act(my("xa"), (sb, 0, n), F.Relu, ("col", o + 1, o + 2))
            act(my("yy"), my("xa"), F.Relu, 64.0, -64.0)
            act(my("xl"), (sb, n, 2 * n), F.Relu, ("col", o + 2, o + 3))
            act(my("nn"), (sb, 2 * n, 3 * n), F.Relu, -960.0 - 128 * o, ("md", t, t + 1))
            two = CFG["two"][p]

            def wd(q, b0=a0, b1=a1):
                return (cnt, K + q + b0, K + q + b1)
            if not two:
                words(cnt, 0, (("xa", 0),), p0, p1)
                act(("xw2", a0, a1), wd(0), F.Copy)
                xs = a0 + min(CFG["xs"][p], a1 - a0)
                for a in range(a0, xs):
                    act(("xt", 64 * a, 64 * a + 64), ("io2",), F.Abs, ("xw2", a, a + 1), -1.0)
                if xs > a0:
                    act(("xh", 64 * a0, 64 * xs), ("xt", 64 * a0, 64 * xs), F.Relu, 1.0, -1.0)
                for a in range(xs, a1):
                    ts(("xh", 64 * a, 64 * a + 64), ("io2",), ("xw2", a, a + 1), A.is_equal)
            act(my("gs"), mng, F.Copy, offs=("hq", a0, a1))
            early = ((gi, 0), ("yy", 16), ("yy", 24))
            if CFG["mn"][p] == 2:
                act(my("cr"), lex, F.Copy, offs=("hq", a0, a1))
                mm((cnt, 128, 128 + n), idm[1], my(gi))
                mm((cnt, 0, n), idm[1], my("yy"))
                tt(my("mn"), (cnt, 128, 128 + n), my("gs"), A.min)
                tt(my("mx"), (cnt, 0, n), my("cr"), A.max)
                words(cnt, 48, early + (("gs", 0), ("mn", 8)), p0, p1)
            elif CFG["mn"][p]:
                gat(my("mn"), mng, ("hq", a0, a1), my(gi), A.min)
                words(cnt, 48, early + (("gs", 0), ("mn", 8)), p0, p1)
            else:
                mms((cnt, 128, 128 + n), ((idm[-1], my(gi)), (idm[1], my("gs"))))
                act(my("mn"), (cnt, 128, 128 + n), F.Abs)
                words(cnt, 48, early[1:] + (("mn", 0),), p0, p1)
            if CFG["mn"][p] < 2:
                gat(my("mx"), lex, ("hq", a0, a1), my("yy"), A.max)
            if two:
                words(cnt, 0, (("xa", 40), ("mx", 40)), p0, p1)
                words(cnt, 16, (("xa", 32), ("mx", 40)), p0, p1)
            else:
                words(cnt, 16, (("mx", 0),), p0, p1)
            if two:
                act(("xw2", a0, a1), wd(0), F.Identity, 479.0)
                act(("xw2", 16 + a0, 16 + a1), wd(16), F.Abs, 479.0)
            tt(("nf", a0, a1), wd(48), ("tsum", 0, 8) if n == 128 else ("tsum", 8, 12), A.is_ge)
            if two:
                for a in range(a0, a1):
                    x, c = ("xt", 64 * a, 64 * a + 64), ("chh", 64 * a, 64 * a + 64)
                    act(x, ("io2",), F.Abs, ("xw2", a, a + 1))
                    ts(c, x, ("xw2", 16 + a, 17 + a), A.is_equal, ("nf", a, a + 1), A.mult)
                    mm(("ptb", 0, 64, 1, 0, 64), c, c, a == 0, a == 15)
                continue
            for a in range(a0, a1):
                x, c = ("xh", 64 * a, 64 * a + 64), ("chh", 64 * a, 64 * a + 64)
                ts(c, ("io9",), wd(16, a, a + 1), A.is_equal, ("nf", a, a + 1), A.mult)
                mm(("ptb", 0, 64, 1, 0, 64), x, c, a == 0, False)
                mm(("ptb", 0, 64, 1, 0, 64), c, x, False, a == 15)
        def unmerged(bank, o, n):
            mms((bank, o, o + n), ((idm[1], (xi, 0, n)), (block("lb", t), ("c120", 0, n)), (idm[1], ("nn", 0, n)), (block("nlb", t), ("yy", 0, n))))
        if ahead:
            part[0] = " n"
            unmerged("psb", K, AW)
            tt(("xc", 0, AW), ("psb", K, K + AW), ("mx", 0, AW), A.min)
            places("xc", 0, AW, ("psb", 0), ("pxp", 0), None)
        part[0] = " f"
        mms(("phv", 0, K), ((idm[1], (xi,)), (idm[1], ("nn",)), (block("nlb", t), ("yy",))))
        act(("xn",), ("phv", 0, K), F.Identity, ("col", 4 + t, 5 + t))
        to_q(("pq", 16, 32), "lb", ("xl", 0, K), ("mx", 0, K))
        ts(("of",), ("pq", 16, 32), 2.0, A.mult, -1024.0, A.add)
        tt(("hd", 0, 32, 2), ("pq", 0, 16), ("dm",), A.subtract)
        ts(("hqs",), ("pq", 0, 16), -1024.0, A.mult, 2.0 ** 24 - 1, A.min)
        tt(("hqs",), ("hqs",), ("cv",), A.subtract)
        mms(("pca", K, 2 * K), ((bom[1], ("xa",)), (bom[-1 / 64.0], ("xl",))))
        act(("ms",), ("pca", K, 2 * K), F.Copy)
        ts(("h1", 0, 64, 1, 0, 64), ("ptb", 0, 64, 1, 0, 64), 1.0, A.min)
        for q in range(4):
            mm(("pca", 64 * q, 64 * q + 64), ("ra", 128 * q, 128 * q + 128, 1, 0, 64), ("h1", 0, 64, 1, 0, 64))
        act(("tb",), ("pca", 0, K), F.Identity, -1.0, ("col", 3, 4))
        if CFG["dv"]:
            mms(("pcb", 0, K), ((idm[-0.5], (gi,)), (idm[0.5], ("gs",))))
            ts(("dh",), ("pcb", 0, K), 1535.75, A.add)
        else:
            mms(("pcb", 0, K), ((idm[0.5], (gi,)), (idm[0.5], ("gs",)), (idm[-1], ("mn",))))
            act(("dg",), ("pcb", 0, K), F.Identity, 127.75)
        gat(("f",), ("tb",), ("of",), ("ms",), A.is_equal)
        if ahead:
            part[0] = " s"
            mms(("psb", 0, AW), ((idm[1], ("hh", K, K + AW)), (idm[-1], ("hh", 0, AW)), (bom[8192], ("f", 0, AW))))
            act(("vb", 0, AW), ("psb", 0, AW), F.Relu, -4096.0)
            mms(("phv", 0, AW), ((idm[1], ("hh", 0, AW)), (bom[-4096], ("f", 0, AW)), (("id32",), ("vb", 0, AW))))
            ts(("ho", K * t, K * t + AW), ("phv", 0, AW), 2048.0, A.add)
            send(("ho", K * t, K * t + AW), ("hin%d" % (t + 1), 0, AW), "ah%d" % (t + 1))
            part[0] = " f"
        mms(("pxp", K, 2 * K), ((idm[1], ("mx",)), (bom[64], ("f",))))
        tt(XO, ("pxp", K, 2 * K), ("xn",), A.min)
        send(XO, ("xin%d" % (t + 1),), "ax%d" % (t + 1))
        mms(("pwd", K, 2 * K), ((bom[512], ("eh",)), (idm[1], ("ia",)), (bom[128], ("f",))))
        part[0] = " c"
        for a0 in reversed(range(0, 16, step)):
            a1 = a0 + step
            for a in reversed(range(a0, a1)):
                row = ("ea", 128 * a, 128 * a + 16 * (a + 1 - a0))
                act(row, ("pwd", K + 16 * a0, K + 16 * a + 16), F.Abs, ("hqs", a, a + 1))
                least(("lq", a, a + 1), row)
            ts(("win", 2 * a0 + 1, 2 * a1, 2), ("lq", a0, a1), 64.0, A.is_equal)
            scan(("sq", 2 * a0, 2 * a1), ("win", 2 * a0, 2 * a1), ("hd", 2 * a0, 2 * a1))
            ts(("so", a0, a1), ("sq", 2 * a0 + 1, 2 * a1, 2), 2.0, A.mult)
            scat(("lx",), ("so", a0, a1), ("xo", K * t + 16 * a0, K * t + 16 * a1))
        part[0] = " g"
        step_ = ((idm[1], ("dh",)),) if CFG["dv"] else ((idm[1], ("dg",)), (idm[1], ("mn",)), (idm[-1], (gi,)))
        mms(("pcb", K, 2 * K), step_ + ((bom[-8], ("yy",)), (bom[-512], ("f",))))
        act(("gm",), ("pcb", K, 2 * K), F.Relu, 7680.0 - 1408 * CFG["dv"])
        mms(("pca", K, 2 * K), ((idm[1], (gi,)), (bom[2], ("yy",)), (bom[128], ("f",)), (idm[1], ("gm",))))
        act(GO, ("pca", K, 2 * K), F.Identity, -2048.0)
        send(GO, ("gin%d" % (t + 1),), "ag%d" % (t + 1))
        if t == NV - 1:
            part[0] = " e"
            act(("lm", W, W + K), GO, F.Copy, acc=("sm", 1, 2))
        for a in reversed(range(0, 16, step)):
            if t == NV - 1:
                act(("gs", 16 * a, 16 * (a + step)), ("lm",), F.Identity, None, -1.0, ("so", a, a + step), ("sm", 2 + a // step, 3 + a // step))
            if a or t < NV - 1:
                scat(("lm",), ("so", a, a + step), ("go", K * t + 16 * a, K * t + 16 * (a + step)))

    total(("sm", 15, 16), ("sm", 0, 2 + CFG["nsc"]))
    for q, y, a, sem in (("Y", T.yl, lex, "st0"), ("Y", T.yx, ("xin%d" % NV,), "st1"), ("Y", T.yg, ("gin%d" % NV,), "st2"), ("S", T.ym, ("sm", 15, 16), "st3")):
        dma(q, y[:], v(a), sem, (a,), (), 1.3 + cols(a) / 2.5e3)
    if "calls" not in ORDER:
        ORDER["calls"] = order(calls)
    issue(g, T, [calls[i] for i in ORDER["calls"]])
    for i in range(4):
        g.wait_ge(T.sem["st%d" % i], 16)
    g.wait_ge(T.sem.loc, neng * sum("sent" in c for c in calls))
